import numpy as np, ml_dtypes
CORES = [113,118,241,246]
N = 4
BF = ml_dtypes.bfloat16
def gentries(a):
    return np.ascontiguousarray(a.reshape(8, 16, -1).transpose(0, 2, 1)).reshape(8, -1)
def gtable(e):
    e = np.asarray(e); return np.ascontiguousarray(e.reshape(8, -1, 16).transpose(0, 2, 1)).reshape(128, -1).astype(np.int32)
W, L, U, T, A, K, Q = 2048, 208, 48, 6, 3, 768, 1248
def pack(x, b, o, w, t):
    return {"xs": np.ascontiguousarray(x.reshape(N, 128, W)).astype(np.float32).astype(BF), "nb": np.ascontiguousarray(b.reshape(N, 128, W)).astype(np.int32),
            "od": np.stack([gtable(a) for a in o]), "wt": np.ascontiguousarray(w.reshape(N, 128, 1)).astype(np.int32), "th": np.ascontiguousarray(t.reshape(N, 8, 1)).astype(np.int32)}
def parts(rng):
    amp = 4 + 86 * rng.random((N, 8, 1, W)); mid = rng.integers(96, 160, (1, 8, 16, 1))
    x = np.clip(np.rint(mid + amp * rng.standard_normal((N, 8, 16, W), dtype=np.float32)), 0, 255).astype(np.int64)
    b = rng.integers(0, W, (N, 8, 16, W)); o = np.argsort(rng.random((N, 8, W)), axis=-1)[..., :Q]
    return x, b, o, rng.integers(0, 256, (N, 8, 16)), rng.integers(300, 1000, (N, 8))
def setup_inputs(rng):
    return pack(*parts(rng))
def setup_inputs_spread(rng):
    x, b, o, w, t = parts(rng)
    x = np.floor(np.exp2(8 * rng.random((N, 8, 1, W))) * rng.random((N, 8, 16, W))).astype(np.int64)
    b = np.floor(W * rng.random((N, 8, 16, W)) ** 3).astype(np.int64)
    w = np.floor(np.exp2(8 * rng.random((N, 8, 16))) - 1).astype(np.int64); t = np.floor(np.exp2(12 * rng.random((N, 8))) - 1).astype(np.int64)
    x[:, 6] = rng.integers(192, 256, (N, 16, W)); w[:, 6] = rng.integers(240, 256, (N, 16)); t[:, 6] = 0
    return pack(x, b, o, w, t)
def setup_inputs_ends(rng):
    lo = rng.integers(0, 2, 8) * 255; lo[7] = 0; base = lo.reshape(1, 8, 1, 1)
    u = rng.random((N, 8, 1, W)); e = 255 * rng.integers(0, 2, (N, 8, 16, W))
    x = np.where(u < 0.5, 255 - base, np.where(u < 0.7, base, e))
    x[..., [0, W - 1]] = base; x[:, ::2, :, 1] = lo[::2].reshape(1, 4, 1); x[:, 7, :, 1:8] = 0; x[:, 7, 15, W - 1] = 255
    b = (W - 1) * rng.integers(0, 2, (N, 8, 16, W))
    b = np.where(rng.random((N, 8, 1, W)) < 0.2, (W - 1) * rng.integers(0, 2, (N, 8, 1, W)), b)
    for step in range(A, T):
        place = (16 * 255 * 255 + 77 * step) & (W - 1)
        b[:, 7, :, place] = 0; b[1::2, 7, 15, place] = W - 1; b[:, 7, 5, (77 * step) & (W - 1)] = W - 1
    s = np.zeros(Q, np.int64); h = Q // 2; s[0::2] = np.arange(Q - h); s[1::2] = W - 1 - np.arange(h)
    key = rng.random((N, 8, T, L)); key[:, :, 0, 0] = -3; key[:, :, 0, 1] = -2; key[:, :, 0, 2] = -1
    o = s.reshape(T, L)[np.arange(T)[:, None], np.argsort(key, axis=-1)].reshape(N, 8, Q)
    for q in range(N):
        x[q, 7][:, o[q, 7][np.array([3, 4, U - 2, U - 1, L - 2, L - 1])]] = 255
    kd = rng.integers(0, 3, (N, 8, 1)); w = np.where(kd == 0, 255, np.where(kd == 1, 0, 255 * rng.integers(0, 2, (N, 8, 16))))
    w[:, 7] = 255; w[:, 0, ::2] = 0; w[:, 0, 1::2] = 255
    t = 4095 * (rng.random((N, 8)) < 0.3).astype(np.int64)
    for q in range(N): t[q, q % 7] = 4095
    t[:, 7] = 0
    return pack(x, b, o, w, t)
def setup_inputs_corners(rng):
    a = (np.arange(65536)[:, None] >> np.arange(16)) & 1
    par = np.stack([(np.arange(16) >> i) & 1 for i in range(4)] + [np.ones(16, np.int64)], axis=1)
    words = a[~np.any(((a @ par) & 1) == 1, axis=1)]
    few = words[np.sum(words, axis=1) <= 10]
    src = (N - 2 - (A - 1) % (N - 1)) % N
    late = (5 - A) * L
    x = rng.integers(100, 132, (N, 8, 16, W)); b = rng.integers(0, W, (N, 8, 16, W)); o = np.zeros((N, 8, Q), np.int64)
    far = np.arange(W) + 1 + rng.integers(W // 4, 3 * W // 4, (N, 8, W)); far = far & (W - 1); far = far - (far & 1); b[:, :, 0] = (far - 1) & (W - 1)
    for q in range(N):
        for g in range(8):
            n = int(rng.choice(np.array([0, 1, U - 1, U, U + 1, L])))
            if q == 0: n = (U, U + 1, L, U - 1, 1, 0, U, L)[g]
            if g == 4: n = U if q == src else 1 if q == (src + 1) % N else int(rng.choice(np.array([0, 1, U - 1, U])))
            if g == 5: n = 0
            odd = rng.permutation(W // 2) * 2 + 1; even = np.arange(W // 2) * 2
            rest = rng.permutation(np.concatenate([odd[n:], even]))
            first = rng.permutation(np.concatenate([odd[:n], rest[:L - n]])); more = rest[L - n:]
            o[q, g] = (np.concatenate([more[:late], first, more[late:]]) if g == 7 else np.concatenate([first, more]))[:Q]
            lone = np.zeros(W, bool)
            if g != 4 and g != 7: lone[odd[n:][rng.random(W // 2 - n) < 0.1]] = True
            lone[rest[:L - n]] = False; lone[odd[:n]] = True
            k = int(np.count_nonzero(lone))
            if g == 4: x[q, g][:, lone] = 30 + 160 * few[rng.permutation(few.shape[0])[:k]].T
            else: x[q, g][:, lone] = 255 * words[rng.permutation(2048)[:k]].T
            if g == 4 and q == src: x[q, g][:, first[np.flatnonzero(lone[first])[-1]]] = 255
    w = np.zeros((N, 8, 16), np.int64) + rng.choice(np.array([0, 1, 255]), (N, 8, 1)); w[:, 3] = 255; w[:, 2] = 0
    t = rng.choice(np.array([600, 600, 600, 0]), (N, 8)); t[0] = 600; t[1, 6] = 0; t[:, 4] = 600; t[:, 5] = 4095; t[:, 7] = 600
    return pack(x, b, o, w, t)
def setup_inputs_ties(rng):
    _, b, o, w, t = parts(rng)
    kd = np.repeat(rng.random((N, 8, W // 2)), 2, axis=-1); half = np.argsort(rng.random((N, 8, 16, W)), axis=2) < 8; kx = kd[:, :, None, :]
    x = np.where(kx < 0.35, 100, np.where(kx < 0.7, 140, np.where(half, 100, 140)))
    for q in range(N):
        for g in range(8):
            com = np.flatnonzero(kd[q, g, ::2] < 0.7) * 2
            b[q, g] = np.where(rng.random((16, W)) < 0.05, b[q, g], com[rng.integers(0, com.shape[0], (16, W))])
    t = rng.choice(np.array([0, 319, 320, 321]), (N, 8)); t[0, :4] = np.array([0, 319, 320, 321]); t[1, 4:] = np.array([320, 321, 0, 320])
    return pack(x, b, o, w, t)
def setup_inputs_near(rng):
    _, b, o, w, t = parts(rng)
    y = (np.add.accumulate(rng.integers(-3, 4, (N, 8, 16, W)), axis=3) + rng.integers(0, 512, (N, 8, 16, 1))) & 511
    x = np.where(y > 255, 511 - y, y); u = np.arange(W)
    b = np.where(rng.random((N, 8, 16, W)) < 0.7, (u + rng.choice(np.array([-17, -16, -15, -1, 0, 1, 15, 16, 17]), (N, 8, 16, W))) & (W - 1), b)
    b = np.where(rng.random((N, 8, 1, W)) < 0.25, (u + rng.integers(-15, 16, (N, 8, 16, W))) & (W - 1), b)
    key = rng.random((N, 8, W)); key[..., :16] -= 1; key[..., W - 16:] -= 1; o = np.argsort(key, axis=-1)[..., :Q]
    t = rng.choice(np.array([40, 100, 400, 900, 4095]), (N, 8)); t[0, 0] = 4095; t[0, 1] = 40; t[1, 2] = 100
    return pack(x, b, o, w, t)
def check_inputs(d):
    bad = []
    for k, lo, hi in (("xs", 0, 255), ("nb", 0, W - 1), ("od", 0, W - 1), ("wt", 0, 255), ("th", 0, 4095)):
        a = np.asarray(d[k]).astype(np.float32)
        if not (np.min(a) >= lo and np.max(a) <= hi): bad.append("range of " + k)
    a = np.asarray(d["xs"]).astype(np.float32)
    if np.any(a != np.floor(a)): bad.append("whole numbers in xs")
    o = np.sort(np.stack([gentries(a) for a in d["od"]]), axis=-1)
    if np.any(o[..., 1:] == o[..., :-1]): bad.append("different numbers in a group's od")
    return bad
def dist(X, c, x):
    n = c.shape[3]
    e = np.take_along_axis(X, c.reshape(N, 8, 1, 16 * n), 3).reshape(N, 8, 16, 16, n)
    return np.add.reduce(np.abs(e - x[:, :, :, None, :]), axis=2)
def reference(xs, nb, od, wt, th):
    X = xs.astype(np.float32).astype(np.int64).reshape(N, 8, 16, W); col = nb.astype(np.int64).reshape(N, 8, 16, W)
    order = np.stack([gentries(a) for a in od]).astype(np.int64); w = wt.astype(np.int64).reshape(N, 8, 16, 1); lim = th.astype(np.int64).reshape(N, 8)
    v = np.zeros((N, 8, L), np.int64); m = np.zeros((N, 8, L), np.int64); age = np.zeros((N, 8, L), np.int64); c = np.zeros((N, 8, 16, L), np.int64)
    free = np.ones((N, 8, L), bool); cur = np.zeros((N, 8, 1), np.int64); gx = np.zeros((N, 8, 16, U), np.int64); gm = np.zeros((N, 8, U), np.int64)
    seen = []; judged = gm
    for t in range(T):
        f = free.astype(np.int64); run = np.add.accumulate(f, axis=2)
        v = np.where(free, np.take_along_axis(order, np.minimum(cur + run - f, Q - 1), 2), v); cur = cur + run[:, :, L - 1:]
        m = np.where(free, 4095, m); age = np.where(free, 0, age)
        seed = (np.take_along_axis(col, ((v - 1) & (W - 1))[:, :, None, :], 3) + 1) & (W - 1)
        c = np.where(free[:, :, None, :], seed, c)
        h = (np.add.reduce(w * gx, axis=2) + 77 * t) & (W - 1)
        gc = np.take_along_axis(col, h[:, :, None, :], 3)
        own = np.take_along_axis(X, v[:, :, None, :], 3)
        D = np.where(np.abs(c - v[:, :, None, :]) < 16, 4095, dist(X, c, own))
        m = np.minimum(m, np.min(D, axis=2)); near = np.take_along_axis(c, np.argmin(D, axis=2)[:, :, None, :], 2)
        judged = np.minimum(gm, np.min(dist(X, gc, gx), axis=2))
        np.put_along_axis(col, v[:, :, None, :], c, 3)
        alive = m >= lim[:, :, None]; age = np.where(alive, age + 1, age)
        go = (alive & (age >= A)).astype(np.int64); before = np.add.accumulate(go, axis=2) - go
        leave = (go == 1) & (before < U) & (t < T - 1)
        c = np.take_along_axis(col, near, 3)
        free = ~alive | leave
        slot = np.where(leave, before, U); nx = np.zeros((N, 8, 16, U + 1), np.int64); nm = np.zeros((N, 8, U + 1), np.int64)
        np.put_along_axis(nx, slot[:, :, None, :], own, 3); np.put_along_axis(nm, slot, m, 2)
        gx = np.roll(nx[..., :U], 1 + t % (N - 1), axis=0); gm = np.roll(nm[..., :U], 1 + t % (N - 1), axis=0)
        best = np.max(judged, axis=(0, 2)); lim = lim + (np.maximum(best[None, :] - lim, 0) >> 2)
        seen.append(lim)
    yn = np.take_along_axis(col, order[:, :, None, :K], 3).reshape(N, 128, K)
    return {"yn": yn.astype(np.float32), "yv": v.astype(np.float32), "ym": m.astype(np.float32), "yg": judged.astype(np.float32), "yt": np.stack(seen, axis=2).astype(np.float32)}

@@ -1,0 +1,646 @@
+from concourse.bass import DstId, RemoteDMATransfer
+from concourse.mybir import AluOpType, AxisListType, ActivationFunctionType
+
+W, L, U, NT, Q, KN = 2048, 208, 48, 6, 1248, 768
+B = 2064
+LP = 224
+H = "float16"
+BIG = float(2 ** 30)
+CH = [[(0, a, h[0]), (a, b, h[1]), (b, L, h[2])] for a, b, h in
+      ((80, 144, "vsv"), (80, 144, "vsv"), (64, 128, "vsv"), (80, 144, "vsv"), (64, 144, "svs"), (80, 144, "vss"))]
+VG = [32, 0, 32, 32, 16, 32]
+GV = [0, 0, 24]
+GK = [0, 0, 1]
+KS = 8
+KEEP = [3, 4]
+OD = {0: (14, 46), 1: (46, 66), 2: (66, 78)}
+NOM = {"cyc": 0.83, "gat": 1.56, "sca": 3.8, "fix": 20.0, "pe": 0.42, "sem": 80.0, "pel": 60.0, "rem": 2800.0, "first": 2500.0, "lam": 2.0}
+BIAS = {'3vdead': 1500, '0sG': -3000, '3vM': -1500, '0vDT': -3000, '1tpb': -250, '2vdead': 250, '5tpb': -250, '3vyy': -600,
+        '3vhm': -1500, '3vpo': -1500, '3vslt': -250, '3vDT': 600, '4vhm': -1500, '3vgr': -1500, '4vpo': -600, '2vM': -3000, '2vDC': -600,
+        '2vgo': 3000, '4vG': -1500, '4scap': 1500, '2vG': 600, '5tpa': 600, '9vTT': 3000, '9vLZ': -3000, '5vDT': -3000, '5vkgT': -3000,
+        '2va1': -1500}
+F, BF, I, U16 = "float32", "bfloat16", "int32", "uint16"
+
+
+def _sb(n, d):
+    return ("sbuf", [128, n], d)
+
+
+SCRATCH = {
+    "nbi": _sb(W, I), "TT": _sb(B + Q, F), "XT": _sb(B + Q, BF), "VT": _sb(B + Q, F),
+    "TO0": _sb(W, F), "TO1": _sb(W, F), "TO2": _sb(W, F), "odi": _sb(78, I), "oda": _sb(78, I), "odb": _sb(78, I), "od16": _sb(78, U16), "om16": _sb(78, U16),
+    "G": _sb(16 * L, BF), "M": _sb(16 * L, BF), "AA": _sb(16 * L, BF), "Gg": _sb(16 * U, BF), "Ag": _sb(16 * U, BF),
+    "own": _sb(L, BF), "ownf": _sb(L, F), "c16": _sb(L, U16), "cr": _sb(L, H), "fl": _sb(L, H),
+    "DC": _sb(2 * LP, H), "DT": _sb(2 * LP, H), "a1": _sb(LP, BF), "a2": _sb(LP, BF),
+    "ks": _sb(LP, F), "yy": _sb(LP, F), "nr": _sb(LP, F), "mex": _sb(LP, F), "mC": _sb(LP, F),
+    "dead": _sb(14, BF), "go": _sb(14, BF), "free": _sb(14, BF), "thrD": _sb(14, F),
+    "LE": _sb(28, H), "L16": _sb(28, U16), "slt": _sb(14, H), "s16": _sb(14, U16), "v16": _sb(14, U16),
+    "mk": _sb(14, F), "mn": _sb(14, F), "mi": _sb(14, I), "F0": _sb(14, F), "F1": _sb(14, F), "FF": _sb(14, F),
+    "thP": _sb(14, F), "thD": _sb(14, F), "thG": _sb(14, F), "thx": _sb(14, F), "cur": _sb(14, F),
+    "row": _sb(144, F), "pci": _sb(1, I), "cI": _sb(8, I), "cF": _sb(24, F), "R16": _sb(128, F), "R32": _sb(128, F),
+    "lanb": _sb(14, F), "par": _sb(14, F), "kk": _sb(LP, F), "lanc": _sb(14, F), "dum": _sb(14, F), "mRG": _sb(14, F),
+    "Zn": _sb(144, BF), "Z2": _sb(144, BF), "Bn": _sb(128, BF), "Z1": _sb(144, BF), "ZM": _sb(144, BF), "ZG": _sb(144, BF), "ZA": _sb(144, BF), "Ib": _sb(128, BF), "In": _sb(128, BF),
+    "If": _sb(128, F), "B1": _sb(128, BF), "BO": _sb(128, BF), "WB": _sb(128, BF), "DP": _sb(128, BF), "DK": _sb(128, BF),
+    "O32": _sb(128, BF), "O3f": _sb(128, F), "Lt": _sb(128, BF), "LZ": _sb(128, BF), "LW": _sb(128, BF),
+    "I4": _sb(128, BF), "I2": _sb(128, BF), "LL": _sb(512, H),
+    "one": _sb(LP, BF), "rst": _sb(LP, F), "rs1": _sb(U, F), "dg": _sb(U, F),
+    "wti": _sb(1, I), "thi": _sb(1, I), "ytl": _sb(8, F), "th4": _sb(4, F),
+    "snd": _sb(560, F), "gin0": _sb(U, F), "gin1": _sb(U, F), "gin2": _sb(U, F),
+    "gr": _sb(U, F), "xb": _sb(2 * U, BF), "cap": _sb(2 * U, F), "hm": _sb(U, F), "hs": _sb(U, F), "hi": _sb(4, I), "ha": _sb(4, I),
+    "h16": _sb(4, U16), "g16": _sb(U, U16), "kg": _sb(64, F), "kgT": _sb(64, F), "js": _sb(64, F), "jC": _sb(64, F),
+    "bt": _sb(48, F), "bc": _sb(4, F), "bi": _sb(1, I), "vf": _sb(L, F), "yno": _sb(KN, F),
+    "pk": ("psum", [128, 512], F), "po": ("psum", [128, 512], F), "pz": ("psum", [128, 512], F), "pw": ("psum", [128, 512], F),
+    "pa": ("psum", [128, 512], F), "pb": ("psum", [128, 512], F), "pc": ("psum", [128, 512], F), "pg": ("psum", [128, 512], F),
+}
+NDMA = 17
+SEMAPHORES = (["qv", "qs", "qt", "qg", "ga0", "ga1", "ga2", "ba0", "ba1", "ba2"] + ["left%d" % j for j in range(6)]
+              + ["d%d" % j for j in range(NDMA)])
+OP = AluOpType
+ACT = ActivationFunctionType
+
+
+def A(name, c0=0, c1=None, st=1, p=None):
+    return ("a", name, c0, SCRATCH[name][1][1] if c1 is None else c1, st, p)
+
+
+def IND(win, off):
+    return ("i", win, off)
+
+
+def width(a):
+    if a[0] == "i":
+        return 16 * width(a[2])
+    return (a[3] - a[2] + a[4] - 1) // a[4]
+
+
+def duration(kind, outs, ins):
+    full = [a for a in outs + ins if isinstance(a, tuple)]
+    if kind == "mm":
+        return max(64, width(ins[1])) * NOM["pe"] * (4 if SCRATCH[ins[1][1]][2] == F else 1)
+    if kind == "iota":
+        return 130 + 2 * NOM["cyc"] * width(outs[0])
+    ind = [a for a in full if a[0] == "i"]
+    if ind:
+        return 60 + width(ind[0]) * NOM["cyc"] * (NOM["sca"] if ind[0] is outs[0] else NOM["gat"])
+    n = max(width(a) for a in full)
+    c = 1.0
+    if kind == "tt":
+        c = 1.0 if any(SCRATCH[a[1]][0] == "psum" for a in ins) else 2.0
+    elif kind != "act" and all(SCRATCH[a[1]][2] in (BF, H, U16) for a in full if width(a) == n):
+        c = 0.5
+    return max(64, n * c) * NOM["cyc"] + NOM["fix"]
+
+
+def best_masks(src, cores, topo):
+    peers = sorted([c for c in cores if c != src], key=lambda c: len(topo.engines(src, c)))
+    used, out = [], {}
+    for c in peers:
+        have = [e for e in topo.engines(src, c) if e not in used]
+        alike = [d for d in peers if d not in out and topo.mask(src, d) == topo.mask(src, c)]
+        n = 1
+        while 2 * n <= len(have) // len(alike) and not (out and n >= max(x for _, x in out.values())):
+            n *= 2
+        used += have[:n]
+        out[c] = (sum(1 << e for e in have[:n]), n)
+    return out
+
+
+def plan(ops):
+    seen, lines = {}, {}
+    for n, o in enumerate(ops):
+        deps, after = set(o["more"]), set()
+        for (name, c0, c1, st, wr) in o["acc"]:
+            ps = SCRATCH[name][0] == "psum"
+            for (m, d0, d1, ds, dw) in seen.get(name, []):
+                if m == n:
+                    continue
+                same = ops[m]["q"] == o["q"] and ops[m]["tok"] is None and o["tok"] is None
+                over = d0 < c1 and c0 < d1 and not (st == ds and (c0 - d0) % st)
+                if same and o["q"] == "t":
+                    if ps and (o["edge"] or ops[m]["edge"]):
+                        after.add(m)
+                elif (ps and not same) or (over and (dw or wr)):
+                    deps.add(m)
+            seen.setdefault(name, []).append((n, c0, c1, st, wr))
+        if o["line"] is not None:
+            if o["line"] in lines:
+                after.add(lines[o["line"]])
+            lines[o["line"]] = n
+        done, ahead, kept, near = 0, 0, set(), set()
+        for m in sorted(after, reverse=True):
+            if not ahead >> m & 1:
+                near.add(m)
+                done |= ops[m]["done"]
+                ahead |= ops[m]["ahead"] | 1 << m
+        for m in sorted(deps, reverse=True):
+            if not done >> m & 1:
+                kept.add(m)
+                done |= ops[m]["done"] | ops[m]["ahead"] | 1 << m
+        o["done"], o["ahead"] = done, ahead
+        o["deps"], o["after"] = kept, near - kept
+    return schedule(ops)
+
+
+def schedule(ops):
+    succ = [[] for _ in ops]
+    for n, o in enumerate(ops):
+        for m in o["deps"] | o["after"]:
+            succ[m].append(n)
+    rest = [0.0] * len(ops)
+    for n in range(len(ops) - 1, -1, -1):
+        o = ops[n]
+        rest[n] = o["dur"] + max([0.0] + [rest[s] + (o["lat"] + NOM["sem"] if n in ops[s]["deps"] else 0.0) for s in succ[n]] + [o["lat"]])
+    for n in range(5):
+        rest[n] += 1e6 * (5 - n)
+    rest = [r + BIAS.get(o["tag"], 0) for r, o in zip(rest, ops)]
+    miss = [len(o["deps"] | o["after"]) for o in ops]
+    ready = [n for n in range(len(ops)) if miss[n] == 0]
+    at = [0.0] * len(ops)
+    free, order = {}, []
+    while ready:
+        est = {n: max(at[n], free.get(ops[n]["q"], 0.0)) for n in ready}
+        first = min(ready, key=lambda n: est[n] + ops[n]["dur"])
+        q, end = ops[first]["q"], est[first] + ops[first]["dur"]
+        n = max([m for m in ready if ops[m]["q"] == q and est[m] <= end], key=lambda m: (rest[m] - NOM["lam"] * est[m], -m)) if q else first
+        ready.remove(n)
+        order.append(n)
+        done = est[n] + ops[n]["dur"]
+        if q:
+            free[q] = done
+        for s in succ[n]:
+            if n in ops[s]["deps"]:
+                at[s] = max(at[s], done + ops[n]["lat"] + NOM["sem"])
+            miss[s] -= 1
+            if miss[s] == 0:
+                ready.append(s)
+    return order
+
+
+def emit(g, T, ops):
+    eng = {"v": g.vector, "s": g.scalar, "t": g.tensor, "g": g, "y": g.sync}
+    qsem = {"v": "qv", "s": "qs", "t": "qt", "g": "qg"}
+    order = plan(ops)
+    last, pos, cnt = {}, {}, {}
+    for n in order:
+        o = ops[n]
+        if o["tok"] is None:
+            last[o["q"]] = n
+            cnt[o["q"]] = cnt.get(o["q"], 0) + 1
+            pos[n] = (o["q"], cnt[o["q"]])
+        else:
+            pos[n] = (("x", n), 1)
+    place = {n: j for j, n in enumerate(order)}
+    known = {}
+    for n in order:
+        o = ops[n]
+        kn = known.setdefault(o["q"], {})
+        o["waits"] = []
+        if o["q"] is not None:
+            for m in sorted(o["deps"], key=lambda m: -place[m]):
+                key, val = pos[m]
+                if kn.get(key, 0) < val:
+                    o["waits"].append(m)
+                    kn[key] = val
+                    for k2, v2 in ops[m]["kn"].items():
+                        if kn.get(k2, 0) < v2:
+                            kn[k2] = v2
+        o["kn"] = dict(kn) if o["q"] is not None else {}
+    need = set(last.values())
+    for o in ops:
+        need.update(o["waits"])
+    cnt, final = {}, {}
+    for n in order:
+        o = ops[n]
+        o["inc"] = None
+        if o["tok"] is None and n in need:
+            cnt[o["q"]] = cnt.get(o["q"], 0) + 1
+            o["inc"] = (qsem[o["q"]], cnt[o["q"]])
+        if o["q"] is None:
+            continue
+        for m in o["waits"]:
+            s, v = ops[m]["tok"] or ops[m]["inc"]
+            eng[o["q"]].wait_ge(T.sem[s], v)
+        ins = o["fn"](eng[o["q"]])
+        if o["inc"]:
+            ins.then_inc(T.sem[o["inc"][0]], 1)
+            final[o["inc"][0]] = o["inc"][1]
+        elif o["tok"]:
+            final[o["tok"][0]] = o["tok"][1]
+    for s, v in final.items():
+        g.wait_ge(T.sem[s], v)
+
+
+def rank_program(g, core, T, topo):
+    rank = T.rank_of(core)
+    if rank is None:
+        return
+    cores = list(T.cores)
+    NR = len(cores)
+    ops = []
+    ndma = [0]
+    sent = {}
+    now = [9]
+    common = [x for x in topo.engines(cores[0], cores[1]) if all(x in topo.engines(a, b) for a in cores for b in cores if a != b)]
+
+    def ap(a):
+        if not isinstance(a, tuple):
+            return a
+        if a[0] == "i":
+            return ap(a[1]).indirect(ap(a[2]))
+        _, name, c0, c1, st, p = a
+        cs = slice(c0, c1) if st == 1 else slice(c0, c1, st)
+        if p is None:
+            return T[name][:, cs]
+        return T[name][slice(p[0], p[1]) if p[2] == 1 else slice(p[0], p[1], p[2]), cs]
+
+    def rec(q, kind, fn, outs, ins, tok=None, lat=0.0, more=()):
+        acc = []
+        for lst, wr in ((ins, False), (outs, True)):
+            for a in lst:
+                if not isinstance(a, tuple):
+                    continue
+                if a[0] == "i":
+                    acc.append((a[1][1], a[1][2], a[1][3], 1, wr))
+                    acc.append((a[2][1], a[2][2], a[2][3], 1, False))
+                else:
+                    acc.append((a[1], a[2], a[3], a[4], wr))
+        dur = (100.0 if q else 0.0) if tok else duration(kind, outs, ins)
+        ops.append({"q": q, "fn": fn, "acc": acc, "tok": tok, "dur": dur, "lat": NOM["pel"] if q == "t" else lat, "more": more,
+                    "edge": False, "line": None, "spec": (kind, outs, ins), "tag": "%d%s%s" % (now[0], q or "-", acc[-1][0])})
+        return len(ops) - 1
+
+    def line(key):
+        ops[-1]["line"] = key
+
+    def cp(out, x):
+        rec("v", "cp", lambda e: e.tensor_copy(ap(out), ap(x)), [out], [x])
+
+    def tt(out, x, y, op):
+        rec("v", "tt", lambda e: e.tensor_tensor(ap(out), ap(x), ap(y), op), [out], [x, y])
+
+    def ts(out, x, s1, op0, s2=None, op1=None):
+        if op1 is None:
+            rec("v", "ts", lambda e: e.tensor_scalar(ap(out), ap(x), ap(s1), None, op0), [out], [x, s1])
+        else:
+            rec("v", "ts", lambda e: e.tensor_scalar(ap(out), ap(x), ap(s1), ap(s2), op0, op1), [out], [x, s1, s2])
+
+    def scan(out, d0, d1, op0, op1):
+        rec("v", "ts", lambda e: e.tensor_tensor_scan(ap(out), ap(d0), ap(d1), 0.0, op0, op1), [out], [d0, d1])
+
+    def tr(out, x):
+        rec("v", "ts", lambda e: e.transpose(ap(out), ap(x)), [out], [x])
+
+    def top(out, x):
+        rec("v", "act", lambda e: e.tensor_reduce(ap(out), ap(x), AxisListType.X, OP.max), [out], [x])
+
+    def ms(out, c):
+        rec("v", "ts", lambda e: e.memset(ap(out), c), [out], [])
+
+    def act(out, x, func=None, bias=None, scale=None):
+        if bias is not None:
+            rec("s", "act", lambda e: e.activation(ap(out), ap(x), ACT.Identity, bias=ap(bias), scale=scale or 1.0), [out], [x, bias])
+        elif scale is not None:
+            rec("s", "act", lambda e: e.activation(ap(out), ap(x), ACT.Identity, scale=ap(scale)), [out], [x, scale])
+        else:
+            rec("s", "act", lambda e: e.activation(ap(out), ap(x), func or ACT.Copy), [out], [x])
+
+    def mm(out, lhs, rhs, start, stop):
+        rec("t", "mm", lambda e: e.matmul(ap(out), ap(lhs), ap(rhs), start, stop), [out], [lhs, rhs])
+        ops[-1]["edge"] = start or stop
+
+    def iota(out, pat, base, cm, flt=True):
+        if flt:
+            rec("g", "iota", lambda e: e.iota(ap(out), pat, base, cm, allow_small_or_imprecise_dtypes=True), [out], [])
+        else:
+            rec("g", "iota", lambda e: e.iota(ap(out), pat, base, cm), [out], [])
+        line("iota")
+
+    def dma(q, out, x, lat=2000.0, more=()):
+        s = "d%d" % ndma[0]
+        ndma[0] += 1
+        return rec(q, "dma", lambda e: e.dma_start(ap(out), ap(x)).then_inc(T.sem[s], 16), [out], [x], (s, 16), lat)
+
+    def col(j):
+        return A("cF", j, j + 1)
+
+    def swap(out0, n, srcs):
+        for q in range(2):
+            terms = [(g0, s) for s in srcs for g0 in range(2)]
+            for j, (g0, s) in enumerate(terms):
+                mm(A("pw", out0 + q, out0 + 2 * n, 2), A("LL", 128 * (2 * q + g0), 128 * (2 * q + g0 + 1)), s(g0), j == 0, j == len(terms) - 1)
+
+    dma("y", A("odi"), T.od[:], 2000.0)
+    dma("s", A("nbi", 0, 1024), T.nb[:, 0:1024], 5500.0)
+    dma("y", A("nbi", 1024, 2048), T.nb[:, 1024:2048], 5500.0)
+    dma("s", A("XT", 0, W), T.xs[:], 7000.0)
+    dma("y", A("XT", W, B), T.xs[:, 0:B - W], 7000.0)
+    iota(A("pci"), [[0, 1]], 0, 1, False)
+    iota(A("row"), [[1, 144]], 0, 0)
+    iota(A("R16"), [[16, 8], [0, 16]], 0, 0)
+    iota(A("kk"), [[0, 14], [1, 16]], 0, 0)
+    iota(A("R32"), [[32, 4], [0, 32]], 0, 0)
+    iota(A("lanb"), [[32, 7], [0, 2]], 0, 0)
+    iota(A("par"), [[0, 7], [16, 2]], 15, 0)
+    iota(A("VT", 0, B), [[1, B]], -2047, 0)
+    ms(A("thi"), 0)
+    dma("y", A("thi", p=(15, 128, 16)), T.th[:], 8000.0)
+    dma("y", A("wti"), T.wt[:], 8000.0)
+    for j, msk in enumerate((15, 112, 96, 16, 31, 127)):
+        ts(A("cI", j, j + 1), A("pci"), msk, OP.bitwise_and)
+    cp(A("cF", 0, 6), A("cI", 0, 6))
+    ms(A("one"), 1.0)
+    ms(A("DC", L, LP), 0.0)
+    ms(A("DC", LP + L, 2 * LP), 0.0)
+    ms(A("a1", L, LP), 1.0)
+    ms(A("a2", L, LP), 0.0)
+    ms(A("TT", W, B + 192), 0.0)
+    ms(A("cur"), float(L + B - 2047 - 4096))
+    ms(A("mk"), BIG)
+    ms(A("mex"), 0.0)
+    ms(A("kg", U, 64), 0.0)
+    ms(A("snd", 0, 3 * U), 0.0)
+    ts(A("oda"), A("odi"), 2047, OP.add)
+    cp(A("od16"), A("odi"))
+    ts(A("odb"), A("oda"), 2047, OP.bitwise_and)
+    cp(A("om16"), A("odb"))
+    ts(col(6), col(1), 15.0, OP.add)
+    ts(col(7), col(0), 0.0, OP.is_gt, float(3 * 2 ** 27), OP.mult)
+    ts(col(8), col(0), 2048.0, OP.mult)
+    ts(col(9), col(3), 0.0, OP.is_equal)
+    ts(col(10), col(3), 0.0, OP.is_gt)
+    ts(col(11), col(5), 16.0, OP.add)
+    ts(col(12), col(5), -16.0, OP.add)
+    ts(col(13), col(0), 15.0, OP.is_lt, BIG, OP.mult)
+    ts(col(14), col(7), float(2 ** 27), OP.add)
+    r128 = A("row", 0, 128)
+    ts(A("Ib"), r128, col(5), OP.is_equal)
+    ts(A("Z1"), A("row"), col(6), OP.is_equal)
+    ts(A("B1"), A("R16"), col(1), OP.is_equal)
+    ts(A("O32"), A("R32"), col(2), OP.is_equal)
+    ts(A("LL", 0, 128), r128, col(5), OP.is_equal, col(9), OP.mult)
+    ts(A("LL", 128, 256), r128, col(11), OP.is_equal, col(9), OP.mult)
+    ts(A("LL", 256, 384), r128, col(12), OP.is_equal, col(10), OP.mult)
+    ts(A("LL", 384, 512), r128, col(5), OP.is_equal, col(10), OP.mult)
+    ts(A("Lt"), r128, col(5), OP.is_gt)
+    tt(A("Lt"), A("Lt"), A("O32"), OP.mult)
+    for name, src, sc in (("ZG", "Z1", -32768.0), ("ZM", "Z1", 65536.0), ("ZA", "Z1", 32768.0), ("In", "Ib", -1.0), ("DK", "Ib", col(8)),
+                          ("DP", "Ib", col(14)), ("BO", "B1", -32768.0), ("I4", "Ib", -4096.0), ("I2", "Ib", -2048.0), ("O3f", "O32", 32768.0),
+                          ("If", "Ib", 1.0), ("Zn", "Z1", -1.0), ("Z2", "Z1", 2.0)):
+        act(A(name), A(src), scale=sc)
+    ts(A("Bn"), A("kk", 0, 128), float(KS), OP.is_ge, -1.0, OP.mult)
+    tt(A("Bn"), A("Bn"), A("B1"), OP.mult)
+    tt(A("LZ"), A("Lt"), A("I4"), OP.subtract)
+    tt(A("LW"), A("Lt"), A("I2"), OP.add)
+    ts(A("rst"), A("kk"), 0.0, OP.is_equal, BIG, OP.mult)
+    ts(A("rs1"), A("kk", 0, U), 0.0, OP.is_gt)
+    ts(A("dg"), A("kk", 0, U), col(0), OP.is_equal)
+    ts(A("lanc"), A("lanb"), col(4), OP.add, -1792.0, OP.add)
+    ts(A("LE", 14, 28), A("lanb"), col(4), OP.add, float(B - 2047), OP.add)
+    ts(A("dum"), A("lanc"), float(L - 1792), OP.is_ge, BIG, OP.mult)
+    ts(A("mRG"), A("par"), col(4), OP.is_equal)
+    cp(col(15), A("wti"))
+    cp(col(16), A("thi"))
+    act(A("WB"), A("B1"), scale=col(15))
+    ts(A("ytl", 0, 3), A("one", 0, 3), col(16), OP.mult)
+    ts(A("TT", 0, 1024), A("nbi", 0, 1024), -2047.0, OP.add)
+    ts(A("TT", 1024, W), A("nbi", 1024, W), -2047.0, OP.add)
+    zz = A("pz", 0, 14)
+    ww = A("pw", 0, 14)
+    kT = A("po", 256, 256 + LP)
+    kmin = A("ks", 15, LP, 16)
+
+    def spread_threshold(t):
+        if t:
+            ts(A("thx"), A("mRG"), A("ytl", t, t + 1), OP.mult)
+        else:
+            act(A("thx"), A("mRG"), scale=A("ytl", t, t + 1))
+        mm(A("pw", 112, 126), A("O3f"), A("thx"), True, True)
+        tt(A("thD"), A("pw", 112, 126), A("dum"), OP.max)
+        cp(A("thP"), A("pw", 112, 126))
+
+    def write_columns(lst):
+        cp(IND(A("TT", 0, W), lst), A("DC", LP, LP + L))
+
+    def guests_in(t):
+        j = t - 3
+        gin, xb = A("gin%d" % j), A("xb", U * (j % 2), U * (j % 2) + U)
+        rec(None, "", None, [gin], [], ("ga%d" % j, len(common)), 0.0, [sent["g", j]])
+        mag = 1.5 * 2 ** 32
+        ts(A("gr"), gin, mag, OP.add, -mag, OP.add)
+        tt(xb, gin, A("gr"), OP.subtract)
+        mm(A("pg", 0, U), A("WB"), xb, True, True)
+        tt(A("hm"), A("pg", 0, U), A("dg"), OP.mult)
+        scan(A("hs"), A("rs1"), A("hm"), OP.mult, OP.add)
+        ts(A("hi", 0, 3), A("hs", 15, U, 16), float(77 * t), OP.add)
+        ts(A("ha", 0, 3), A("hi", 0, 3), 2047, OP.bitwise_and)
+        cp(A("h16", 0, 3), A("ha", 0, 3))
+        ts(A("g16"), IND(A("TO%d" % j) if t in KEEP else A("TT", 0, W), A("h16", 0, 3)), 2047.0, OP.add)
+        act(A("cap", U * (j % 2), U * (j % 2) + U), A("gr"), bias=col(13), scale=2.0 ** -9)
+        h = GV[j]
+        act(A("Gg", 16 * h, 16 * U), IND(A("XT", 0, W), A("g16", h, U)))
+        if h:
+            cp(A("Gg", 0, 16 * h), IND(A("XT", 0, W), A("g16", 0, h)))
+
+    def sizes(src, first, n, mine, banks, out, at=0):
+        for bank, c0, k0, k1 in banks:
+            for k in range(k0, k1):
+                piece = A(bank, c0 + n * (k - k0), c0 + n * (k - k0 + 1))
+                mm(piece, A("Ib"), A(src, 16 * first + k, 16 * (first + n), 16), True, False)
+                mm(piece, A("In"), mine, False, True)
+            act(A(out, at + n * k0, at + n * k1), A(bank, c0, c0 + n * (k1 - k0)), ACT.Abs)
+
+    def guests_judged(t):
+        j = t - 3
+        xb, key = A("xb", U * (j % 2), U * (j % 2) + U), A("pg", 64, 64 + U)
+        if GK[j]:
+            sizes("Gg", 0, U, xb, [("pc", 0, 0, KS)], "Ag")
+            mm(key, A("Bn"), xb, True, False)
+            for k in range(KS, 16):
+                mm(key, A("Zn", 15 - k, 143 - k), A("Gg", k, 16 * U, 16), False, False)
+            for k in range(KS, 16):
+                tt(A("Ag", U * k, U * k + U), A("Gg", k, 16 * U, 16), xb, OP.max)
+                mm(key, A("Z2", 15 - k, 143 - k), A("Ag", U * k, U * k + U), False, False)
+            for k in range(KS):
+                mm(key, A("Z1", 15 - k, 143 - k), A("Ag", U * k, U * k + U), False, k == KS - 1)
+        else:
+            sizes("Gg", 0, U, xb, [("pc", 0, 0, 10), ("pg", 128, 10, 16)], "Ag")
+            for k in range(16):
+                mm(key, A("Z1", 15 - k, 143 - k), A("Ag", U * k, U * k + U), k == 0, k == 15)
+        tt(A("kg", 0, U), A("pg", 64, 64 + U), A("cap", U * (j % 2), U * (j % 2) + U), OP.min)
+        tr(A("kgT"), A("kg"))
+        scan(A("js"), A("rst", 0, 64), A("kgT"), OP.add, OP.min)
+        tr(A("jC"), A("js"))
+        mine = A("bt", 16 * j + 4 * rank, 16 * j + 4 * rank + 1)
+        top(mine, A("jC"))
+        masks = best_masks(core, cores, topo)
+
+        def send(e):
+            trs = []
+            for c, (msk, _) in masks.items():
+                rid, pid = topo.addr(c, core)
+                trs.append(RemoteDMATransfer(dst_ids=[DstId(rid=rid, pnc=pid)], dma_engine_mask=msk, remote_sem=T.sem["ba%d" % j],
+                                             src=ap(mine), dst=ap(mine)))
+            return e.remote_dma_fused(trs, local_sem=T.sem["left%d" % (3 + j)])
+        sent["b", j] = rec("g", "", send, [], [mine], ("left%d" % (3 + j), sum(n for _, n in masks.values())), NOM["rem"])
+
+    def threshold(t):
+        j = t - 3
+        n = sum(best_masks(c, cores, topo)[core][1] for c in cores if c != core)
+        old = A("ytl", t - 1, t)
+        act(A("th4", j, j + 1), old, bias=0.375, scale=0.25)
+        rec(None, "", None, [A("bt", 16 * j + 4 * r, 16 * j + 4 * r + 1) for r in range(NR) if r != rank], [], ("ba%d" % j, n), 0.0, [sent["b", j]])
+        top(A("bc", j, j + 1), A("bt", 16 * j, 16 * j + 16, 4))
+        ts(A("bi"), A("bc", j, j + 1), 0.25, OP.mult, A("th4", j, j + 1), OP.subtract)
+        ts(A("ytl", t, t + 1), A("bi"), 0.0, OP.max, old, OP.add)
+
+    def floor_m(scale):
+        ts(A("mi"), A("mn"), 2.0 ** -15, OP.mult, -0.46875, OP.add)
+        ts(A("mex", 15, LP, 16), A("mi"), 4095.0, OP.min, scale, OP.mult)
+        tr(A("mC"), A("mex"))
+
+    spread_threshold(0)
+    for t in range(NT):
+        now[0] = t
+        hi = B + L * (t + 1)
+        came = 3 <= t
+        leave = 2 <= t <= 4
+        e16 = A("L16", 14, 27)
+        cc = A("DC", LP, LP + L)
+        if t == 0:
+            own, vrep, ownat = A("XT", B, B + L), A("VT", B, B + L), ("XT", B)
+            ts(A("c16"), IND(A("nbi"), A("om16", 0, 13)), 1.0, OP.add)
+            act(A("XT", B, B + LP), IND(A("XT", 0, W), A("od16", 0, 14)))
+            act(A("VT", B, B + LP), IND(A("VT", 0, W), A("od16", 0, 14)))
+            raw = A("cr")
+            ts(raw, A("c16"), -2047.0, OP.add)
+        else:
+            own, vrep, ownat = A("own"), IND(A("VT", 0, hi), e16), ("own", 0)
+            raw = IND(A("TT", 0, hi), A("L16", 0, 13))
+            act(own, IND(A("XT", 0, hi), e16))
+            ts(A("c16"), raw, 2047.0, OP.add)
+        if VG[t]:
+            cp(A("G", 0, 16 * VG[t]), IND(A("XT", 0, B), A("c16", 0, VG[t])))
+        for l0, l1, how in CH[t]:
+            l0 = max(l0, VG[t])
+            act(A("G", 16 * l0, 16 * l1), IND(A("XT", 0, B), A("c16", l0, l1)))
+            line("s")
+        mm(A("po", 0, L), A("Ib"), own, True, True)
+        ts(A("fl"), A("c16"), 2048.0, OP.is_ge, -2048.0, OP.mult)
+        tt(cc, raw, A("fl"), OP.add)
+        tt(A("DC", 0, L), vrep, cc, OP.subtract)
+        ts(A("a1", 0, L), A("DC", 0, L), -16.0, OP.is_gt)
+        ts(A("a2", 0, L), A("DC", 0, L), 16.0, OP.is_ge, -1.0, OP.mult)
+        if t == 0:
+            tr(A("DT", LP, 2 * LP), A("DC", LP, 2 * LP))
+            v16 = A("od16", 0, 13)
+        else:
+            tr(A("DT"), A("DC"))
+            swap(64, 7, [lambda g0: A("DT", 16 * g0, LP, 32), lambda g0: A("DT", LP + 16 * g0, 2 * LP, 32)])
+            ts(A("v16"), A("pw", 64, 78), 2047.0, OP.add)
+            v16 = A("v16", 0, 13)
+        if leave:
+            act(A("ownf"), own)
+        if t >= 4:
+            guests_judged(t - 1)
+            threshold(t - 1)
+        if t == 4:
+            spread_threshold(3)
+        if came and t not in KEEP:
+            guests_in(t)
+        write_columns(v16)
+        if t + 1 in KEEP:
+            sent["copy", t - 2] = dma("y", A("TO%d" % (t - 2)), A("TT", 0, W), 5000.0)
+        if t in KEEP:
+            guests_in(t)
+        mm(A("pk", 0, LP), A("DK"), A("one"), True, False)
+        mm(A("pk", 0, LP), A("DP"), A("a1"), False, False)
+        mm(A("pk", 0, LP), A("DP"), A("a2"), False, False)
+        for n, (l0, l1, how) in enumerate(CH[t]):
+            mine = A(ownat[0], ownat[1] + l0, ownat[1] + l1)
+            end = n == len(CH[t]) - 1
+            if how == "s":
+                sizes("G", l0, l1 - l0, mine, [("pa", 0, 0, 8), ("pb", 0, 8, 16)], "AA", 16 * l0)
+                for k in range(16):
+                    at = 16 * l0 + (l1 - l0) * k
+                    mm(A("pk", l0, l1), A("ZA", 15 - k, 143 - k), A("AA", at, at + l1 - l0), False, end and k == 15)
+                continue
+            mm(A("pk", l0, l1), A("BO"), mine, False, False)
+            for k in range(16):
+                mm(A("pk", l0, l1), A("ZG", 15 - k, 143 - k), A("G", 16 * l0 + k, 16 * l1, 16), False, False)
+            for k in range(16):
+                tt(A("M", L * k + l0, L * k + l1), A("G", 16 * l0 + k, 16 * l1, 16), A("po", l0, l1), OP.max)
+                line("v")
+                mm(A("pk", l0, l1), A("ZM", 15 - k, 143 - k), A("M", L * k + l0, L * k + l1), False, end and k == 15)
+        tr(kT, A("pk", 0, LP))
+        scan(A("ks"), A("rst"), kT, OP.add, OP.min)
+        tt(A("mn"), kmin, A("mk"), OP.min)
+        if t == 5:
+            guests_judged(t)
+            dma("y", T.yg[:], A("jC", 0, U, p=(15, 128, 16)))
+            floor_m(1.0)
+            dma("s", T.ym[:], A("mC", 0, L, p=(15, 128, 16)))
+            for h in range(2):
+                act(A("yno", 384 * h, 384 * h + 384), IND(A("TT", 0, W), A("od16", 24 * h, 24 * h + 24)), bias=2047.0)
+                dma("y", T.yn[:, 384 * h:384 * h + 384], A("yno", 384 * h, 384 * h + 384), 2800.0)
+            act(A("vf"), vrep, bias=2047.0)
+            dma("y", T.yv[:], A("vf", p=(0, 128, 16)))
+            threshold(5)
+            dma("y", T.yt[:], A("ytl", 0, NT, p=(15, 128, 16)))
+            break
+        act(A("TT", B + 192, hi + L), IND(A("TT", 0, W), A("om16", 12, 13 * (t + 2))), bias=1.0)
+        if t in OD:
+            j0, j1 = OD[t]
+            act(A("XT", B + 16 * j0, B + 16 * j1), IND(A("XT", 0, W), A("od16", j0, j1)))
+            act(A("VT", B + 16 * j0, B + 16 * j1), IND(A("VT", 0, W), A("od16", j0, j1)))
+        low = A("mn") if t == 4 else kmin
+        tt(A("dead"), low, A("thP"), OP.is_lt)
+        fr = A("dead")
+        if leave:
+            tt(A("FF"), A("F0"), A("F1"), OP.max)
+            tt(A("thG"), A("FF"), A("thD"), OP.max)
+            tt(A("go"), low, A("thG"), OP.is_ge)
+            mm(ww, A("LW"), A("go"), True, False)
+            for d in range(1, 7):
+                mm(A("pw", 2 * d, 14), A("O32"), A("go", 0, 14 - 2 * d), False, d == 6)
+            ts(A("thrD"), A("dead"), 4096.0, OP.mult, -2000.0, OP.add)
+            fr = A("free")
+            tt(fr, ww, A("thrD"), OP.is_lt)
+            tt(A("slt"), ww, A("lanc"), OP.min)
+        mm(zz, A("If"), A("cur"), True, False)
+        mm(zz, A("LZ"), fr, False, False)
+        for d in range(1, 7):
+            mm(A("pz", 2 * d, 14), A("O32"), A(fr[1], 0, 14 - 2 * d), False, d == 6)
+        tt(kT, A("ks"), kT, OP.subtract)
+        tt(A("yy"), A("DT", LP, 2 * LP), kT, OP.subtract)
+        scan(A("nr"), kT, A("yy"), OP.max, OP.min)
+        tt(A("LE", 14, 28), zz, A("LE", 14, 28), OP.max)
+        tt(A("LE", 0, 14), zz, A("nr", 15, LP, 16), OP.max)
+        if leave:
+            swap(96, 7, [lambda g0: A("slt", g0, 14, 2)])
+        swap(16, 14, [lambda g0: A("LE", g0, 28, 2)])
+        ts(A("L16"), A("pw", 16, 44), 2047.0, OP.add)
+        if t < 4:
+            mm(A("pz", 16, 30), A("If"), A("cur"), True, False)
+            for d in range(1, 7):
+                mm(A("pz", 16, 30 - 2 * d), A("O32"), A(fr[1], 2 * d, 14), False, False)
+                mm(A("pz", 16 + 2 * d, 30), A("O32"), A(fr[1], 0, 14 - 2 * d), False, False)
+            mm(A("pz", 16, 30), A("O32"), fr, False, True)
+            act(A("cur"), A("pz", 16, 30))
+        Fp = A("F%d" % (t % 2))
+        act(Fp, fr, scale=BIG)
+        if leave:
+            j = t - 2
+            ts(A("s16"), A("pw", 96, 110), 2048.0, OP.add)
+            floor_m(512.0)
+            s0 = U * (2 - j)
+            tt(IND(A("snd", s0, s0 + 464), A("s16", 0, 13)), A("mC", 0, L), A("ownf"), OP.add)
+            dst = cores[(rank + 1 + t % (NR - 1)) % NR]
+
+            def send(e, dst=dst, s0=s0, j=j):
+                rid, pid = topo.addr(dst, core)
+                return e.remote_dma(ap(A("gin%d" % j)), ap(A("snd", s0, s0 + U)), T.sem["ga%d" % j], T.sem["left%d" % j], pid, rid,
+                                    sum(1 << x for x in common))
+            sent["g", j] = rec("g", "", send, [], [A("snd", s0, s0 + U)], ("left%d" % j, len(common)), NOM["rem"] + (NOM["first"] if j == 0 else 0.0),
+                                [sent["copy", j]] if ("copy", j) in sent else [])
+        tt(A("mk"), A("mn"), Fp, OP.max)
+    emit(g, T, ops)

@@ -1,3 +1,4 @@
+import math
 from concourse.bass import DstId, RemoteDMATransfer
 from concourse.mybir import AluOpType, AxisListType, ActivationFunctionType
 
@@ -6,19 +7,47 @@ B = 2064
 LP = 224
 H = "float16"
 BIG = float(2 ** 30)
-CH = [[(0, a, h[0]), (a, b, h[1]), (b, L, h[2])] for a, b, h in
-      ((80, 144, "vsv"), (80, 144, "vsv"), (64, 128, "vsv"), (80, 144, "vsv"), (64, 144, "svs"), (80, 144, "vss"))]
-VG = [32, 0, 32, 32, 16, 32]
-GV = [0, 0, 24]
-GK = [0, 0, 1]
-KS = 8
-KEEP = [3, 4]
-OD = {0: (14, 46), 1: (46, 66), 2: (66, 78)}
-NOM = {"cyc": 0.83, "gat": 1.56, "sca": 3.8, "fix": 20.0, "pe": 0.42, "sem": 80.0, "pel": 60.0, "rem": 2800.0, "first": 2500.0, "lam": 2.0}
-BIAS = {'3vdead': 1500, '0sG': -3000, '3vM': -1500, '0vDT': -3000, '1tpb': -250, '2vdead': 250, '5tpb': -250, '3vyy': -600,
-        '3vhm': -1500, '3vpo': -1500, '3vslt': -250, '3vDT': 600, '4vhm': -1500, '3vgr': -1500, '4vpo': -600, '2vM': -3000, '2vDC': -600,
-        '2vgo': 3000, '4vG': -1500, '4scap': 1500, '2vG': 600, '5tpa': 600, '9vTT': 3000, '9vLZ': -3000, '5vDT': -3000, '5vkgT': -3000,
-        '2va1': -1500}
+
+
+def cells(text):
+    ends = [int(x[:-2]) for x in text.split()]
+    return [(a, b, x[-2], x[-1]) for a, b, x in zip([0] + ends, ends, text.split())]
+
+
+PAR = {
+    "two": True,
+    "kb": 128,
+    "pieces": [cells(x) for x in ["64vk 128sk 208sk"] + ["64sk 128sk 208sk"] * 5],
+    "sums": [[0, 64, 128, 208]] * 6,
+    "oq": "vvvsss",
+    "c0": 0,
+    "guests": [[(0, 32, "s", "s"), (32, 48, "s", "s")]] * 2 + [[(0, 32, "v", "v"), (32, 48, "s", "s")]],
+    "ring": [4, 4, 4, 2, 2, 2], "gb": [2, 2, 2], "gv": [0, 0, 24], "g2": True,
+    "gpos": [0, 0, 0], "xq": "s", "gofirst": [2, 3, 4], "clear": True, "efirst": [],
+    "ks": [[0, 8, 6], [4, 4, 6], [8, 8, 6], [8, 8, 6], [8, 8, 6], [8, 8, 6]],
+    "keep": [3, 4],
+    "split": [],
+}
+PAR.update({"two": False, "c0": 64, "g2": False, "gb": [3, 3, 2], "gv": [24, 0, 24], "clear": False,
+            "pieces": [cells(x) for x in ["64vk 128sk 208sk"] + ["32vk 64sk 128sk 208sk"] * 2 + ["64sk 128sk 208sk"] * 3],
+            "ks": [[0, 8, 8], [0, 8, 6], [0, 8, 6], [8, 8, 6], [8, 8, 6], [0, 4, 6]],
+            "guests": [[(0, 32, "v", x), (32, 48, "s", "s")] for x in "vsv"]})
+NOM = {"cyc": 0.83, "gat": 1.56, "sca": 3.8, "vfix": 20.0, "sfix": 50.0, "pe": 0.42, "sem": 80.0, "pel": 60.0, "rem": 3300.0, "w": 0.0, "wt": 0.0, "issue": 1000.0, "seed": 5,
+       "first": 2500.0, "passes": 3, "far": 1.0, "tries": 170000, "hot": 600.0, "cold": 8.0, "early": 0.0, "self": 30.0, "lead": 4.0 * PAR["two"], "nb": 5500.0, "xs": 7200.0, "copy": 6000.0}
+DUE = {"c0": 0, "own": 0.1, "G0": 0.2, "c1": 0.3, "oT": 0.4, "G1": 0.5, "G2": 1, "G3": 1.5, "D0": 1.1, "D1": 1.5, "D2": 2.2,
+       "M0": 1.2, "M1": 1.6, "M2": 2.3, "cc": 1.3, "dif": 1.4, "a1": 3, "DT": 3.1, "v16": 3.2, "wr": 3.3, "ini": 3,
+       "SG0": 3.5, "SM0": 3.6, "SA0": 3.65, "SG1": 3.7, "SM1": 3.8, "SA1": 3.85, "SG2": 3.9, "SM2": 4, "SA2": 4.05,
+       "k0": 4.5, "n0": 4.6, "k1": 5, "fate": 5.1, "n1": 5.2, "LE": 5.3, "LN": 5.35, "L16": 5.4, "slt": 5.5, "mn": 5.55, "s16": 5.6, "pack": 5.7,
+       "seed": 6, "tab": 7, "out": 8, "cur": 12, "tt0": -90, "tt1": -90, "tt2": -87, "tt3": -87,
+       "2wr": -2, "2v16": -2, "2mn": 5.1, "2s16": 5.15, "2pack": 5.2, "3gh": -5, "3gG": -5, "3gM": -5, "3gj": -5, "3thr": -5,
+       "4DT": 8, "4n0": 8, "4n1": 8.1, "4LE": 8.2, "4LN": 8.3, "4L16": 8.4, "4wr": 9, "4v16": 9, "4seed": 9.5,
+       "4gh": 11, "4gG": 11.1, "4gM": 11.2, "4gj": 11.3, "4thr": 19, "5gh": -1, "5gG": -1, "5gM": -1, "5gj": -1, "5thr": -1}
+DUE = {'c0': -19.67, 'own': -4.77, 'G0': 4.33, 'c1': 15.8, 'oT': 7.26, 'G1': -5.14, 'G2': 22.26, 'G3': -5.52, 'D0': 1.97, 'D1': 0.24, 'D2': 1.57, 'M0': -14.71, 'M1': -2.4, 'M2': 20.56, 'cc': 5.29, 'dif': 27.91, 'a1': 12.61, 'DT': -12.14, 'v16': 17.2, 'wr': 6.19, 'ini': 9.62, 'SG0': 14.13, 'SM0': 20.11, 'SA0': 2.53, 'SG1': -3.69, 'SM1': -8.32, 'SA1': 13.36, 'SG2': 13.53, 'SM2': -10.25, 'SA2': -16.19, 'k0': 3.89, 'n0': 5.74, 'k1': -1.64, 'fate': 9.7, 'n1': 0.33, 'LE': 14.68, 'LN': 0.72, 'L16': 6.18, 'slt': 14.62, 'mn': 30.29, 's16': 15.6, 'pack': 5.81, 'seed': 7.37, 'tab': 12.11, 'out': 10.0, 'cur': 8.62, 'tt0': -90, 'tt1': -90, 'tt2': -87, 'tt3': -87, '2wr': 0.25, '2v16': -2.0, '4DT': 0.63, '4n1': 9.35, '4LN': 6.17, '4gh': 9.25, '4gG': 11.1, '4gj': 19.18, '4thr': 24.75, '5gh': -0.88, '5gj': -3.5, '2dif': -3.48, '2SA2': 10.92, '5c0': -0.75, 'gj': -5.38, '1k1': 10, '2SM1': 5.8, 'gh': -6.63, '3k1': 4.87, '0SA2': 10.79, 'gM': 15.99, '3M0': 1.32, 'mk': 12.64, '4SM1': 3.17, '5SA2': 7.05, '1c0': -1.63, '3DT': -7.15, '3own': -8.91, 'gG': 0.36, '4SA2': 5.42, '1SA2': 6.05, 'th': 1.75, '4M0': 2.58, '5SG2': 1.66, '1wr': 2.17, '4c0': -2.25, '1dif': -10.34, '2M1': -1.53, '2c0': -3.24, '1SM1': -1.95, 'ownf': 3.24, '5SG1': 0.57, '3c0': -8.87, '1G3': -2.0, '4k1': 17.37, '3SA1': 3.35, 'thr': 4.88, '5M0': 1.83, '2M0': -2.43, '4th': 11.5, '2DT': -1.16, '5SM1': 6.55, '2SG2': -1.21, '3SM2': 11.38, '5SM2': 3.63, '3SA2': 4.3, '2SM2': 3.26, '5k1': 6.37, '4SM2': 6.75, '3D1': 3.38, '3SM1': 0.18, '1n1': 7.21, '1SM2': 11.75, '3ownf': 3.37, '1DT': -3.53, '1M0': -0.55, '2G3': 10.75, '2k1': 12.13, '0cur': 6.25, '0k1': 15.37, '1SG0': -5.12, '1ini': 1.62, '2G1': 6.24, '4D1': 3.64, '3n1': 11.09, '4M1': 4.97, '0SM2': 0.75, '3LN': 3.72, '3SA0': 12.02, '1LN': 3.22, '2n1': 11.34, '4pack': 2.32, '5G0': 0.2, '5G1': -0.51}
+NOM.update({"passes": 2, "tries": 48000, "sem": 130.0, "self": 110.0, "hot": 250.0, "seed": 43})
+BIAS = DUE
+VARIANTS = [{"sem": 130.0, "self": 110.0, "sfix": 50.0, "gat": 1.3, "sca": 3.0},
+            {"vfix": 26.0, "sfix": 80.0, "sem": 140.0, "self": 120.0, "pel": 70.0, "cyc": 1.08, "pe": 0.55, "gat": 1.8, "sca": 4.8, "far": 1.15}]
+ORDER = {}
 F, BF, I, U16 = "float32", "bfloat16", "int32", "uint16"
 
 
@@ -26,33 +55,38 @@ def _sb(n, d):
     return ("sbuf", [128, n], d)
 
 
+def _ps():
+    return ("psum", [128, 512], F)
+
+
 SCRATCH = {
     "nbi": _sb(W, I), "TT": _sb(B + Q, F), "XT": _sb(B + Q, BF), "VT": _sb(B + Q, F),
-    "TO0": _sb(W, F), "TO1": _sb(W, F), "TO2": _sb(W, F), "odi": _sb(78, I), "oda": _sb(78, I), "odb": _sb(78, I), "od16": _sb(78, U16), "om16": _sb(78, U16),
-    "G": _sb(16 * L, BF), "M": _sb(16 * L, BF), "AA": _sb(16 * L, BF), "Gg": _sb(16 * U, BF), "Ag": _sb(16 * U, BF),
-    "own": _sb(L, BF), "ownf": _sb(L, F), "c16": _sb(L, U16), "cr": _sb(L, H), "fl": _sb(L, H),
-    "DC": _sb(2 * LP, H), "DT": _sb(2 * LP, H), "a1": _sb(LP, BF), "a2": _sb(LP, BF),
-    "ks": _sb(LP, F), "yy": _sb(LP, F), "nr": _sb(LP, F), "mex": _sb(LP, F), "mC": _sb(LP, F),
-    "dead": _sb(14, BF), "go": _sb(14, BF), "free": _sb(14, BF), "thrD": _sb(14, F),
+    "TO0": _sb(W, F), "TO1": _sb(W, F), "odi": _sb(78, I), "oda": _sb(78, I), "odb": _sb(78, I), "od16": _sb(78, U16), "om16": _sb(78, U16),
+    "G": _sb(16 * L, BF), "M": _sb(16 * L, BF), "Gg": _sb(16 * U, BF), "Ag": _sb(16 * U, BF),
+    "own": _sb(2 * 320, BF), "oT": _sb(512, BF), "xT": _sb(128, BF), "Z0": _sb(128, BF), "RP": _sb(512, BF), "ownf": _sb(L, F), "c16": _sb(L, U16), "cr": _sb(L, H), "fl": _sb(L, H),
+    "DC": _sb(2 * LP, H), "DT": _sb(2 * LP, H), "a1": _sb(LP, BF),
+    "ks": _sb(2 * LP, F), "yy": _sb(LP, F), "nr": _sb(LP, F), "mex": _sb(LP, F), "mC": _sb(LP, F),
+    "dead": _sb(14, BF), "go": _sb(14, BF), "fr": _sb(42, BF),
     "LE": _sb(28, H), "L16": _sb(28, U16), "slt": _sb(14, H), "s16": _sb(14, U16), "v16": _sb(14, U16),
-    "mk": _sb(14, F), "mn": _sb(14, F), "mi": _sb(14, I), "F0": _sb(14, F), "F1": _sb(14, F), "FF": _sb(14, F),
-    "thP": _sb(14, F), "thD": _sb(14, F), "thG": _sb(14, F), "thx": _sb(14, F), "cur": _sb(14, F),
-    "row": _sb(144, F), "pci": _sb(1, I), "cI": _sb(8, I), "cF": _sb(24, F), "R16": _sb(128, F), "R32": _sb(128, F),
-    "lanb": _sb(14, F), "par": _sb(14, F), "kk": _sb(LP, F), "lanc": _sb(14, F), "dum": _sb(14, F), "mRG": _sb(14, F),
-    "Zn": _sb(144, BF), "Z2": _sb(144, BF), "Bn": _sb(128, BF), "Z1": _sb(144, BF), "ZM": _sb(144, BF), "ZG": _sb(144, BF), "ZA": _sb(144, BF), "Ib": _sb(128, BF), "In": _sb(128, BF),
-    "If": _sb(128, F), "B1": _sb(128, BF), "BO": _sb(128, BF), "WB": _sb(128, BF), "DP": _sb(128, BF), "DK": _sb(128, BF),
-    "O32": _sb(128, BF), "O3f": _sb(128, F), "Lt": _sb(128, BF), "LZ": _sb(128, BF), "LW": _sb(128, BF),
-    "I4": _sb(128, BF), "I2": _sb(128, BF), "LL": _sb(512, H),
-    "one": _sb(LP, BF), "rst": _sb(LP, F), "rs1": _sb(U, F), "dg": _sb(U, F),
+    "mn": _sb(14, F), "mi": _sb(14, I), "thP": _sb(14, F), "thx": _sb(28, F), "cur": _sb(14, F),
+    "row": _sb(160, BF), "IW": _sb(160, BF), "cI": _sb(6, I), "cF": _sb(12, F), "R16": _sb(128, BF), "R32": _sb(128, BF), "kk": _sb(LP, BF),
+    "lanb": _sb(14, F), "par": _sb(14, F), "lanc": _sb(14, F), "mRG": _sb(14, F),
+    "Zn": _sb(144, BF), "Z2": _sb(144, BF), "Z1": _sb(144, BF), "ZM": _sb(144, BF), "ZG": _sb(144, BF), "WZ": _sb(144, BF),
+    "Bn": _sb(128, BF), "Ib": _sb(128, BF), "In": _sb(128, BF), "If": _sb(128, F), "B1": _sb(128, BF), "BO": _sb(128 * 8, BF),
+    "DP": _sb(128, BF), "DK": _sb(128, BF), "O32": _sb(128, BF), "O3f": _sb(128, F), "Lt": _sb(128, BF), "LZ": _sb(128, BF), "LW": _sb(128, BF),
+    "ID": _sb(128, BF), "IB": _sb(128, BF), "LL": _sb(512, BF),
+    "one": _sb(LP, BF), "rst": _sb(LP, F),
     "wti": _sb(1, I), "thi": _sb(1, I), "ytl": _sb(8, F), "th4": _sb(4, F),
-    "snd": _sb(560, F), "gin0": _sb(U, F), "gin1": _sb(U, F), "gin2": _sb(U, F),
-    "gr": _sb(U, F), "xb": _sb(2 * U, BF), "cap": _sb(2 * U, F), "hm": _sb(U, F), "hs": _sb(U, F), "hi": _sb(4, I), "ha": _sb(4, I),
+    "snd": _sb(528, F), "gin0": _sb(U, F), "gin1": _sb(U, F), "gin2": _sb(U, F),
+    "gr": _sb(U, F), "xb": _sb(2 * U, BF), "cap": _sb(2 * U, F), "hi": _sb(4, I), "ha": _sb(4, I),
     "h16": _sb(4, U16), "g16": _sb(U, U16), "kg": _sb(64, F), "kgT": _sb(64, F), "js": _sb(64, F), "jC": _sb(64, F),
-    "bt": _sb(48, F), "bc": _sb(4, F), "bi": _sb(1, I), "vf": _sb(L, F), "yno": _sb(KN, F),
-    "pk": ("psum", [128, 512], F), "po": ("psum", [128, 512], F), "pz": ("psum", [128, 512], F), "pw": ("psum", [128, 512], F),
-    "pa": ("psum", [128, 512], F), "pb": ("psum", [128, 512], F), "pc": ("psum", [128, 512], F), "pg": ("psum", [128, 512], F),
+    "bt": _sb(48, F), "bc": _sb(4, F), "bi": _sb(1, I), "vf": _sb(L, F), "yno": _sb(B + Q, F), "cf": _sb(L, F),
+    "pk0": _ps(), "pk1": _ps(), "po0": _ps(), "pg": _ps(),
+    "pr": ("psum", [128, 1536 if PAR["two"] else 2048], F),
 }
-NDMA = 17
+if PAR["two"]:
+    SCRATCH["po1"] = _ps()
+NDMA = 19
 SEMAPHORES = (["qv", "qs", "qt", "qg", "ga0", "ga1", "ga2", "ba0", "ba1", "ba2"] + ["left%d" % j for j in range(6)]
               + ["d%d" % j for j in range(NDMA)])
 OP = AluOpType
@@ -77,8 +111,8 @@ def duration(kind, outs, ins):
     full = [a for a in outs + ins if isinstance(a, tuple)]
     if kind == "mm":
         return max(64, width(ins[1])) * NOM["pe"] * (4 if SCRATCH[ins[1][1]][2] == F else 1)
-    if kind == "iota":
-        return 130 + 2 * NOM["cyc"] * width(outs[0])
+    if kind in ("iota", "pick"):
+        return (130 if kind == "iota" else 170) + 2 * NOM["cyc"] * width(outs[0])
     ind = [a for a in full if a[0] == "i"]
     if ind:
         return 60 + width(ind[0]) * NOM["cyc"] * (NOM["sca"] if ind[0] is outs[0] else NOM["gat"])
@@ -86,9 +120,9 @@ def duration(kind, outs, ins):
     c = 1.0
     if kind == "tt":
         c = 1.0 if any(SCRATCH[a[1]][0] == "psum" for a in ins) else 2.0
-    elif kind != "act" and all(SCRATCH[a[1]][2] in (BF, H, U16) for a in full if width(a) == n):
+    elif kind not in ("act", "red") and all(SCRATCH[a[1]][2] in (BF, H, U16) for a in full if width(a) == n):
         c = 0.5
-    return max(64, n * c) * NOM["cyc"] + NOM["fix"]
+    return max(64, n * c) * NOM["cyc"] + NOM["sfix" if kind == "act" else "vfix"]
 
 
 def best_masks(src, cores, topo):
@@ -116,10 +150,11 @@ def plan(ops):
                     continue
                 same = ops[m]["q"] == o["q"] and ops[m]["tok"] is None and o["tok"] is None
                 over = d0 < c1 and c0 < d1 and not (st == ds and (c0 - d0) % st)
+                bank = ps and d0 // 512 <= (c1 - 1) // 512 and c0 // 512 <= (d1 - 1) // 512
                 if same and o["q"] == "t":
-                    if ps and (o["edge"] or ops[m]["edge"]):
+                    if bank and (o["edge"] or ops[m]["edge"]):
                         after.add(m)
-                elif (ps and not same) or (over and (dw or wr)):
+                elif (bank and not same) or (over and (dw or wr)):
                     deps.add(m)
             seen.setdefault(name, []).append((n, c0, c1, st, wr))
         if o["line"] is not None:
@@ -136,53 +171,236 @@ def plan(ops):
             if not done >> m & 1:
                 kept.add(m)
                 done |= ops[m]["done"] | ops[m]["ahead"] | 1 << m
+        if o["q"] is None:
+            done, ahead = 0, 0
         o["done"], o["ahead"] = done, ahead
         o["deps"], o["after"] = kept, near - kept
-    return schedule(ops)
+    if len(ops) not in ORDER:
+        ORDER[len(ops)] = schedule(ops)
+    return ORDER[len(ops)]
 
 
 def schedule(ops):
-    succ = [[] for _ in ops]
+    N = len(ops)
+    pred, succ = [[] for _ in ops], [[] for _ in ops]
     for n, o in enumerate(ops):
         for m in o["deps"] | o["after"]:
-            succ[m].append(n)
-    rest = [0.0] * len(ops)
-    for n in range(len(ops) - 1, -1, -1):
-        o = ops[n]
-        rest[n] = o["dur"] + max([0.0] + [rest[s] + (o["lat"] + NOM["sem"] if n in ops[s]["deps"] else 0.0) for s in succ[n]] + [o["lat"]])
-    for n in range(5):
-        rest[n] += 1e6 * (5 - n)
-    rest = [r + BIAS.get(o["tag"], 0) for r, o in zip(rest, ops)]
-    miss = [len(o["deps"] | o["after"]) for o in ops]
-    ready = [n for n in range(len(ops)) if miss[n] == 0]
-    at = [0.0] * len(ops)
-    free, order = {}, []
+            gap = 0.0 if m not in o["deps"] else ops[m]["lat"] + NOM["self" if ops[m]["q"] == o["q"] else "sem"]
+            pred[n].append((m, gap))
+            succ[m].append((n, gap))
+    rest = [0.0] * N
+    for n in range(N - 1, -1, -1):
+        rest[n] = ops[n]["dur"] + max([ops[n]["lat"]] + [rest[s] + gap for s, gap in succ[n]])
+
+    def place(key, edges, others, first):
+        miss = [len(e) for e in edges]
+        start, busy, seq = [0.0] * N, {}, []
+        todo, at, ready, waiting = sorted(range(N), key=key), 0, [], set()
+        while len(seq) < N:
+            if ready:
+                n = min(ready, key=key)
+                ready.remove(n)
+            else:
+                n = todo[at]
+                at += 1
+                if miss[n]:
+                    waiting.add(n)
+                    continue
+            t = max([first[n]] + [start[m] + ops[m]["dur"] + gap for m, gap in edges[n]])
+            if ops[n]["q"]:
+                row = busy.setdefault(ops[n]["q"], [])
+                lo, hi = 0, len(row)
+                while lo < hi:
+                    mid = (lo + hi) // 2
+                    if row[mid][1] <= t:
+                        lo = mid + 1
+                    else:
+                        hi = mid
+                while lo < len(row) and row[lo][0] < t + ops[n]["dur"]:
+                    t = max(t, row[lo][1])
+                    lo += 1
+                row.insert(lo, (t, t + ops[n]["dur"]))
+            start[n] = t
+            seq.append(n)
+            for s, _ in others[n]:
+                miss[s] -= 1
+                if miss[s] == 0 and s in waiting:
+                    waiting.remove(s)
+                    ready.append(s)
+        return start, seq
+
+    zero, tail = [0.0] * N, [o["lat"] for o in ops]
+    loads = [1e6 * max(0, 4 - n) for n in range(N)]
+    prio = [0.0] * N
+    for n in range(N - 1, -1, -1):
+        t, c, name = ops[n]["tag"]
+        own = 10 * t + NOM["lead"] * c + DUE.get("%d%s" % (t, name), DUE.get(name, 99))
+        prio[n] = min([own - loads[n]] + [prio[s] for s, _ in succ[n]])
+    best = None
+    for _ in range(NOM["passes"]):
+        start, seq = place(lambda n: (prio[n], -rest[n], n), pred, succ, zero)
+        end = max(start[n] + ops[n]["dur"] + tail[n] for n in range(N))
+        if best is None or end < best[0]:
+            best = (end, start, {n: j for j, n in enumerate(seq)})
+        back, _ = place(lambda n: (-start[n] - ops[n]["dur"], -n), succ, pred, tail)
+        prio = [-back[n] - ops[n]["dur"] - loads[n] for n in range(N)]
+    return improve(ops, sorted(range(N), key=lambda n: (best[1][n], best[2][n])))
+
+
+def improve(ops, order):
+    if not NOM["tries"]:
+        return order
+    of, runs, last, open_ = [0] * len(ops), [], None, {}
+    for n, o in enumerate(ops):
+        name, into = o["tag"][2], None
+        if (o["q"] == "v" and name[0] == "M") or (o["q"] == "t" and name[:2] == "SM"):
+            key = (o["q"], o["tag"])
+            if key in open_ and len(runs[open_[key]]) < 4:
+                into = open_[key]
+            else:
+                open_[key] = len(runs)
+        elif o["q"] == "t":
+            if last is not None and ops[last]["tag"] == o["tag"] and not any(ops[m]["q"] in ("v", "s") and m > runs[of[last]][0] for m in o["deps"]):
+                into = of[last]
+            last = n
+        if into is None:
+            into = len(runs)
+            runs.append([])
+        of[n] = into
+        runs[into].append(n)
+    for r in runs:
+        if ops[r[0]]["tag"][2][:2] == "SM" and NOM["wt"]:
+            r.reverse()
+    R = len(runs)
+    queue = ["vstgy-".index(ops[r[0]]["q"] or "-") for r in runs]
+    models, keep = [], dict(NOM)
+    for change in VARIANTS:
+        NOM.update(change)
+        dur = [o["dur"] if o["tok"] else duration(*o["spec"]) for o in ops]
+        lat = [NOM["pel"] if o["q"] == "t" else o["lat"] * NOM["far"] for o in ops]
+        edges = []
+        for j, r in enumerate(runs):
+            e, off = {}, 0.0
+            for n in r:
+                for m in ops[n]["deps"] | ops[n]["after"]:
+                    if of[m] != j:
+                        gap = 0.0 if m not in ops[n]["deps"] else lat[m] + NOM["self" if ops[m]["q"] == ops[n]["q"] else "sem"]
+                        gap -= off + sum(dur[x] for x in runs[of[m]][runs[of[m]].index(m) + 1:])
+                        e[of[m]] = max(e.get(of[m], -1e18), gap)
+                off += dur[n]
+            edges.append(sorted(e.items()))
+        waits = [len(set(ops[m]["q"] for n in r for m in ops[n]["deps"] if of[m] != of[n])) * NOM["wt" if ops[r[0]]["q"] == "t" else "w"] for r in runs]
+        models.append(([sum(dur[n] for n in r) + w for r, w in zip(runs, waits)], edges, [lat[r[-1]] for r in runs]))
+        NOM.update(keep)
+    preds, succs = [[m for m, _ in e] for e in models[0][1]], [[] for _ in runs]
+    for j in range(R):
+        for m in preds[j]:
+            succs[m].append(j)
+    first, miss, seq = {}, [len(p) for p in preds], []
+    for j, n in enumerate(order):
+        first.setdefault(of[n], j)
+    ready = [j for j in range(R) if not miss[j]]
     while ready:
-        est = {n: max(at[n], free.get(ops[n]["q"], 0.0)) for n in ready}
-        first = min(ready, key=lambda n: est[n] + ops[n]["dur"])
-        q, end = ops[first]["q"], est[first] + ops[first]["dur"]
-        n = max([m for m in ready if ops[m]["q"] == q and est[m] <= end], key=lambda m: (rest[m] - NOM["lam"] * est[m], -m)) if q else first
-        ready.remove(n)
-        order.append(n)
-        done = est[n] + ops[n]["dur"]
-        if q:
-            free[q] = done
-        for s in succ[n]:
-            if n in ops[s]["deps"]:
-                at[s] = max(at[s], done + ops[n]["lat"] + NOM["sem"])
-            miss[s] -= 1
-            if miss[s] == 0:
-                ready.append(s)
-    return order
+        j = min(ready, key=lambda x: first[x])
+        ready.remove(j)
+        seq.append(j)
+        for x in succs[j]:
+            miss[x] -= 1
+            if not miss[x]:
+                ready.append(x)
+
+    def times(seq, mark, state):
+        total, new = 0.0, []
+        for (dur, edges, tail), (fin, marks) in zip(models, state):
+            fin, marks = fin[:], marks[:mark + 1]
+            free, end = marks[mark][0][:], marks[mark][1]
+            for z in range(32 * mark, R):
+                if z % 32 == 0 and z > 32 * mark:
+                    marks.append((free[:], end))
+                n = seq[z]
+                c = queue[n]
+                t = free[c]
+                for m, gap in edges[n]:
+                    x = fin[m] + gap
+                    if x > t:
+                        t = x
+                t += dur[n]
+                fin[n] = t
+                if c != 5:
+                    free[c] = t
+                t += tail[n]
+                if t > end:
+                    end = t
+            total += end
+            new.append((fin, marks))
+        return total / len(models), new
+
+    def blocked(seq, k, fin):
+        dur, edges, tail = models[k]
+        before, ahead, pairs = {}, {}, []
+        for n in seq:
+            ahead[n] = before.get(queue[n])
+            before[queue[n]] = n
+        n = max(range(R), key=lambda x: fin[x] + tail[x])
+        while n is not None:
+            why = [m for m, gap in edges[n] if fin[m] + gap >= fin[n] - dur[n] - 1e-6]
+            if why:
+                n = why[0]
+            else:
+                if ahead[n] is not None and ahead[n] not in preds[n]:
+                    pairs.append((ahead[n], n))
+                n = ahead[n]
+        return pairs
+
+    now, state = times(seq, 0, [([0.0] * R, [([0.0] * 6, 0.0)]) for _ in models])
+    best, place, x, pairs = (now, seq), [0] * R, NOM["seed"], None
+    for j, a in enumerate(seq):
+        place[a] = j
+    for it in range(NOM["tries"]):
+        x = (x * 6364136223846793005 + 1442695040888963407) % 2 ** 64
+        if pairs is None or it % 16 == 0:
+            k = (x >> 60) % len(models)
+            pairs = blocked(seq, k, state[k][0])
+        m, n = pairs[(x >> 33) % len(pairs)]
+        i, j = place[m], place[n]
+        if i > j:
+            continue
+        far, forward = (0, 0, 1, 2, 4, 8)[(x >> 20) % 6], (x >> 30) % 2
+        z = i if forward else j
+        while far and 0 < z < R - 1:
+            z += -1 if forward else 1
+            if queue[seq[z]] == queue[n]:
+                far -= 1
+                i, j = (z, j) if forward else (i, z)
+        part, move = seq[i:j + 1], {n if forward else m}
+        for a in (reversed(part) if forward else part):
+            if a in move:
+                move.update(b for b in (preds if forward else succs)[a] if i <= place[b] <= j)
+        if m in move and n in move:
+            continue
+        new = seq[:i] + [a for a in part if (a in move) == bool(forward)] + [a for a in part if (a in move) != bool(forward)] + seq[j + 1:]
+        v, after = times(new, i // 32, state)
+        heat = NOM["hot"] * (NOM["cold"] / NOM["hot"]) ** (it / NOM["tries"])
+        if v < now or (x >> 8) % 4096 < 4096 * math.exp((now - v) / heat):
+            now, seq, state = v, new, after
+            if it % 3 == 0:
+                pairs = None
+            for z in range(i, j + 1):
+                place[seq[z]] = z
+            if v < best[0]:
+                best = (v, new)
+    ORDER["nominal"] = best[0]
+    return [n for j in best[1] for n in runs[j]]
 
 
 def emit(g, T, ops):
     eng = {"v": g.vector, "s": g.scalar, "t": g.tensor, "g": g, "y": g.sync}
     qsem = {"v": "qv", "s": "qs", "t": "qt", "g": "qg"}
     order = plan(ops)
-    last, pos, cnt = {}, {}, {}
+    last, pos, cnt, close = {}, {}, {}, {}
     for n in order:
         o = ops[n]
+        close[o["group"]] = n
         if o["tok"] is None:
             last[o["q"]] = n
             cnt[o["q"]] = cnt.get(o["q"], 0) + 1
@@ -193,6 +411,7 @@ def emit(g, T, ops):
     known = {}
     for n in order:
         o = ops[n]
+        o["stop"][0] = close[o["group"]] == n
         kn = known.setdefault(o["q"], {})
         o["waits"] = []
         if o["q"] is not None:
@@ -239,7 +458,14 @@ def rank_program(g, core, T, topo):
     ops = []
     ndma = [0]
     sent = {}
-    now = [9]
+    now = [9, 0, "set"]
+    groups = {}
+    KB = [(0, PAR["kb"], PAR["kb"]), (PAR["kb"], L, LP)]
+    CH = KB if PAR["two"] else [(0, L, LP)]
+    cut = CH[-1][0]
+    KEEP = PAR["keep"]
+    turn = [0]
+    kss = sorted(set([0] + [k for row in PAR["ks"] for k in row if k < 16]))
     common = [x for x in topo.engines(cores[0], cores[1]) if all(x in topo.engines(a, b) for a in cores for b in cores if a != b)]
 
     def ap(a):
@@ -266,7 +492,7 @@ def rank_program(g, core, T, topo):
                     acc.append((a[1], a[2], a[3], a[4], wr))
         dur = (100.0 if q else 0.0) if tok else duration(kind, outs, ins)
         ops.append({"q": q, "fn": fn, "acc": acc, "tok": tok, "dur": dur, "lat": NOM["pel"] if q == "t" else lat, "more": more,
-                    "edge": False, "line": None, "spec": (kind, outs, ins), "tag": "%d%s%s" % (now[0], q or "-", acc[-1][0])})
+                    "edge": False, "line": None, "group": None, "stop": [False], "tag": tuple(now), "spec": (kind, outs, ins)})
         return len(ops) - 1
 
     def line(key):
@@ -291,7 +517,7 @@ def rank_program(g, core, T, topo):
         rec("v", "ts", lambda e: e.transpose(ap(out), ap(x)), [out], [x])
 
     def top(out, x):
-        rec("v", "act", lambda e: e.tensor_reduce(ap(out), ap(x), AxisListType.X, OP.max), [out], [x])
+        rec("v", "red", lambda e: e.tensor_reduce(ap(out), ap(x), AxisListType.X, OP.max), [out], [x])
 
     def ms(out, c):
         rec("v", "ts", lambda e: e.memset(ap(out), c), [out], [])
@@ -300,172 +526,203 @@ def rank_program(g, core, T, topo):
         if bias is not None:
             rec("s", "act", lambda e: e.activation(ap(out), ap(x), ACT.Identity, bias=ap(bias), scale=scale or 1.0), [out], [x, bias])
         elif scale is not None:
-            rec("s", "act", lambda e: e.activation(ap(out), ap(x), ACT.Identity, scale=ap(scale)), [out], [x, scale])
+            rec("s", "act", lambda e: e.activation(ap(out), ap(x), func or ACT.Identity, scale=ap(scale)), [out], [x, scale])
         else:
             rec("s", "act", lambda e: e.activation(ap(out), ap(x), func or ACT.Copy), [out], [x])
 
-    def mm(out, lhs, rhs, start, stop):
-        rec("t", "mm", lambda e: e.matmul(ap(out), ap(lhs), ap(rhs), start, stop), [out], [lhs, rhs])
-        ops[-1]["edge"] = start or stop
+    def mm(out, lhs, rhs, start=False):
+        stop = [False]
+        rec("t", "mm", lambda e: e.matmul(ap(out), ap(lhs), ap(rhs), start, stop[0]), [out], [lhs, rhs])
+        if start:
+            groups[out[1], out[2] // 512] = len(ops)
+        ops[-1].update({"edge": start, "group": groups[out[1], out[2] // 512], "stop": stop})
 
     def iota(out, pat, base, cm, flt=True):
         if flt:
             rec("g", "iota", lambda e: e.iota(ap(out), pat, base, cm, allow_small_or_imprecise_dtypes=True), [out], [])
         else:
             rec("g", "iota", lambda e: e.iota(ap(out), pat, base, cm), [out], [])
-        line("iota")
+        if out[1] in ("cI", "row", "R16", "R32", "VT"):
+            line("iota")
 
-    def dma(q, out, x, lat=2000.0, more=()):
+    def pick(out, x, pat, cmp, fill, base, cm):
+        rec("g", "pick", lambda e: e.affine_select(ap(out), ap(x), pat, cmp, fill, base, cm), [out], [x])
+
+    def dma(q, out, x, lat=2200.0):
         s = "d%d" % ndma[0]
         ndma[0] += 1
-        return rec(q, "dma", lambda e: e.dma_start(ap(out), ap(x)).then_inc(T.sem[s], 16), [out], [x], (s, 16), lat)
+        n = rec(q, "dma", lambda e: e.dma_start(ap(out), ap(x)).then_inc(T.sem[s], 16), [out], [x], (s, 16), lat - NOM["issue"])
+        ops[-1]["dur"] = NOM["issue"]
+        if now[0] == 9:
+            line("load" + q)
+        return n
 
     def col(j):
         return A("cF", j, j + 1)
 
-    def swap(out0, n, srcs):
+    def swap(bank, out0, n, srcs):
         for q in range(2):
             terms = [(g0, s) for s in srcs for g0 in range(2)]
             for j, (g0, s) in enumerate(terms):
-                mm(A("pw", out0 + q, out0 + 2 * n, 2), A("LL", 128 * (2 * q + g0), 128 * (2 * q + g0 + 1)), s(g0), j == 0, j == len(terms) - 1)
+                mm(A(bank, out0 + q, out0 + 2 * n, 2), A("LL", 128 * (2 * q + g0), 128 * (2 * q + g0 + 1)), s(g0), j == 0)
 
-    dma("y", A("odi"), T.od[:], 2000.0)
-    dma("s", A("nbi", 0, 1024), T.nb[:, 0:1024], 5500.0)
-    dma("y", A("nbi", 1024, 2048), T.nb[:, 1024:2048], 5500.0)
-    dma("s", A("XT", 0, W), T.xs[:], 7000.0)
-    dma("y", A("XT", W, B), T.xs[:, 0:B - W], 7000.0)
-    iota(A("pci"), [[0, 1]], 0, 1, False)
-    iota(A("row"), [[1, 144]], 0, 0)
+    def before(out, name, at, c):
+        b0, b1 = CH[c][0] // 32, CH[c][2] // 32
+        for d in range(1, b1):
+            lo = max(b0, d)
+            mm(A(out[1], out[2] + 2 * (lo - b0), out[3]), A("O32"), A(name, at + 2 * (lo - d), at + 2 * (b1 - d)))
+
+    dma("y", A("odi"), T.od[:], 2300.0)
+    dma("s", A("nbi"), T.nb[:], NOM["nb"])
+    dma("y", A("XT", 0, W), T.xs[:], NOM["xs"] - NOM["issue"])
+    cp(A("XT", W, B), A("XT", 0, B - W))
+    iota(A("cI"), [[0, 6]], 0, 1, False)
+    iota(A("row"), [[1, 160]], -16, 0)
     iota(A("R16"), [[16, 8], [0, 16]], 0, 0)
-    iota(A("kk"), [[0, 14], [1, 16]], 0, 0)
     iota(A("R32"), [[32, 4], [0, 32]], 0, 0)
-    iota(A("lanb"), [[32, 7], [0, 2]], 0, 0)
+    iota(A("VT", 0, B // 2), [[1, B // 2]], -2047, 0)
+    iota(A("RP"), [[1, 32], [0, 16]], 0, 0)
+    iota(A("kk"), [[0, 14], [1, 16]], 0, 0)
+    iota(A("lanb"), [[32, 7], [0, 2]], -352, 0)
     iota(A("par"), [[0, 7], [16, 2]], 15, 0)
-    iota(A("VT", 0, B), [[1, B]], -2047, 0)
+    act(A("VT", B // 2, B), A("VT", 0, B // 2), bias=float(B // 2))
     ms(A("thi"), 0)
-    dma("y", A("thi", p=(15, 128, 16)), T.th[:], 8000.0)
-    dma("y", A("wti"), T.wt[:], 8000.0)
-    for j, msk in enumerate((15, 112, 96, 16, 31, 127)):
-        ts(A("cI", j, j + 1), A("pci"), msk, OP.bitwise_and)
-    cp(A("cF", 0, 6), A("cI", 0, 6))
+    dma("y", A("thi", p=(15, 128, 16)), T.th[:], NOM["xs"])
+    dma("y", A("wti"), T.wt[:], NOM["xs"])
+    for j, msk in ((0, 15), (1, 112), (2, 31), (4, 96), (5, 16)):
+        ts(A("cI", j, j + 1), A("cI", j, j + 1), msk, OP.bitwise_and)
+    cp(A("cF", 0, 6), A("cI"))
     ms(A("one"), 1.0)
-    ms(A("DC", L, LP), 0.0)
-    ms(A("DC", LP + L, 2 * LP), 0.0)
-    ms(A("a1", L, LP), 1.0)
-    ms(A("a2", L, LP), 0.0)
-    ms(A("TT", W, B + 192), 0.0)
-    ms(A("cur"), float(L + B - 2047 - 4096))
-    ms(A("mk"), BIG)
-    ms(A("mex"), 0.0)
-    ms(A("kg", U, 64), 0.0)
-    ms(A("snd", 0, 3 * U), 0.0)
+    ms(A("DC"), 0.0)
+    ms(A("own"), 0.0)
+    ms(A("a1", L, LP), -1.0)
+    for piece, value in ((A("cur"), L + B - 2047 - 4096), (A("TT", W, B + 192), 0), (A("mex"), 0), (A("snd", 0, 3 * U), 0), (A("kg", U, 64), 0)):
+        iota(piece, [[0, width(piece)]], value, 0)
     ts(A("oda"), A("odi"), 2047, OP.add)
     cp(A("od16"), A("odi"))
     ts(A("odb"), A("oda"), 2047, OP.bitwise_and)
     cp(A("om16"), A("odb"))
-    ts(col(6), col(1), 15.0, OP.add)
-    ts(col(7), col(0), 0.0, OP.is_gt, float(3 * 2 ** 27), OP.mult)
-    ts(col(8), col(0), 2048.0, OP.mult)
-    ts(col(9), col(3), 0.0, OP.is_equal)
-    ts(col(10), col(3), 0.0, OP.is_gt)
-    ts(col(11), col(5), 16.0, OP.add)
-    ts(col(12), col(5), -16.0, OP.add)
-    ts(col(13), col(0), 15.0, OP.is_lt, BIG, OP.mult)
-    ts(col(14), col(7), float(2 ** 27), OP.add)
-    r128 = A("row", 0, 128)
-    ts(A("Ib"), r128, col(5), OP.is_equal)
-    ts(A("Z1"), A("row"), col(6), OP.is_equal)
+    ts(col(6), col(0), 1.0, OP.add, 2.0, OP.min)
+    ts(col(7), col(0), 15.0, OP.is_lt, BIG, OP.mult)
+    ts(col(10), col(5), 0.0, OP.is_equal)
+    ts(col(11), col(5), 0.0, OP.is_gt)
+    ts(A("IW"), A("row"), col(3), OP.is_equal)
+    ts(A("Ib"), A("row", 16, 144), col(3), OP.is_equal)
+    ts(A("Z1"), A("row", 1, 145), col(1), OP.is_equal)
     ts(A("B1"), A("R16"), col(1), OP.is_equal)
-    ts(A("O32"), A("R32"), col(2), OP.is_equal)
-    ts(A("LL", 0, 128), r128, col(5), OP.is_equal, col(9), OP.mult)
-    ts(A("LL", 128, 256), r128, col(11), OP.is_equal, col(9), OP.mult)
-    ts(A("LL", 256, 384), r128, col(12), OP.is_equal, col(10), OP.mult)
-    ts(A("LL", 384, 512), r128, col(5), OP.is_equal, col(10), OP.mult)
-    ts(A("Lt"), r128, col(5), OP.is_gt)
+    ts(A("O32"), A("R32"), col(4), OP.is_equal)
+    ts(A("RP"), A("RP"), col(2), OP.is_equal)
+    ts(A("DK"), A("Ib"), col(0), OP.mult, 2048.0, OP.mult)
+    ts(A("DP"), A("Ib"), col(6), OP.mult, float(2 ** 27), OP.mult)
+    ts(A("Lt"), A("row", 16, 144), col(3), OP.is_gt)
     tt(A("Lt"), A("Lt"), A("O32"), OP.mult)
-    for name, src, sc in (("ZG", "Z1", -32768.0), ("ZM", "Z1", 65536.0), ("ZA", "Z1", 32768.0), ("In", "Ib", -1.0), ("DK", "Ib", col(8)),
-                          ("DP", "Ib", col(14)), ("BO", "B1", -32768.0), ("I4", "Ib", -4096.0), ("I2", "Ib", -2048.0), ("O3f", "O32", 32768.0),
-                          ("If", "Ib", 1.0), ("Zn", "Z1", -1.0), ("Z2", "Z1", 2.0)):
-        act(A(name), A(src), scale=sc)
-    ts(A("Bn"), A("kk", 0, 128), float(KS), OP.is_ge, -1.0, OP.mult)
-    tt(A("Bn"), A("Bn"), A("B1"), OP.mult)
-    tt(A("LZ"), A("Lt"), A("I4"), OP.subtract)
-    tt(A("LW"), A("Lt"), A("I2"), OP.add)
     ts(A("rst"), A("kk"), 0.0, OP.is_equal, BIG, OP.mult)
-    ts(A("rs1"), A("kk", 0, U), 0.0, OP.is_gt)
-    ts(A("dg"), A("kk", 0, U), col(0), OP.is_equal)
-    ts(A("lanc"), A("lanb"), col(4), OP.add, -1792.0, OP.add)
-    ts(A("LE", 14, 28), A("lanb"), col(4), OP.add, float(B - 2047), OP.add)
-    ts(A("dum"), A("lanc"), float(L - 1792), OP.is_ge, BIG, OP.mult)
-    ts(A("mRG"), A("par"), col(4), OP.is_equal)
-    cp(col(15), A("wti"))
-    cp(col(16), A("thi"))
-    act(A("WB"), A("B1"), scale=col(15))
-    ts(A("ytl", 0, 3), A("one", 0, 3), col(16), OP.mult)
-    ts(A("TT", 0, 1024), A("nbi", 0, 1024), -2047.0, OP.add)
-    ts(A("TT", 1024, W), A("nbi", 1024, W), -2047.0, OP.add)
-    zz = A("pz", 0, 14)
-    ww = A("pw", 0, 14)
-    kT = A("po", 256, 256 + LP)
-    kmin = A("ks", 15, LP, 16)
+    for q in range(2):
+        for g0 in range(2):
+            at = 16 + 16 * (q - g0)
+            act(A("LL", 128 * (2 * q + g0), 128 * (2 * q + g0 + 1)), A("IW", at, at + 128), scale=col(10 + q))
+    for name, src, sc in (("ZG", "Z1", -32768.0), ("ZM", "Z1", 65536.0), ("O3f", "O32", 32768.0), ("In", "Ib", -1.0), ("If", "Ib", 1.0),
+                          ("Zn", "Z1", -1.0), ("Z2", "Z1", 2.0), ("Bn", "B1", -1.0)):
+        act(A(name), A(src), scale=sc)
+    act(A("BO", 0, 128), A("B1"), scale=-32768.0)
+    for j, k in enumerate(kss[1:]):
+        pick(A("BO", 128 * j + 128, 128 * j + 256), A("BO", 0, 128), [[0, 8], [1, 16]], OP.is_ge, 0.0, -k, 0)
+    for name, value in (("LZ", 4096.0), ("LW", -560.0)):
+        pick(A(name), A("Lt"), [[1, 128]], OP.not_equal, value, 0, -1)
+    rec("g", "iota", lambda e: e.iota(ap(A("Z0")), [[0, 128]], 0, 0, allow_small_or_imprecise_dtypes=True), [A("Z0")], [])
+    for name, value in (("IB", BIG), ("ID", 1024.0)):
+        pick(A(name), A("Z0"), [[1, 128]], OP.not_equal, value, 0, -1)
+    act(A("lanc"), A("lanb"), bias=col(2))
+    for l0, l1, lp in CH:
+        ts(A("LE", l0 // 16 + lp // 16, lp // 8), A("lanb", l0 // 16, lp // 16), col(2), OP.add, float(B - 2047 + 352), OP.add)
+    ts(A("mRG"), A("par"), col(2), OP.is_equal)
+    cp(col(8), A("wti"))
+    cp(col(9), A("thi"))
+    act(A("WZ"), A("Z1"), scale=col(8))
+    act(A("ytl", 0, 3), A("one", 0, 3), scale=col(9))
+    for j in range(4):
+        now[2] = "tt%d" % j
+        ts(A("TT", 512 * j, 512 * j + 512), A("nbi", 512 * j, 512 * j + 512), -2047.0, OP.add)
+    now[2] = "set"
+    act(A("thx", 0, 14), A("mRG"), scale=A("ytl", 0, 1))
+    mm(A("pg", 0, 14), A("O3f"), A("thx", 0, 14), True)
+    cp(A("thP"), A("pg", 0, 14))
+    tabled = (0, 14, 26, 40, 52, 66, 78)
+    act(A("VT", B, B + LP), IND(A("VT", 0, W), A("od16", 0, 14)))
+    for j0, j1 in ((14, 40), (40, 78)):
+        act(A("VT", B + 16 * j0, B + 16 * j1), IND(A("VT", 0, W), A("od16", j0, j1)))
 
-    def spread_threshold(t):
-        if t:
-            ts(A("thx"), A("mRG"), A("ytl", t, t + 1), OP.mult)
-        else:
-            act(A("thx"), A("mRG"), scale=A("ytl", t, t + 1))
-        mm(A("pw", 112, 126), A("O3f"), A("thx"), True, True)
-        tt(A("thD"), A("pw", 112, 126), A("dum"), OP.max)
-        cp(A("thP"), A("pw", 112, 126))
+    def own_of(t, l0, l1):
+        return A("own", 320 * (t % 2) + l0, 320 * (t % 2) + l1)
 
-    def write_columns(lst):
-        cp(IND(A("TT", 0, W), lst), A("DC", LP, LP + L))
+    def dif_at(c):
+        return 0 if c < len(CH) - 1 else LP + cut
 
     def guests_in(t):
         j = t - 3
+        now[0], now[2] = t, "gh"
         gin, xb = A("gin%d" % j), A("xb", U * (j % 2), U * (j % 2) + U)
         rec(None, "", None, [gin], [], ("ga%d" % j, len(common)), 0.0, [sent["g", j]])
-        mag = 1.5 * 2 ** 32
-        ts(A("gr"), gin, mag, OP.add, -mag, OP.add)
-        tt(xb, gin, A("gr"), OP.subtract)
-        mm(A("pg", 0, U), A("WB"), xb, True, True)
-        tt(A("hm"), A("pg", 0, U), A("dg"), OP.mult)
-        scan(A("hs"), A("rs1"), A("hm"), OP.mult, OP.add)
-        ts(A("hi", 0, 3), A("hs", 15, U, 16), float(77 * t), OP.add)
+        mag = 1.5 * 2 ** 23
+        ts(xb, gin, mag, OP.add, -mag, OP.add)
+        for p in range(16):
+            mm(A("pg", 0, 3), A("WZ", 15 - p, 143 - p), A("xb", xb[2] + p, xb[3], 16), p == 0)
+        ts(A("hi", 0, 3), A("pg", 0, 3), float(77 * t), OP.add)
         ts(A("ha", 0, 3), A("hi", 0, 3), 2047, OP.bitwise_and)
         cp(A("h16", 0, 3), A("ha", 0, 3))
         ts(A("g16"), IND(A("TO%d" % j) if t in KEEP else A("TT", 0, W), A("h16", 0, 3)), 2047.0, OP.add)
-        act(A("cap", U * (j % 2), U * (j % 2) + U), A("gr"), bias=col(13), scale=2.0 ** -9)
-        h = GV[j]
-        act(A("Gg", 16 * h, 16 * U), IND(A("XT", 0, W), A("g16", h, U)))
-        if h:
-            cp(A("Gg", 0, 16 * h), IND(A("XT", 0, W), A("g16", 0, h)))
+        tt(A("gr"), gin, xb, OP.subtract)
+        act(A("cap", U * (j % 2), U * (j % 2) + U), A("gr"), bias=col(7), scale=8192.0)
 
-    def sizes(src, first, n, mine, banks, out, at=0):
-        for bank, c0, k0, k1 in banks:
-            for k in range(k0, k1):
-                piece = A(bank, c0 + n * (k - k0), c0 + n * (k - k0 + 1))
-                mm(piece, A("Ib"), A(src, 16 * first + k, 16 * (first + n), 16), True, False)
-                mm(piece, A("In"), mine, False, True)
-            act(A(out, at + n * k0, at + n * k1), A(bank, c0, c0 + n * (k1 - k0)), ACT.Abs)
+    def against(out, got, mine, a, b, how, shift=0):
+        need, have = -(-(b - a) // 32), PAR["ring"][now[0]]
+        if turn[0] % have + need > have:
+            turn[0] = 0
+        bank, at = "pr", 512 * (turn[0] % have)
+        if mine == "xT" and PAR["gb"] is not None:
+            gb = PAR["gb"][now[0] - 3]
+            at = 512 * gb + 16 * (a if gb < 3 and not PAR["two"] else 0)
+            if a and PAR["g2"]:
+                bank, at = "pg", 256
+        else:
+            turn[0] += need
+        for x in range(a, b, 32):
+            n, p0 = min(32, b - x), (x + shift) % 128
+            cell = A(bank, at + 16 * (x - a), at + 16 * (x - a + n))
+            mm(cell, A(mine, x + shift - p0, x + shift - p0 + 128, p=(p0, p0 + n, 1)), A("RP", 0, 16 * n, p=(p0, p0 + n, 1)), True)
+            if how == "s":
+                mm(cell, A("In"), A(got[1], got[2] + 16 * (x - a), got[2] + 16 * (x - a + n)))
+        if how == "v":
+            tt(out, got, A(bank, at, at + 16 * (b - a)), OP.max)
+        else:
+            act(out, A(bank, at, at + 16 * (b - a)), ACT.Abs, None, 0.5)
 
     def guests_judged(t):
         j = t - 3
         xb, key = A("xb", U * (j % 2), U * (j % 2) + U), A("pg", 64, 64 + U)
-        if GK[j]:
-            sizes("Gg", 0, U, xb, [("pc", 0, 0, KS)], "Ag")
-            mm(key, A("Bn"), xb, True, False)
-            for k in range(KS, 16):
-                mm(key, A("Zn", 15 - k, 143 - k), A("Gg", k, 16 * U, 16), False, False)
-            for k in range(KS, 16):
-                tt(A("Ag", U * k, U * k + U), A("Gg", k, 16 * U, 16), xb, OP.max)
-                mm(key, A("Z2", 15 - k, 143 - k), A("Ag", U * k, U * k + U), False, False)
-            for k in range(KS):
-                mm(key, A("Z1", 15 - k, 143 - k), A("Ag", U * k, U * k + U), False, k == KS - 1)
-        else:
-            sizes("Gg", 0, U, xb, [("pc", 0, 0, 10), ("pg", 128, 10, 16)], "Ag")
+        now[0], now[2] = t, "gM"
+        mm(A("pg", 128, 256, p=(0, U, 1)), xb, A("Ib"), True)
+        (cp if PAR["xq"] == "v" else act)(A("xT", p=(0, U, 1)), A("pg", 128, 256, p=(0, U, 1)))
+        first, h = True, PAR["gv"][j]
+        now[2] = "gG"
+        if h:
+            cp(A("Gg", 0, 16 * h), IND(A("XT", 0, W), A("g16", 0, h)))
+        act(A("Gg", 16 * h, 16 * U), IND(A("XT", 0, W), A("g16", h, U)))
+        for a, b, who, how in PAR["guests"][j]:
+            now[2] = "gM"
+            against(A("Ag", 16 * a, 16 * b), A("Gg", 16 * a, 16 * b), "xT", a, b, how)
+        now[2] = "gs"
+        runs = [(a, b) for a, b, who, how in PAR["guests"][j] if how == "v"]
+        if runs:
+            a, b = runs[0][0], runs[-1][1]
+            mm(key, A("Z0"), xb, True)
+            first = False
+            mm(A("pg", 64 + a, 64 + b), A("Bn"), A("xb", xb[2] + a, xb[2] + b))
             for k in range(16):
-                mm(key, A("Z1", 15 - k, 143 - k), A("Ag", U * k, U * k + U), k == 0, k == 15)
+                mm(A("pg", 64 + a, 64 + b), A("Zn", 15 - k, 143 - k), A("Gg", 16 * a + k, 16 * b, 16))
+        now[2] = "gj"
+        for k in range(16):
+            mm(key, A("Z2", 15 - k, 143 - k), A("Ag", k, 16 * U, 16), first and k == 0)
         tt(A("kg", 0, U), A("pg", 64, 64 + U), A("cap", U * (j % 2), U * (j % 2) + U), OP.min)
         tr(A("kgT"), A("kg"))
         scan(A("js"), A("rst", 0, 64), A("kgT"), OP.add, OP.min)
@@ -487,160 +744,332 @@ def rank_program(g, core, T, topo):
         j = t - 3
         n = sum(best_masks(c, cores, topo)[core][1] for c in cores if c != core)
         old = A("ytl", t - 1, t)
+        now[0], now[2] = t, "thr"
         act(A("th4", j, j + 1), old, bias=0.375, scale=0.25)
         rec(None, "", None, [A("bt", 16 * j + 4 * r, 16 * j + 4 * r + 1) for r in range(NR) if r != rank], [], ("ba%d" % j, n), 0.0, [sent["b", j]])
         top(A("bc", j, j + 1), A("bt", 16 * j, 16 * j + 16, 4))
         ts(A("bi"), A("bc", j, j + 1), 0.25, OP.mult, A("th4", j, j + 1), OP.subtract)
         ts(A("ytl", t, t + 1), A("bi"), 0.0, OP.max, old, OP.add)
+        if t == 3:
+            ts(A("thx", 14, 28), A("mRG"), A("ytl", t, t + 1), OP.mult)
 
-    def floor_m(scale):
-        ts(A("mi"), A("mn"), 2.0 ** -15, OP.mult, -0.46875, OP.add)
-        ts(A("mex", 15, LP, 16), A("mi"), 4095.0, OP.min, scale, OP.mult)
-        tr(A("mC"), A("mex"))
+    def floor_m(scale, l0, lp):
+        ts(A("mi", l0 // 16, lp // 16), A("mn", l0 // 16, lp // 16), 2.0 ** -15, OP.mult, -0.46875, OP.add)
+        ts(A("mex", l0 + 15, lp, 16), A("mi", l0 // 16, lp // 16), 4095.0, OP.min, scale, OP.mult)
+        tr(A("mC", l0, lp), A("mex", l0, lp))
 
-    spread_threshold(0)
-    for t in range(NT):
-        now[0] = t
+    def pack(t, l0, l1, lp):
+        floor_m(2.0 ** -13, l0, lp)
+        s0 = U * (4 - t)
+        tt(IND(A("snd", s0, s0 + 432), A("s16", l0 // 16, l1 // 16)), A("mC", l0, l1), A("ownf", l0, l1), OP.add)
+
+    def front(t, c):
+        now[:2] = [t, c]
+        l0, l1, lp = CH[c]
+        n, w0, w1, wp = l1 - l0, l0 // 16, l1 // 16, lp // 16
         hi = B + L * (t + 1)
-        came = 3 <= t
-        leave = 2 <= t <= 4
-        e16 = A("L16", 14, 27)
-        cc = A("DC", LP, LP + L)
+        po = "po%d" % c
+        c16, cc, fl = A("c16", l0, l1), A("DC", cut + l0, cut + l1) if t < 5 else A("cf", l0, l1), A("fl", l0, l1)
+        dif = A("DC", dif_at(c), dif_at(c) + n)
+        own = own_of(t, l0, l1)
+        e16 = A("L16", w0 + wp, wp + w1)
+        parts = [(l0, PAR["c0"]), (PAR["c0"], l1)] if l0 < PAR["c0"] < l1 else [(l0, l1)]
+        for j, (a, b) in enumerate(parts):
+            now[2] = "c%d" % j
+            if t == 0:
+                ts(A("c16", a, b), IND(A("nbi"), A("om16", a // 16, b // 16)), 1.0, OP.add)
+            else:
+                ts(A("c16", a, b), IND(A("TT", 0, hi), A("L16", w0 + a // 16, w0 + b // 16)), 2047.0, OP.add)
+        now[2] = "own"
+        act(own, IND(A("XT", 0, hi), e16) if t else IND(A("XT", 0, W), A("od16", w0, w1)))
+        now[2] = "oT"
+        kinds = [x[3] for x in PAR["pieces"][t] if l0 <= x[0] < l1]
+        if "k" in kinds:
+            mm(A(po, 0, n) if PAR["two"] else A("pr", l0, l1), A("Ib"), own, True)
+        if set(kinds) != {"k"}:
+            wide, high = -(-n // 128) * 128, (0, min(n, 128), 1)
+            for j in range(0, wide, 128):
+                mm(A(po, j, j + 128, p=high), own_of(t, l0 + j, l0 + j + high[1]), A("Ib"), True)
+            (cp if PAR["oq"][t] == "v" else act)(A("oT", 256 * c, 256 * c + wide, p=high), A(po, 0, wide, p=high))
+        now[2] = "cc"
         if t == 0:
-            own, vrep, ownat = A("XT", B, B + L), A("VT", B, B + L), ("XT", B)
-            ts(A("c16"), IND(A("nbi"), A("om16", 0, 13)), 1.0, OP.add)
-            act(A("XT", B, B + LP), IND(A("XT", 0, W), A("od16", 0, 14)))
-            act(A("VT", B, B + LP), IND(A("VT", 0, W), A("od16", 0, 14)))
-            raw = A("cr")
-            ts(raw, A("c16"), -2047.0, OP.add)
+            vrep, raw = A("VT", B + l0, B + l1), A("cr", l0, l1)
+            ts(raw, c16, -2047.0, OP.add)
         else:
-            own, vrep, ownat = A("own"), IND(A("VT", 0, hi), e16), ("own", 0)
-            raw = IND(A("TT", 0, hi), A("L16", 0, 13))
-            act(own, IND(A("XT", 0, hi), e16))
-            ts(A("c16"), raw, 2047.0, OP.add)
-        if VG[t]:
-            cp(A("G", 0, 16 * VG[t]), IND(A("XT", 0, B), A("c16", 0, VG[t])))
-        for l0, l1, how in CH[t]:
-            l0 = max(l0, VG[t])
-            act(A("G", 16 * l0, 16 * l1), IND(A("XT", 0, B), A("c16", l0, l1)))
-            line("s")
-        mm(A("po", 0, L), A("Ib"), own, True, True)
-        ts(A("fl"), A("c16"), 2048.0, OP.is_ge, -2048.0, OP.mult)
-        tt(cc, raw, A("fl"), OP.add)
-        tt(A("DC", 0, L), vrep, cc, OP.subtract)
-        ts(A("a1", 0, L), A("DC", 0, L), -16.0, OP.is_gt)
-        ts(A("a2", 0, L), A("DC", 0, L), 16.0, OP.is_ge, -1.0, OP.mult)
-        if t == 0:
-            tr(A("DT", LP, 2 * LP), A("DC", LP, 2 * LP))
-            v16 = A("od16", 0, 13)
-        else:
-            tr(A("DT"), A("DC"))
-            swap(64, 7, [lambda g0: A("DT", 16 * g0, LP, 32), lambda g0: A("DT", LP + 16 * g0, 2 * LP, 32)])
-            ts(A("v16"), A("pw", 64, 78), 2047.0, OP.add)
-            v16 = A("v16", 0, 13)
-        if leave:
-            act(A("ownf"), own)
-        if t >= 4:
-            guests_judged(t - 1)
-            threshold(t - 1)
-        if t == 4:
-            spread_threshold(3)
-        if came and t not in KEEP:
-            guests_in(t)
-        write_columns(v16)
-        if t + 1 in KEEP:
-            sent["copy", t - 2] = dma("y", A("TO%d" % (t - 2)), A("TT", 0, W), 5000.0)
-        if t in KEEP:
-            guests_in(t)
-        mm(A("pk", 0, LP), A("DK"), A("one"), True, False)
-        mm(A("pk", 0, LP), A("DP"), A("a1"), False, False)
-        mm(A("pk", 0, LP), A("DP"), A("a2"), False, False)
-        for n, (l0, l1, how) in enumerate(CH[t]):
-            mine = A(ownat[0], ownat[1] + l0, ownat[1] + l1)
-            end = n == len(CH[t]) - 1
-            if how == "s":
-                sizes("G", l0, l1 - l0, mine, [("pa", 0, 0, 8), ("pb", 0, 8, 16)], "AA", 16 * l0)
-                for k in range(16):
-                    at = 16 * l0 + (l1 - l0) * k
-                    mm(A("pk", l0, l1), A("ZA", 15 - k, 143 - k), A("AA", at, at + l1 - l0), False, end and k == 15)
-                continue
-            mm(A("pk", l0, l1), A("BO"), mine, False, False)
-            for k in range(16):
-                mm(A("pk", l0, l1), A("ZG", 15 - k, 143 - k), A("G", 16 * l0 + k, 16 * l1, 16), False, False)
-            for k in range(16):
-                tt(A("M", L * k + l0, L * k + l1), A("G", 16 * l0 + k, 16 * l1, 16), A("po", l0, l1), OP.max)
-                line("v")
-                mm(A("pk", l0, l1), A("ZM", 15 - k, 143 - k), A("M", L * k + l0, L * k + l1), False, end and k == 15)
-        tr(kT, A("pk", 0, LP))
-        scan(A("ks"), A("rst"), kT, OP.add, OP.min)
-        tt(A("mn"), kmin, A("mk"), OP.min)
+            vrep, raw = IND(A("VT", 0, hi), e16), IND(A("TT", 0, hi), A("L16", 2 * w0, w0 + w1))
+        ts(fl, c16, 2048.0, OP.is_ge, -2048.0, OP.mult)
+        tt(cc, raw, fl, OP.add)
+        now[2] = "dif"
+        tt(dif, vrep, cc, OP.subtract)
+        near = 1.5 * 2 ** 28 + 32
+        now[2] = "a1"
+        ts(A("a1", l0, l1), dif, near, OP.add, near, OP.is_equal)
+        now[2] = "DT"
         if t == 5:
-            guests_judged(t)
-            dma("y", T.yg[:], A("jC", 0, U, p=(15, 128, 16)))
-            floor_m(1.0)
-            dma("s", T.ym[:], A("mC", 0, L, p=(15, 128, 16)))
-            for h in range(2):
-                act(A("yno", 384 * h, 384 * h + 384), IND(A("TT", 0, W), A("od16", 24 * h, 24 * h + 24)), bias=2047.0)
-                dma("y", T.yn[:, 384 * h:384 * h + 384], A("yno", 384 * h, 384 * h + 384), 2800.0)
-            act(A("vf"), vrep, bias=2047.0)
-            dma("y", T.yv[:], A("vf", p=(0, 128, 16)))
-            threshold(5)
-            dma("y", T.yt[:], A("ytl", 0, NT, p=(15, 128, 16)))
-            break
-        act(A("TT", B + 192, hi + L), IND(A("TT", 0, W), A("om16", 12, 13 * (t + 2))), bias=1.0)
-        if t in OD:
-            j0, j1 = OD[t]
+            now[2] = "wr"
+            ts(IND(A("yno"), e16), cc, 1.0, OP.mult, 2047.0, OP.add)
+        elif t == 0:
+            tr(A("DT", cut + l0, cut + lp), A("DC", cut + l0, cut + lp))
+        else:
+            tr(A("DT", 2 * l0, 2 * lp), A("DC", 2 * l0, 2 * lp))
+            now[2] = "v16"
+            if c == len(CH) - 1:
+                for q in range(2):
+                    for g0 in range(2):
+                        turned = A("LL", 128 * (2 * q + g0), 128 * (2 * q + g0 + 1))
+                        mm(A(po, 256 + q, 270, 2), turned, A("DT", cut + 16 * g0, cut + LP, 32), g0 == 0)
+                        for d, (x0, x1, xp) in enumerate(CH):
+                            mm(A(po, 256 + x0 // 16 + q, 256 + xp // 16, 2), turned, A("DT", dif_at(d) + 16 * g0, dif_at(d) + xp - x0, 32))
+                ts(A("v16"), A(po, 256, 270), 2047.0, OP.add)
+        for kb, (b0, b1, bp) in enumerate(KB):
+            if l0 <= b0 < l1:
+                keys(t, kb)
+
+    def keys(t, kb):
+        b0, b1, bp = KB[kb]
+        pk = "pk%d" % kb
+        now[2] = "ini"
+        mm(A(pk, 0, bp - b0), A("DK"), A("one", 0, bp - b0), True)
+        now[2] = "pen"
+        mm(A(pk, 0, bp - b0), A("DP"), A("a1", b0, bp))
+        pieces = [x for x in PAR["pieces"][t] if b0 <= x[0] < b1]
+        for a, b, who, how in pieces:
+            got, out = A("G", 16 * a, 16 * b), A("M", 16 * a, 16 * b)
+            j = [x[0] for x in PAR["pieces"][t]].index(a)
+            now[2] = "G%d" % j
+            (cp if who == "v" else act)(got, IND(A("XT", 0, B), A("c16", a, b)))
+            now[2] = "M%d" % j
+            if how != "k":
+                against(out, got, "oT", a, b, how, 256 - cut if PAR["two"] and kb else 0)
+        cuts = [x for x in PAR["sums"][t] if b0 <= x <= b1]
+        for a, b in zip(cuts, cuts[1:]):
+            j = PAR["sums"][t].index(a)
+            if [x[3] for x in pieces if x[0] == a] == ["k"]:
+                ks, n, key = PAR["ks"][t][j], b - a, A(pk, a - b0, b - b0)
+                turns = -(-ks // (512 // n))
+                now[2] = "D%d" % j
+                for r in range(turns):
+                    k0, k1, at = ks * r // turns, ks * (r + 1) // turns, 512 * (turn[0] % (3 if t < 3 else 2) if PAR["two"] else 1 + turn[0] % (2 if t < 3 or PAR["gb"][t - 3] == 3 else 1))
+                    turn[0] += 1
+                    for k in range(k0, k1):
+                        cell = A("pr", at + n * (k - k0), at + n * (k - k0 + 1))
+                        mm(cell, A("In"), own_of(t, a, b), True)
+                        mm(cell, A("Ib"), A("G", 16 * a + k, 16 * b, 16))
+                    act(A("M", 16 * a + n * k0, 16 * a + n * k1), A("pr", at, at + n * (k1 - k0)), ACT.Abs, None, 0.5)
+                now[2] = "SG%d" % j
+                if ks < 16:
+                    mm(key, A("BO", 128 * kss.index(ks), 128 * kss.index(ks) + 128), own_of(t, a, b))
+                for k in range(ks, 16):
+                    mm(key, A("ZG", 15 - k, 143 - k), A("G", 16 * a + k, 16 * b, 16))
+                for k in list(range(ks, 16)) + list(range(ks)):
+                    piece = A("M", 16 * a + n * k, 16 * a + n * (k + 1))
+                    if k >= ks:
+                        now[2] = "M%d" % j
+                        tt(piece, A("G", 16 * a + k, 16 * b, 16), A("po%d" % kb, a - b0, b - b0) if PAR["two"] else A("pr", a, b), OP.max)
+                    now[2] = "S%s%d" % ("M" if k >= ks else "A", j)
+                    mm(key, A("ZM", 15 - k, 143 - k), piece)
+                continue
+            runs = []
+            for x in pieces:
+                if a <= x[0] < b and x[3] == "v":
+                    if runs and runs[-1][1] == x[0]:
+                        runs[-1][1] = x[1]
+                    else:
+                        runs.append([x[0], x[1]])
+            now[2] = "SG%d" % PAR["sums"][t].index(a)
+            for r0, r1 in runs:
+                mm(A(pk, r0 - b0, r1 - b0), A("BO", 0, 128), own_of(t, r0, r1))
+                for k in range(16):
+                    mm(A(pk, r0 - b0, r1 - b0), A("ZG", 15 - k, 143 - k), A("G", 16 * r0 + k, 16 * r1, 16))
+            now[2] = "SM%d" % PAR["sums"][t].index(a)
+            for k in range(16):
+                mm(A(pk, a - b0, b - b0), A("ZM", 15 - k, 143 - k), A("M", 16 * a + k, 16 * b, 16))
+
+    def least(t, kb):
+        l0, l1, lp = KB[kb]
+        pk, n, k0 = "pk%d" % kb, lp - l0, LP * (t % 2)
+        kT, ks = A(pk, 256, 256 + n), A("ks", k0 + l0, k0 + lp)
+        now[2] = "k%d" % kb
+        tr(kT, A(pk, 0, n))
+        scan(ks, A("rst", 0, n), kT, OP.add, OP.min)
+        now[2] = "n%d" % kb
+        if t < 5:
+            tt(kT, ks, kT, OP.subtract)
+            tt(A("yy", l0, lp), A("DT", cut + l0, cut + lp), kT, OP.subtract)
+            scan(A("nr", l0, lp), kT, A("yy", l0, lp), OP.max, OP.min)
+
+    def middle(t):
+        now[0], now[2] = t, "ownf"
+        hi = B + L * (t + 1)
+        if 2 <= t <= 4:
+            act(A("ownf"), own_of(t, 0, L))
+        now[2] = "wr"
+        if t < 5:
+            cp(IND(A("TT", 0, W), A("v16" if t else "od16", 0, 13)), A("DC", cut, cut + L))
+        if t == 4:
+            now[2] = "out"
+            act(A("yno", B, B + KN), IND(A("TT", 0, W), A("od16", 0, KN // 16)), bias=2047.0)
+        if t + 1 in KEEP:
+            sent["copy", t - 2] = dma("y", A("TO%d" % (t - 2)), A("TT", 0, W), NOM["copy"])
+        if t < 5:
+            now[2] = "seed"
+            act(A("TT", B + 192, hi + L), IND(A("TT", 0, W), A("om16", 12, 13 * (t + 2))), bias=1.0)
+            now[2] = "tab"
+            j0, j1 = tabled[t + 1] if t else 0, tabled[t + 2]
             act(A("XT", B + 16 * j0, B + 16 * j1), IND(A("XT", 0, W), A("od16", j0, j1)))
-            act(A("VT", B + 16 * j0, B + 16 * j1), IND(A("VT", 0, W), A("od16", j0, j1)))
-        low = A("mn") if t == 4 else kmin
-        tt(A("dead"), low, A("thP"), OP.is_lt)
-        fr = A("dead")
+
+    def back(t, c):
+        now[:2] = [t, c]
+        l0, l1, lp = CH[c]
+        n, w0, wp = lp - l0, l0 // 16, lp // 16
+        nw = wp - w0
+        po = "po%d" % c
+        leave = 2 <= t <= 4
+        kmin = A("ks", LP * (t % 2) + l0 + 15, LP * (t % 2) + lp, 16)
+
+        def flags(s):
+            return A("fr", 14 * (s % 3) + w0, 14 * (s % 3) + wp)
+        zb = "pk%d" % c
+        mn, mk, thD, thG = A("mn", w0, wp), A(po if t >= 4 else zb, 464, 464 + nw), A(po, 304, 304 + nw), A(po, 320, 320 + nw)
+        thx = A("thx", 14 * (t == 4) + w0, 14 * (t == 4) + wp)
+
+        whole = t != 4 and c == len(CH) - 1
+        if whole:
+            mn, mk = A("mn"), A(mk[1], 464, 478)
+
+        def so_far():
+            now[2] = "mk"
+            mm(mk, A("If"), mn if t > 1 else A("ks", 15, LP, 16), True)
+            mm(mk, A("IB"), A("fr", 14 * ((t - 1) % 3), 14 * ((t - 1) % 3) + 14) if whole else flags(t - 1))
+        if t == 4 or (t == 5 and whole):
+            so_far()
+        now[2] = "th"
         if leave:
-            tt(A("FF"), A("F0"), A("F1"), OP.max)
-            tt(A("thG"), A("FF"), A("thD"), OP.max)
-            tt(A("go"), low, A("thG"), OP.is_ge)
-            mm(ww, A("LW"), A("go"), True, False)
-            for d in range(1, 7):
-                mm(A("pw", 2 * d, 14), A("O32"), A("go", 0, 14 - 2 * d), False, d == 6)
-            ts(A("thrD"), A("dead"), 4096.0, OP.mult, -2000.0, OP.add)
-            fr = A("free")
-            tt(fr, ww, A("thrD"), OP.is_lt)
-            tt(A("slt"), ww, A("lanc"), OP.min)
-        mm(zz, A("If"), A("cur"), True, False)
-        mm(zz, A("LZ"), fr, False, False)
-        for d in range(1, 7):
-            mm(A("pz", 2 * d, 14), A("O32"), A(fr[1], 0, 14 - 2 * d), False, d == 6)
-        tt(kT, A("ks"), kT, OP.subtract)
-        tt(A("yy"), A("DT", LP, 2 * LP), kT, OP.subtract)
-        scan(A("nr"), kT, A("yy"), OP.max, OP.min)
-        tt(A("LE", 14, 28), zz, A("LE", 14, 28), OP.max)
-        tt(A("LE", 0, 14), zz, A("nr", 15, LP, 16), OP.max)
+            now[2] = "old"
+            mm(thG, A("IB"), flags(t - 1), True)
+            mm(thG, A("IB"), flags(t - 2))
+            now[2] = "th"
+            mm(thG, A("O3f"), thx)
+        if t == 4:
+            mm(thD, A("O3f"), thx, True)
+        for kb in range(2):
+            if l0 <= KB[kb][0] < l1:
+                least(t, kb)
+        if 0 < t < 4 and whole:
+            so_far()
+        now[2] = "fate"
+        kall = A("ks", LP * (t % 2) + 15, LP * (t % 2) + LP, 16)
+        if t == 4 or (t == 5 and whole):
+            tt(mn, kall if whole else kmin, mk, OP.min)
+        if t == 5:
+            return
+        fr, ww, zz = flags(t), A(po, 336, 336 + nw), A(zb, 480, 480 + nw)
+        low = mn if t == 4 else kmin
         if leave:
-            swap(96, 7, [lambda g0: A("slt", g0, 14, 2)])
-        swap(16, 14, [lambda g0: A("LE", g0, 28, 2)])
-        ts(A("L16"), A("pw", 16, 44), 2047.0, OP.add)
+            tt(A("go", w0, wp), low, thG, OP.is_ge)
+        tt(A("dead", w0, wp) if leave else fr, low, thD if t == 4 else A("thP", w0, wp), OP.is_lt)
+        if leave:
+            mm(ww, A("LW"), A("go", w0, wp), True)
+            mm(ww, A("ID"), A("dead", w0, wp))
+            before(ww, "go", 0, c)
+            stay = 1.5 * 2 ** 33
+            ts(fr, ww, stay, OP.add, stay, OP.not_equal)
+            now[2] = "slt"
+            tt(A("slt", w0, wp), ww, A("lanc", w0, wp), OP.min)
+        now[2] = "cu"
+        mm(zz, A("If"), A("cur", w0, wp), True)
+        now[2] = "LE"
+        mm(zz, A("LZ"), fr)
+        before(zz, "fr", 14 * (t % 3), c)
+        tt(A("LE", w0 + wp, 2 * wp), zz, A("LE", w0 + wp, 2 * wp), OP.max)
+        now[2] = "LN"
+        tt(A("LE", 2 * w0, w0 + wp), zz, A("nr", l0 + 15, lp, 16), OP.max)
+
+        def slots():
+            now[2] = "s16"
+            swap(po, 384, nw // 2, [lambda g0: A("slt", w0 + g0, wp, 2)])
+            ts(A("s16", w0, wp), A(po, 384, 384 + nw), 560.0, OP.add)
+        if t in PAR["gofirst"]:
+            slots()
+        if t in PAR["efirst"]:
+            now[2] = "E16"
+            swap(po, 352 + nw, nw // 2, [lambda g0: A("LE", w0 + wp + g0, 2 * wp, 2)])
+            ts(A("L16", w0 + wp, 2 * wp), A(po, 352 + nw, 352 + 2 * nw), 2047.0, OP.add)
+            now[2] = "L16"
+            swap("pk1", 448, nw // 2, [lambda g0: A("LE", 2 * w0 + g0, w0 + wp, 2)])
+            ts(A("L16", 2 * w0, w0 + wp), A("pk1", 448, 448 + nw), 2047.0, OP.add)
+        else:
+            now[2] = "L16"
+            swap(po, 352, nw, [lambda g0: A("LE", 2 * w0 + g0, 2 * wp, 2)])
+            ts(A("L16", 2 * w0, 2 * wp), A(po, 352, 352 + 2 * nw), 2047.0, OP.add)
+        if leave and t not in PAR["gofirst"]:
+            slots()
+        now[2] = "mn"
+        if 0 < t < 4 and whole:
+            tt(mn, kall, mk, OP.min)
+        now[2] = "pack"
+        if t in PAR["split"]:
+            pack(t, l0, l1, lp)
+
+    def after(t):
+        now[0], now[2] = t, "cur"
+        f0 = 14 * (t % 3)
         if t < 4:
-            mm(A("pz", 16, 30), A("If"), A("cur"), True, False)
+            mm(A("pk1", 496, 510), A("If"), A("cur"), True)
             for d in range(1, 7):
-                mm(A("pz", 16, 30 - 2 * d), A("O32"), A(fr[1], 2 * d, 14), False, False)
-                mm(A("pz", 16 + 2 * d, 30), A("O32"), A(fr[1], 0, 14 - 2 * d), False, False)
-            mm(A("pz", 16, 30), A("O32"), fr, False, True)
-            act(A("cur"), A("pz", 16, 30))
-        Fp = A("F%d" % (t % 2))
-        act(Fp, fr, scale=BIG)
-        if leave:
+                mm(A("pk1", 496, 510 - 2 * d), A("O32"), A("fr", f0 + 2 * d, f0 + 14))
+                mm(A("pk1", 496 + 2 * d, 510), A("O32"), A("fr", f0, f0 + 14 - 2 * d))
+            mm(A("pk1", 496, 510), A("O32"), A("fr", f0, f0 + 14))
+            act(A("cur"), A("pk1", 496, 510), bias=float(L - LP))
+        now[2] = "pack"
+        if t >= 2:
             j = t - 2
-            ts(A("s16"), A("pw", 96, 110), 2048.0, OP.add)
-            floor_m(512.0)
+            if t not in PAR["split"]:
+                pack(t, 0, L, LP)
             s0 = U * (2 - j)
-            tt(IND(A("snd", s0, s0 + 464), A("s16", 0, 13)), A("mC", 0, L), A("ownf"), OP.add)
             dst = cores[(rank + 1 + t % (NR - 1)) % NR]
 
-            def send(e, dst=dst, s0=s0, j=j):
+            def send(e):
                 rid, pid = topo.addr(dst, core)
                 return e.remote_dma(ap(A("gin%d" % j)), ap(A("snd", s0, s0 + U)), T.sem["ga%d" % j], T.sem["left%d" % j], pid, rid,
                                     sum(1 << x for x in common))
             sent["g", j] = rec("g", "", send, [], [A("snd", s0, s0 + U)], ("left%d" % j, len(common)), NOM["rem"] + (NOM["first"] if j == 0 else 0.0),
-                                [sent["copy", j]] if ("copy", j) in sent else [])
-        tt(A("mk"), A("mn"), Fp, OP.max)
+                               [sent["copy", j]] if ("copy", j) in sent and PAR["clear"] else [])
+
+    def guests(t, where):
+        if t >= 3 and PAR["gpos"][t - 3] == where:
+            guests_judged(t)
+            if t == 5:
+                dma("y", T.yg[:], A("jC", 0, U, p=(15, 128, 16)))
+            threshold(t)
+
+    for c in range(len(CH)):
+        front(0, c)
+    middle(0)
+    for t in range(NT - 1):
+        if PAR["two"]:
+            back(t, 0)
+            guests(t, 1)
+            front(t + 1, 0)
+            guests(t, 2)
+        back(t, len(CH) - 1)
+        after(t)
+        if not PAR["two"]:
+            guests(t, 1)
+        front(t + 1, len(CH) - 1)
+        guests(t, 3)
+        if t + 1 >= 3:
+            guests_in(t + 1)
+        middle(t + 1)
+        guests(t + 1, 0)
+    dma("y", T.yt[:], A("ytl", 0, NT, p=(15, 128, 16)))
+    now[2] = "out"
+    dma("y", T.yn[:], A("yno", B, B + KN), 3500.0)
+    for c, (l0, l1, lp) in enumerate(CH):
+        now[2] = "out"
+        act(A("vf", l0, l1), IND(A("VT", 0, B + Q), A("L16", (l0 + lp) // 16, (lp + l1) // 16)), bias=2047.0)
+        back(5, c)
+    dma("y", T.yv[:], A("vf", p=(0, 128, 16)))
+    floor_m(1.0, 0, LP)
+    dma("s", T.ym[:], A("mC", 0, L, p=(15, 128, 16)))
     emit(g, T, ops)

@@ -7,52 +7,40 @@ B = 2064
 LP = 224
 H = "float16"
 BIG = float(2 ** 30)
-
-
-def cells(text):
-    ends = [int(x[:-2]) for x in text.split()]
-    return [(a, b, x[-2], x[-1]) for a, b, x in zip([0] + ends, ends, text.split())]
-
-
+G8 = (0, 8, 1)
 PAR = {
-    "two": True,
-    "kb": 128,
-    "pieces": [cells(x) for x in ["64vk 128sk 208sk"] + ["64sk 128sk 208sk"] * 5],
-    "sums": [[0, 64, 128, 208]] * 6,
-    "oq": "vvvsss",
-    "c0": 0,
-    "guests": [[(0, 32, "s", "s"), (32, 48, "s", "s")]] * 2 + [[(0, 32, "v", "v"), (32, 48, "s", "s")]],
-    "ring": [4, 4, 4, 2, 2, 2], "gb": [2, 2, 2], "gv": [0, 0, 24], "g2": True,
-    "gpos": [0, 0, 0], "xq": "s", "gofirst": [2, 3, 4], "clear": True, "efirst": [],
-    "ks": [[0, 8, 6], [4, 4, 6], [8, 8, 6], [8, 8, 6], [8, 8, 6], [8, 8, 6]],
+    "cut": 128,
+    "pieces": [[(64, 32, 8), (128, 0, 8), (208, 0, 6)]] * 3 + [[(64, 0, 8), (128, 0, 8), (208, 0, 6)]] * 3,
+    "guests": "vsv", "gv": [24, 0, 24],
     "keep": [3, 4],
-    "split": [],
+    "split": [2, 4],
+    "ring": [2, 2, 2, 1, 1, 1],
+    "win": [2, 3, 4],
+    "whole": [0, 1, 2, 3, 4, 5],
+    "wide": True, "wr2": [], "vb": "pr0",
 }
-PAR.update({"two": False, "c0": 64, "g2": False, "gb": [3, 3, 2], "gv": [24, 0, 24], "clear": False,
-            "pieces": [cells(x) for x in ["64vk 128sk 208sk"] + ["32vk 64sk 128sk 208sk"] * 2 + ["64sk 128sk 208sk"] * 3],
-            "ks": [[0, 8, 8], [0, 8, 6], [0, 8, 6], [8, 8, 6], [8, 8, 6], [0, 4, 6]],
-            "guests": [[(0, 32, "v", x), (32, 48, "s", "s")] for x in "vsv"]})
-NOM = {"cyc": 0.83, "gat": 1.56, "sca": 3.8, "vfix": 20.0, "sfix": 50.0, "pe": 0.42, "sem": 80.0, "pel": 60.0, "rem": 3300.0, "w": 0.0, "wt": 0.0, "issue": 1000.0, "seed": 5,
-       "first": 2500.0, "passes": 3, "far": 1.0, "tries": 170000, "hot": 600.0, "cold": 8.0, "early": 0.0, "self": 30.0, "lead": 4.0 * PAR["two"], "nb": 5500.0, "xs": 7200.0, "copy": 6000.0}
-DUE = {"c0": 0, "own": 0.1, "G0": 0.2, "c1": 0.3, "oT": 0.4, "G1": 0.5, "G2": 1, "G3": 1.5, "D0": 1.1, "D1": 1.5, "D2": 2.2,
-       "M0": 1.2, "M1": 1.6, "M2": 2.3, "cc": 1.3, "dif": 1.4, "a1": 3, "DT": 3.1, "v16": 3.2, "wr": 3.3, "ini": 3,
-       "SG0": 3.5, "SM0": 3.6, "SA0": 3.65, "SG1": 3.7, "SM1": 3.8, "SA1": 3.85, "SG2": 3.9, "SM2": 4, "SA2": 4.05,
-       "k0": 4.5, "n0": 4.6, "k1": 5, "fate": 5.1, "n1": 5.2, "LE": 5.3, "LN": 5.35, "L16": 5.4, "slt": 5.5, "mn": 5.55, "s16": 5.6, "pack": 5.7,
-       "seed": 6, "tab": 7, "out": 8, "cur": 12, "tt0": -90, "tt1": -90, "tt2": -87, "tt3": -87,
-       "2wr": -2, "2v16": -2, "2mn": 5.1, "2s16": 5.15, "2pack": 5.2, "3gh": -5, "3gG": -5, "3gM": -5, "3gj": -5, "3thr": -5,
-       "4DT": 8, "4n0": 8, "4n1": 8.1, "4LE": 8.2, "4LN": 8.3, "4L16": 8.4, "4wr": 9, "4v16": 9, "4seed": 9.5,
-       "4gh": 11, "4gG": 11.1, "4gM": 11.2, "4gj": 11.3, "4thr": 19, "5gh": -1, "5gG": -1, "5gM": -1, "5gj": -1, "5thr": -1}
-DUE = {'c0': -19.67, 'own': -4.77, 'G0': 4.33, 'c1': 15.8, 'oT': 7.26, 'G1': -5.14, 'G2': 22.26, 'G3': -5.52, 'D0': 1.97, 'D1': 0.24, 'D2': 1.57, 'M0': -14.71, 'M1': -2.4, 'M2': 20.56, 'cc': 5.29, 'dif': 27.91, 'a1': 12.61, 'DT': -12.14, 'v16': 17.2, 'wr': 6.19, 'ini': 9.62, 'SG0': 14.13, 'SM0': 20.11, 'SA0': 2.53, 'SG1': -3.69, 'SM1': -8.32, 'SA1': 13.36, 'SG2': 13.53, 'SM2': -10.25, 'SA2': -16.19, 'k0': 3.89, 'n0': 5.74, 'k1': -1.64, 'fate': 9.7, 'n1': 0.33, 'LE': 14.68, 'LN': 0.72, 'L16': 6.18, 'slt': 14.62, 'mn': 30.29, 's16': 15.6, 'pack': 5.81, 'seed': 7.37, 'tab': 12.11, 'out': 10.0, 'cur': 8.62, 'tt0': -90, 'tt1': -90, 'tt2': -87, 'tt3': -87, '2wr': 0.25, '2v16': -2.0, '4DT': 0.63, '4n1': 9.35, '4LN': 6.17, '4gh': 9.25, '4gG': 11.1, '4gj': 19.18, '4thr': 24.75, '5gh': -0.88, '5gj': -3.5, '2dif': -3.48, '2SA2': 10.92, '5c0': -0.75, 'gj': -5.38, '1k1': 10, '2SM1': 5.8, 'gh': -6.63, '3k1': 4.87, '0SA2': 10.79, 'gM': 15.99, '3M0': 1.32, 'mk': 12.64, '4SM1': 3.17, '5SA2': 7.05, '1c0': -1.63, '3DT': -7.15, '3own': -8.91, 'gG': 0.36, '4SA2': 5.42, '1SA2': 6.05, 'th': 1.75, '4M0': 2.58, '5SG2': 1.66, '1wr': 2.17, '4c0': -2.25, '1dif': -10.34, '2M1': -1.53, '2c0': -3.24, '1SM1': -1.95, 'ownf': 3.24, '5SG1': 0.57, '3c0': -8.87, '1G3': -2.0, '4k1': 17.37, '3SA1': 3.35, 'thr': 4.88, '5M0': 1.83, '2M0': -2.43, '4th': 11.5, '2DT': -1.16, '5SM1': 6.55, '2SG2': -1.21, '3SM2': 11.38, '5SM2': 3.63, '3SA2': 4.3, '2SM2': 3.26, '5k1': 6.37, '4SM2': 6.75, '3D1': 3.38, '3SM1': 0.18, '1n1': 7.21, '1SM2': 11.75, '3ownf': 3.37, '1DT': -3.53, '1M0': -0.55, '2G3': 10.75, '2k1': 12.13, '0cur': 6.25, '0k1': 15.37, '1SG0': -5.12, '1ini': 1.62, '2G1': 6.24, '4D1': 3.64, '3n1': 11.09, '4M1': 4.97, '0SM2': 0.75, '3LN': 3.72, '3SA0': 12.02, '1LN': 3.22, '2n1': 11.34, '4pack': 2.32, '5G0': 0.2, '5G1': -0.51}
-NOM.update({"passes": 2, "tries": 48000, "sem": 130.0, "self": 110.0, "hot": 250.0, "seed": 43})
-BIAS = DUE
-VARIANTS = [{"sem": 130.0, "self": 110.0, "sfix": 50.0, "gat": 1.3, "sca": 3.0},
+NOM = {"cyc": 0.83, "gat": 1.56, "sca": 3.8, "vfix": 20.0, "sfix": 50.0, "pe": 0.42, "sem": 130.0, "pel": 60.0, "self": 110.0, "rem": 3300.0,
+       "first": 2500.0, "issue": 1000.0, "far": 1.0, "nb": 5500.0, "xs": 7200.0, "copy": 6000.0,
+       "seed": 3, "passes": 2, "tries": 1200000, "hot": 300.0, "cold": 30.0, "span": 80, "hop": 32, "sweeps": 40, "soft": 0.08, "alone": 0.75, "lead": 4.0, "run": 3, "back": 6000.0}
+DUE = {"set": -100, "tt0": -90, "tt1": -90, "tt2": -87, "tt3": -87, "c": 0, "own": .3, "G0": .6, "G1": .6, "G2": .6, "oT": 1, "cc": 1,
+       "dif": 1.4, "a1": 1.6, "DT": 1.8, "v16": 2, "wr": 2.3, "mk": 2.9, "old": 2.9, "th": 2.95, "ini": 3, "pen": 3.5, "seed": 4,
+       "SG0": 3.9, "SG1": 3.9, "SG2": 3.9, "M0": 4, "M1": 4, "M2": 4, "D0": 4.2, "D1": 4.6, "D2": 4.2, "SM0": 5, "SM1": 5, "SM2": 5,
+       "SA0": 5, "SA1": 5.2, "SA2": 5, "ownf": 5, "y0": 5, "w0": 5.5, "cu": 5.5, "z0": 5.6, "k": 6, "fate": 6.3, "n": 6.5, "slt": 6.6,
+       "mn": 7, "s16": 7, "LN": 7.4, "LE": 7.5, "pack": 7.5, "L16": 8, "out": 8, "tab": 9, "cur": 9, "win": 9}
+for part in ("gh", "gG", "gR", "g0", "gM", "gs", "gj", "thr"):
+    DUE.update({"3" + part: -5, "4" + part: 11, "5" + part: -1})
+VARIANTS = [{"vfix": 23.0, "sfix": 65.0, "cyc": 0.95, "pe": 0.48, "far": 1.07}, {"gat": 1.3, "sca": 3.0},
             {"vfix": 26.0, "sfix": 80.0, "sem": 140.0, "self": 120.0, "pel": 70.0, "cyc": 1.08, "pe": 0.55, "gat": 1.8, "sca": 4.8, "far": 1.15}]
+STAGES = [((0.2, 1, 1), [(0.5, {("v", 2, 0, "c")}), (0.5, {("v", 2, 1, "c")})]),
+          ((0.25, 1, 1), [(0.7, {("g", 2, 1, "pack")}), (0.15, {("v", 3, 0, "c")}), (0.15, {("v", 3, 1, "c")})]),
+          ((0.35, 1, 1), [(0.8, {("g", 4, 1, "pack")}), (0.1, {("g", 3, 1, "pack")}), (0.1, {("v", 5, 0, "c")})]),
+          ((0.2, 1, 1), [(1.0, None)])]
 ORDER = {}
 F, BF, I, U16 = "float32", "bfloat16", "int32", "uint16"
 
 
-def _sb(n, d):
-    return ("sbuf", [128, n], d)
+def _sb(n, d, k=None):
+    return ("sbuf", [128, n] if k is None else [128, n, k], d)
 
 
 def _ps():
@@ -63,29 +51,27 @@ SCRATCH = {
     "nbi": _sb(W, I), "TT": _sb(B + Q, F), "XT": _sb(B + Q, BF), "VT": _sb(B + Q, F),
     "TO0": _sb(W, F), "TO1": _sb(W, F), "odi": _sb(78, I), "oda": _sb(78, I), "odb": _sb(78, I), "od16": _sb(78, U16), "om16": _sb(78, U16),
     "G": _sb(16 * L, BF), "M": _sb(16 * L, BF), "Gg": _sb(16 * U, BF), "Ag": _sb(16 * U, BF),
-    "own": _sb(2 * 320, BF), "oT": _sb(512, BF), "xT": _sb(128, BF), "Z0": _sb(128, BF), "RP": _sb(512, BF), "ownf": _sb(L, F), "c16": _sb(L, U16), "cr": _sb(L, H), "fl": _sb(L, H),
-    "DC": _sb(2 * LP, H), "DT": _sb(2 * LP, H), "a1": _sb(LP, BF),
-    "ks": _sb(2 * LP, F), "yy": _sb(LP, F), "nr": _sb(LP, F), "mex": _sb(LP, F), "mC": _sb(LP, F),
+    "own": _sb(2 * L, BF), "xT": _sb(128, BF), "Z0": _sb(128, BF), "RP": _sb(512, BF), "ownf": _sb(2 * L, F), "c16": _sb(L, U16),
+    "cr": _sb(L, H), "fl": _sb(L, H), "DC": _sb(2 * LP, H), "DT": _sb(2 * LP, H), "a1": _sb(LP, BF),
+    "ks": _sb(2 * LP, F), "ne": _sb(LP, BF), "nr": _sb(2 * LP, H), "mex": _sb(LP, F), "mC": _sb(LP, F),
+    "base": _sb(14, H), "w16": _sb(2, U16), "ow16": _sb(16, U16), "omf": _sb(96, F),
     "dead": _sb(14, BF), "go": _sb(14, BF), "fr": _sb(42, BF),
-    "LE": _sb(28, H), "L16": _sb(28, U16), "slt": _sb(14, H), "s16": _sb(14, U16), "v16": _sb(14, U16),
-    "mn": _sb(14, F), "mi": _sb(14, I), "thP": _sb(14, F), "thx": _sb(28, F), "cur": _sb(14, F),
-    "row": _sb(160, BF), "IW": _sb(160, BF), "cI": _sb(6, I), "cF": _sb(12, F), "R16": _sb(128, BF), "R32": _sb(128, BF), "kk": _sb(LP, BF),
+    "L16": _sb(2, U16, 14), "slt": _sb(14, H), "s16": _sb(14, U16), "v16": _sb(14, U16),
+    "mn": _sb(14, F), "mi": _sb(14, I), "thP": _sb(14, F), "thx": _sb(28, F), "cur": _sb(14, H), "cz": _sb(16, H),
+    "row": _sb(160, BF), "IW": _sb(160, BF), "cI": _sb(8, I), "cF": _sb(12, F), "R16": _sb(128, BF), "R32": _sb(128, BF),
     "lanb": _sb(14, F), "par": _sb(14, F), "lanc": _sb(14, F), "mRG": _sb(14, F),
-    "Zn": _sb(144, BF), "Z2": _sb(144, BF), "Z1": _sb(144, BF), "ZM": _sb(144, BF), "ZG": _sb(144, BF), "WZ": _sb(144, BF),
+    "Sx": _sb(136, BF), "Sy": _sb(136, BF), "Sm": _sb(8, BF), "Sf": _sb(8, F), "S2": _sb(8, BF), "Iq": _sb(U, F), "r17": _sb(136, F),
+    "td": _sb(27, F), "tq": _sb(2, F), "Z1": _sb(144, BF), "ZM": _sb(144, BF), "ZG": _sb(144, BF), "WZ": _sb(144, BF),
     "Bn": _sb(128, BF), "Ib": _sb(128, BF), "In": _sb(128, BF), "If": _sb(128, F), "B1": _sb(128, BF), "BO": _sb(128 * 8, BF),
     "DP": _sb(128, BF), "DK": _sb(128, BF), "O32": _sb(128, BF), "O3f": _sb(128, F), "Lt": _sb(128, BF), "LZ": _sb(128, BF), "LW": _sb(128, BF),
     "ID": _sb(128, BF), "IB": _sb(128, BF), "LL": _sb(512, BF),
-    "one": _sb(LP, BF), "rst": _sb(LP, F),
-    "wti": _sb(1, I), "thi": _sb(1, I), "ytl": _sb(8, F), "th4": _sb(4, F),
+    "one": _sb(LP, BF), "rst": _sb(128, F),
+    "wti": _sb(1, I), "thi": _sb(1, I), "ytl": _sb(72, F),
     "snd": _sb(528, F), "gin0": _sb(U, F), "gin1": _sb(U, F), "gin2": _sb(U, F),
-    "gr": _sb(U, F), "xb": _sb(2 * U, BF), "cap": _sb(2 * U, F), "hi": _sb(4, I), "ha": _sb(4, I),
-    "h16": _sb(4, U16), "g16": _sb(U, U16), "kg": _sb(64, F), "kgT": _sb(64, F), "js": _sb(64, F), "jC": _sb(64, F),
-    "bt": _sb(48, F), "bc": _sb(4, F), "bi": _sb(1, I), "vf": _sb(L, F), "yno": _sb(B + Q, F), "cf": _sb(L, F),
-    "pk0": _ps(), "pk1": _ps(), "po0": _ps(), "pg": _ps(),
-    "pr": ("psum", [128, 1536 if PAR["two"] else 2048], F),
+    "xb": _sb(2 * U, BF), "hi": _sb(4, I), "ha": _sb(4, I), "h16": _sb(4, U16), "g16": _sb(U, U16), "js": _sb(136, F), "jC": _sb(U, F),
+    "bt": _sb(108, F), "vf": _sb(L, F), "yno": _sb(B + Q, F), "cf": _sb(L, F),
+    "pk0": _ps(), "pk1": _ps(), "po0": _ps(), "po1": _ps(), "pr0": _ps(), "pr1": _ps(), "pq": _ps(), "pg": _ps(),
 }
-if PAR["two"]:
-    SCRATCH["po1"] = _ps()
 NDMA = 19
 SEMAPHORES = (["qv", "qs", "qt", "qg", "ga0", "ga1", "ga2", "ba0", "ba1", "ba2"] + ["left%d" % j for j in range(6)]
               + ["d%d" % j for j in range(NDMA)])
@@ -97,6 +83,10 @@ def A(name, c0=0, c1=None, st=1, p=None):
     return ("a", name, c0, SCRATCH[name][1][1] if c1 is None else c1, st, p)
 
 
+def A3(name, a0, a1, k0, k1=None):
+    return ("b", name, a0, a1, k0, k1)
+
+
 def IND(win, off):
     return ("i", win, off)
 
@@ -104,13 +94,21 @@ def IND(win, off):
 def width(a):
     if a[0] == "i":
         return 16 * width(a[2])
+    if a[0] == "b":
+        return (1 if a[3] is None else a[3] - a[2]) * (1 if a[5] is None else a[5] - a[4])
     return (a[3] - a[2] + a[4] - 1) // a[4]
+
+
+def extent(a):
+    if a[0] == "b":
+        return (a[1], a[2], a[2] + 1 if a[3] is None else a[3], 1, a[4], a[4] + 1 if a[5] is None else a[5])
+    return (a[1], a[2], a[3], a[4], 0, 1)
 
 
 def duration(kind, outs, ins):
     full = [a for a in outs + ins if isinstance(a, tuple)]
     if kind == "mm":
-        return max(64, width(ins[1])) * NOM["pe"] * (4 if SCRATCH[ins[1][1]][2] == F else 1)
+        return max(min(64, width(ins[0])), width(ins[1])) * NOM["pe"] * (4 if SCRATCH[ins[1][1]][2] == F else 1)
     if kind in ("iota", "pick"):
         return (130 if kind == "iota" else 170) + 2 * NOM["cyc"] * width(outs[0])
     ind = [a for a in full if a[0] == "i"]
@@ -143,20 +141,19 @@ def plan(ops):
     seen, lines = {}, {}
     for n, o in enumerate(ops):
         deps, after = set(o["more"]), set()
-        for (name, c0, c1, st, wr) in o["acc"]:
+        for (name, c0, c1, st, k0, k1, wr) in o["acc"]:
             ps = SCRATCH[name][0] == "psum"
-            for (m, d0, d1, ds, dw) in seen.get(name, []):
+            for (m, d0, d1, ds, j0, j1, dw) in seen.get(name, []):
                 if m == n:
                     continue
                 same = ops[m]["q"] == o["q"] and ops[m]["tok"] is None and o["tok"] is None
-                over = d0 < c1 and c0 < d1 and not (st == ds and (c0 - d0) % st)
-                bank = ps and d0 // 512 <= (c1 - 1) // 512 and c0 // 512 <= (d1 - 1) // 512
+                over = d0 < c1 and c0 < d1 and j0 < k1 and k0 < j1 and not (st == ds and (c0 - d0) % st)
                 if same and o["q"] == "t":
-                    if bank and (o["edge"] or ops[m]["edge"]):
+                    if ps and (o["edge"] or ops[m]["edge"]):
                         after.add(m)
-                elif (bank and not same) or (over and (dw or wr)):
+                elif (ps and not same) or (over and (dw or wr)):
                     deps.add(m)
-            seen.setdefault(name, []).append((n, c0, c1, st, wr))
+            seen.setdefault(name, []).append((n, c0, c1, st, k0, k1, wr))
         if o["line"] is not None:
             if o["line"] in lines:
                 after.add(lines[o["line"]])
@@ -230,7 +227,7 @@ def schedule(ops):
         return start, seq
 
     zero, tail = [0.0] * N, [o["lat"] for o in ops]
-    loads = [1e6 * max(0, 4 - n) for n in range(N)]
+    loads = [1e6 * max(0, 5 - n) for n in range(N)]
     prio = [0.0] * N
     for n in range(N - 1, -1, -1):
         t, c, name = ops[n]["tag"]
@@ -247,15 +244,13 @@ def schedule(ops):
     return improve(ops, sorted(range(N), key=lambda n: (best[1][n], best[2][n])))
 
 
-def improve(ops, order):
-    if not NOM["tries"]:
-        return order
+def gather_runs(ops, order):
     of, runs, last, open_ = [0] * len(ops), [], None, {}
     for n, o in enumerate(ops):
         name, into = o["tag"][2], None
         if (o["q"] == "v" and name[0] == "M") or (o["q"] == "t" and name[:2] == "SM"):
             key = (o["q"], o["tag"])
-            if key in open_ and len(runs[open_[key]]) < 4:
+            if key in open_ and len(runs[open_[key]]) < NOM["run"]:
                 into = open_[key]
             else:
                 open_[key] = len(runs)
@@ -268,9 +263,6 @@ def improve(ops, order):
             runs.append([])
         of[n] = into
         runs[into].append(n)
-    for r in runs:
-        if ops[r[0]]["tag"][2][:2] == "SM" and NOM["wt"]:
-            r.reverse()
     R = len(runs)
     queue = ["vstgy-".index(ops[r[0]]["q"] or "-") for r in runs]
     models, keep = [], dict(NOM)
@@ -289,8 +281,7 @@ def improve(ops, order):
                         e[of[m]] = max(e.get(of[m], -1e18), gap)
                 off += dur[n]
             edges.append(sorted(e.items()))
-        waits = [len(set(ops[m]["q"] for n in r for m in ops[n]["deps"] if of[m] != of[n])) * NOM["wt" if ops[r[0]]["q"] == "t" else "w"] for r in runs]
-        models.append(([sum(dur[n] for n in r) + w for r, w in zip(runs, waits)], edges, [lat[r[-1]] for r in runs]))
+        models.append(([sum(dur[n] for n in r) for r in runs], edges, [lat[r[-1]] for r in runs]))
         NOM.update(keep)
     preds, succs = [[m for m, _ in e] for e in models[0][1]], [[] for _ in runs]
     for j in range(R):
@@ -308,41 +299,46 @@ def improve(ops, order):
             miss[x] -= 1
             if not miss[x]:
                 ready.append(x)
+    return runs, queue, models, preds, succs, seq
 
-    def times(seq, mark, state):
+
+def improve(ops, order):
+    if not NOM["tries"]:
+        return order
+    runs, queue, models, preds, succs, seq = gather_runs(ops, order)
+    R = len(runs)
+
+    def times(seq, mark, state, goals, stop):
         total, new = 0.0, []
         for (dur, edges, tail), (fin, marks) in zip(models, state):
             fin, marks = fin[:], marks[:mark + 1]
-            free, end = marks[mark][0][:], marks[mark][1]
-            for z in range(32 * mark, R):
-                if z % 32 == 0 and z > 32 * mark:
-                    marks.append((free[:], end))
-                n = seq[z]
-                c = queue[n]
-                t = free[c]
-                for m, gap in edges[n]:
-                    x = fin[m] + gap
-                    if x > t:
-                        t = x
-                t += dur[n]
-                fin[n] = t
-                if c != 5:
-                    free[c] = t
-                t += tail[n]
-                if t > end:
-                    end = t
-            total += end
+            free = marks[mark][:]
+            for z0 in range(16 * mark, stop, 16):
+                if z0 > 16 * mark:
+                    marks.append(free[:])
+                for n in seq[z0:z0 + 16]:
+                    c = queue[n]
+                    t = free[c]
+                    for m, gap in edges[n]:
+                        x = fin[m] + gap
+                        if x > t:
+                            t = x
+                    t += dur[n]
+                    fin[n] = t
+                    if c != 5:
+                        free[c] = t
+            for w, group in goals:
+                total += w * max([fin[n] + tail[n] for n in group])
             new.append((fin, marks))
         return total / len(models), new
 
-    def blocked(seq, k, fin):
+    def blocked(seq, k, fin, n, since, stop):
         dur, edges, tail = models[k]
-        before, ahead, pairs = {}, {}, []
-        for n in seq:
-            ahead[n] = before.get(queue[n])
-            before[queue[n]] = n
-        n = max(range(R), key=lambda x: fin[x] + tail[x])
-        while n is not None:
+        before, ahead, pairs = [None] * 6, {}, []
+        for x in seq[:stop]:
+            ahead[x] = before[queue[x]]
+            before[queue[x]] = x
+        while n is not None and (fin[n] > since[k] or not pairs):
             why = [m for m, gap in edges[n] if fin[m] + gap >= fin[n] - dur[n] - 1e-6]
             if why:
                 n = why[0]
@@ -352,44 +348,218 @@ def improve(ops, order):
                 n = ahead[n]
         return pairs
 
-    now, state = times(seq, 0, [([0.0] * R, [([0.0] * 6, 0.0)]) for _ in models])
-    best, place, x, pairs = (now, seq), [0] * R, NOM["seed"], None
-    for j, a in enumerate(seq):
-        place[a] = j
-    for it in range(NOM["tries"]):
-        x = (x * 6364136223846793005 + 1442695040888963407) % 2 ** 64
-        if pairs is None or it % 16 == 0:
-            k = (x >> 60) % len(models)
-            pairs = blocked(seq, k, state[k][0])
-        m, n = pairs[(x >> 33) % len(pairs)]
-        i, j = place[m], place[n]
-        if i > j:
-            continue
-        far, forward = (0, 0, 1, 2, 4, 8)[(x >> 20) % 6], (x >> 30) % 2
-        z = i if forward else j
-        while far and 0 < z < R - 1:
-            z += -1 if forward else 1
-            if queue[seq[z]] == queue[n]:
-                far -= 1
-                i, j = (z, j) if forward else (i, z)
-        part, move = seq[i:j + 1], {n if forward else m}
-        for a in (reversed(part) if forward else part):
-            if a in move:
-                move.update(b for b in (preds if forward else succs)[a] if i <= place[b] <= j)
-        if m in move and n in move:
-            continue
-        new = seq[:i] + [a for a in part if (a in move) == bool(forward)] + [a for a in part if (a in move) != bool(forward)] + seq[j + 1:]
-        v, after = times(new, i // 32, state)
-        heat = NOM["hot"] * (NOM["cold"] / NOM["hot"]) ** (it / NOM["tries"])
-        if v < now or (x >> 8) % 4096 < 4096 * math.exp((now - v) / heat):
-            now, seq, state = v, new, after
-            if it % 3 == 0:
-                pairs = None
-            for z in range(i, j + 1):
-                place[seq[z]] = z
-            if v < best[0]:
-                best = (v, new)
-    ORDER["nominal"] = best[0]
+    x, since = NOM["seed"], [0.0] * len(models)
+    place = [0] * R
+    for share, named in STAGES:
+        goals = []
+        for w, names in named:
+            goals.append((w, [j for j, r in enumerate(runs) if (ops[r[0]]["q"],) + ops[r[0]]["tag"] in names] if names else
+                          [j for j in range(R) if not succs[j]]))
+        since = [s * share[1] for s in since]
+        for j, a in enumerate(seq):
+            place[a] = j
+        ends = [n for _, group in goals for n in group]
+        stop = max(place[n] for n in ends) + 1
+        now, state = times(seq, 0, [([0.0] * R, [[0.0] * 6]) for _ in models], goals, R)
+        best, pairs, tries = (now, seq, state), None, int(NOM["tries"] * share[0])
+        for it in range(tries):
+            x = (x * 6364136223846793005 + 1442695040888963407) % 2 ** 64
+            if not pairs or it % 16 == 0:
+                k = (x >> 60) % len(models)
+                group = goals[(x >> 50) % len(goals)][1]
+                fin, tail = state[k][0], models[k][2]
+                pairs = blocked(seq, k, fin, max(group, key=lambda n: fin[n] + tail[n]), since, stop)
+                if not pairs:
+                    continue
+            m, n = pairs[(x >> 33) % len(pairs)]
+            i, j = place[m], place[n]
+            if i > j:
+                continue
+            far, forward = (0, 0, 1, 2, 4, 8)[(x >> 20) % 6], (x >> 30) % 2
+            z = i if forward else j
+            while far and 0 < z < R - 1:
+                z += -1 if forward else 1
+                if queue[seq[z]] == queue[n]:
+                    far -= 1
+                    i, j = (z, j) if forward else (i, z)
+            part, move = seq[i:j + 1], {n if forward else m}
+            for a in (reversed(part) if forward else part):
+                if a in move:
+                    move.update([b for b in (preds if forward else succs)[a] if i <= place[b] <= j])
+            if m in move and n in move:
+                continue
+            new = seq[:i] + [a for a in part if (a in move) == bool(forward)] + [a for a in part if (a in move) != bool(forward)] + seq[j + 1:]
+            v, after = times(new, i // 16, state, goals, max(stop, j + 1))
+            heat = NOM["hot"] * share[2] * (NOM["cold"] / NOM["hot"]) ** (it / tries)
+            if v < now or (x >> 8) % 4096 < 4096 * math.exp((now - v) / heat):
+                now, seq, state = v, new, after
+                if it % 3 == 0:
+                    pairs = None
+                for z in range(i, j + 1):
+                    place[seq[z]] = z
+                if j + 1 >= stop:
+                    stop = max(place[n] for n in ends) + 1
+                if v < best[0]:
+                    best = (v, new, after)
+        seq = best[1]
+        since = [max(fin[n] for n in goals[0][1]) - NOM["back"] for fin, _ in best[2]]
+        ORDER.setdefault("stages", []).append(best[0])
+    return [n for j in seq for n in runs[j]]
+
+
+def improve(ops, order):
+    if not NOM["tries"]:
+        return order
+    runs, queue, every, preds, succs, seq = gather_runs(ops, order)
+    R, span, hop, sweeps, soft = len(runs), NOM["span"], NOM["hop"], NOM["sweeps"], NOM["soft"]
+    onward = []
+    for dur, edges, tail in every:
+        e = [[] for _ in range(R)]
+        for n in range(R):
+            for m, gap in edges[n]:
+                e[m].append((n, gap))
+        onward.append(e)
+    starts = list(range(0, max(1, R - span + hop), hop))
+    tries = NOM["tries"] // (sweeps * len(starts))
+    x, place, best = NOM["seed"], [0] * R, None
+
+    def times(win, mark, state, limit):
+        total, new = 0.0, []
+        for k in range(K):
+            dur, edges, out, outq = models[k][0], models[k][1], exits[k], exitq[k]
+            fin, marks = state[k][0][:], state[k][1][:mark + 1]
+            free, end, last = marks[mark]
+            free = free[:]
+            for z0 in range(8 * mark, len(win), 8):
+                if z0 > 8 * mark:
+                    marks.append((free[:], end, last))
+                for n in win[z0:z0 + 8]:
+                    c = queue[n]
+                    t = free[c]
+                    for m, gap in edges[n]:
+                        y = fin[m] + gap
+                        if y > t:
+                            t = y
+                    t += dur[n]
+                    fin[n] = t
+                    if c != 5:
+                        free[c] = t
+                    t += out[n]
+                    if t > end:
+                        end, last = t, n
+                if k == K - 1 and total + end > limit:
+                    return 1e18, None
+            for c in range(3):
+                t = free[c] + outq[c]
+                total += soft * t
+                if t > end:
+                    end, last = t, -1 - c
+            total += end
+            new.append((fin, marks, end, last))
+        return total, new
+
+    def blocked(win, k, fin, n):
+        dur, edges = models[k][0], models[k][1]
+        before, ahead, pairs = [None] * 6, {}, []
+        for a in win:
+            ahead[a] = before[queue[a]]
+            before[queue[a]] = a
+        if n < 0:
+            n = before[-1 - n]
+        while n in ahead:
+            t, why = fin[n] - dur[n] - 1e-6, None
+            for m, gap in edges[n]:
+                if fin[m] + gap >= t:
+                    why = m
+                    break
+            if why is None:
+                why = ahead[n]
+                if why is not None and why not in preds[n]:
+                    pairs.append((why, n))
+            n = why
+        return pairs
+
+    for sweep in range(sweeps + 1):
+        alone = sweep < NOM["alone"] * sweeps
+        models, later = (every[:1], onward[:1]) if alone or len(every) == 1 else (every[1:], onward[1:])
+        K = len(models)
+        if alone:
+            best = None
+        heat = K * NOM["hot"] * (NOM["cold"] / NOM["hot"]) ** (sweep / max(1, sweeps - 1))
+        far, whole = [], 0.0
+        for k in range(K):
+            dur, tail, e = models[k][0], models[k][2], later[k]
+            d, nxt = [0.0] * R, [0.0] * 6
+            for n in reversed(seq):
+                t = max(tail[n], nxt[queue[n]])
+                for s, gap in e[n]:
+                    if d[s] + gap > t:
+                        t = d[s] + gap
+                d[n] = t + dur[n]
+                if queue[n] != 5:
+                    nxt[queue[n]] = d[n]
+            far.append(d)
+            whole += max(d) / K
+        if not alone and (best is None or whole < best[0]):
+            best = (whole, seq[:])
+        ORDER.setdefault("sweeps", []).append(round(whole))
+        if sweep == sweeps:
+            break
+        fins, frees = [[0.0] * R for _ in models], [[0.0] * 6 for _ in models]
+        for a in starts:
+            win, rest = seq[a:a + span], seq[a + span:]
+            for j, n in enumerate(win):
+                place[n] = j
+            inside = set(win)
+            exits, exitq = [], []
+            for k in range(K):
+                out = [0.0] * R
+                for n in win:
+                    out[n] = max([models[k][2][n]] + [far[k][s] + gap for s, gap in later[k][n] if s not in inside])
+                exits.append(out)
+                outq = [0.0] * 6
+                for n in reversed(rest[:200]):
+                    outq[queue[n]] = far[k][n]
+                exitq.append(outq)
+            now, state = times(win, 0, [(fins[k], [(frees[k], 0.0, -1)]) for k in range(K)], 1e18)
+            pairs, size = None, len(win)
+            for it in range(tries):
+                x = (x * 6364136223846793005 + 1442695040888963407) % 2 ** 64
+                if pairs is None:
+                    k = (x >> 60) % K
+                    pairs = blocked(win, k, state[k][0], state[k][3])
+                if not pairs:
+                    pairs = None
+                    if it > 8:
+                        break
+                    continue
+                m, n = pairs[(x >> 33) % len(pairs)]
+                i, j = place[m], place[n]
+                step, forward = (0, 0, 1, 2, 4, 8)[(x >> 20) % 6], (x >> 30) % 2
+                z = i if forward else j
+                while step and 0 < z < size - 1:
+                    z += -1 if forward else 1
+                    if queue[win[z]] == queue[n]:
+                        step -= 1
+                        i, j = (z, j) if forward else (i, z)
+                part, move = win[i:j + 1], {n if forward else m}
+                for b in (reversed(part) if forward else part):
+                    if b in move:
+                        move.update([y for y in (preds if forward else succs)[b] if y in inside and i <= place[y] <= j])
+                if m in move and n in move:
+                    continue
+                new = win[:i] + [b for b in part if (b in move) == bool(forward)] + [b for b in part if (b in move) != bool(forward)] + win[j + 1:]
+                limit = now - heat * math.log(((x >> 8) % 4096 + 0.5) / 4096)
+                v, after = times(new, i // 8, state, limit - soft * 2.9 * state[-1][2])
+                if v <= limit:
+                    now, win, state, pairs = v, new, after, None
+                    for z in range(i, j + 1):
+                        place[win[z]] = z
+                elif it % 16 == 15:
+                    pairs = None
+            seq[a:a + span] = win
+            fins = [s[0] for s in state]
+            frees = [s[1][hop // 8][0] if hop // 8 < len(s[1]) else s[1][-1][0] for s in state]
     return [n for j in best[1] for n in runs[j]]
 
 
@@ -460,12 +630,10 @@ def rank_program(g, core, T, topo):
     sent = {}
     now = [9, 0, "set"]
     groups = {}
-    KB = [(0, PAR["kb"], PAR["kb"]), (PAR["kb"], L, LP)]
-    CH = KB if PAR["two"] else [(0, L, LP)]
-    cut = CH[-1][0]
-    KEEP = PAR["keep"]
-    turn = [0]
-    kss = sorted(set([0] + [k for row in PAR["ks"] for k in row if k < 16]))
+    cut = PAR["cut"]
+    CH = [(0, cut, cut), (cut, L, LP)]
+    KEEP, SPLIT, WIN = PAR["keep"], PAR["split"], PAR["win"]
+    kss = sorted(set([0] + [x[2] for row in PAR["pieces"] for x in row if x[2] < 16]))
     common = [x for x in topo.engines(cores[0], cores[1]) if all(x in topo.engines(a, b) for a in cores for b in cores if a != b)]
 
     def ap(a):
@@ -473,6 +641,8 @@ def rank_program(g, core, T, topo):
             return a
         if a[0] == "i":
             return ap(a[1]).indirect(ap(a[2]))
+        if a[0] == "b":
+            return T[a[1]][:, a[2] if a[3] is None else slice(a[2], a[3]), a[4] if a[5] is None else slice(a[4], a[5])]
         _, name, c0, c1, st, p = a
         cs = slice(c0, c1) if st == 1 else slice(c0, c1, st)
         if p is None:
@@ -486,10 +656,10 @@ def rank_program(g, core, T, topo):
                 if not isinstance(a, tuple):
                     continue
                 if a[0] == "i":
-                    acc.append((a[1][1], a[1][2], a[1][3], 1, wr))
-                    acc.append((a[2][1], a[2][2], a[2][3], 1, False))
+                    acc.append(extent(a[1]) + (wr,))
+                    acc.append(extent(a[2]) + (False,))
                 else:
-                    acc.append((a[1], a[2], a[3], a[4], wr))
+                    acc.append(extent(a) + (wr,))
         dur = (100.0 if q else 0.0) if tok else duration(kind, outs, ins)
         ops.append({"q": q, "fn": fn, "acc": acc, "tok": tok, "dur": dur, "lat": NOM["pel"] if q == "t" else lat, "more": more,
                     "edge": False, "line": None, "group": None, "stop": [False], "tag": tuple(now), "spec": (kind, outs, ins)})
@@ -534,15 +704,15 @@ def rank_program(g, core, T, topo):
         stop = [False]
         rec("t", "mm", lambda e: e.matmul(ap(out), ap(lhs), ap(rhs), start, stop[0]), [out], [lhs, rhs])
         if start:
-            groups[out[1], out[2] // 512] = len(ops)
-        ops[-1].update({"edge": start, "group": groups[out[1], out[2] // 512], "stop": stop})
+            groups[out[1]] = len(ops)
+        ops[-1].update({"edge": start, "group": groups[out[1]], "stop": stop})
 
     def iota(out, pat, base, cm, flt=True):
         if flt:
             rec("g", "iota", lambda e: e.iota(ap(out), pat, base, cm, allow_small_or_imprecise_dtypes=True), [out], [])
         else:
             rec("g", "iota", lambda e: e.iota(ap(out), pat, base, cm), [out], [])
-        if out[1] in ("cI", "row", "R16", "R32", "VT"):
+        if out[1] in ("cI", "row", "R16", "R32") or out[1:3] == ("VT", 0):
             line("iota")
 
     def pick(out, x, pat, cmp, fill, base, cm):
@@ -560,50 +730,53 @@ def rank_program(g, core, T, topo):
     def col(j):
         return A("cF", j, j + 1)
 
-    def swap(bank, out0, n, srcs):
+    def swap(bank, out0, n, src):
         for q in range(2):
-            terms = [(g0, s) for s in srcs for g0 in range(2)]
-            for j, (g0, s) in enumerate(terms):
-                mm(A(bank, out0 + q, out0 + 2 * n, 2), A("LL", 128 * (2 * q + g0), 128 * (2 * q + g0 + 1)), s(g0), j == 0)
+            for g0 in range(2):
+                mm(A(bank, out0 + q, out0 + 2 * n, 2), A("LL", 128 * (2 * q + g0), 128 * (2 * q + g0 + 1)), src(g0), g0 == 0)
 
-    def before(out, name, at, c):
+    def before(out, name, at, c, early):
         b0, b1 = CH[c][0] // 32, CH[c][2] // 32
         for d in range(1, b1):
             lo = max(b0, d)
-            mm(A(out[1], out[2] + 2 * (lo - b0), out[3]), A("O32"), A(name, at + 2 * (lo - d), at + 2 * (b1 - d)))
+            if (d >= b1 - b0) == early:
+                mm(A(out[1], out[2] + 2 * (lo - b0), out[3]), A("O32"), A(name, at + 2 * (lo - d), at + 2 * (b1 - d)))
 
     dma("y", A("odi"), T.od[:], 2300.0)
-    dma("s", A("nbi"), T.nb[:], NOM["nb"])
-    dma("y", A("XT", 0, W), T.xs[:], NOM["xs"] - NOM["issue"])
+    dma("s", A("nbi", 0, W // 2), T.nb[:, 0:W // 2], NOM["nb"] - 1600)
+    dma("y", A("nbi", W // 2, W), T.nb[:, W // 2:W], NOM["nb"] - NOM["issue"])
+    dma("y", A("XT", 0, W), T.xs[:], NOM["xs"] - 2 * NOM["issue"])
     cp(A("XT", W, B), A("XT", 0, B - W))
-    iota(A("cI"), [[0, 6]], 0, 1, False)
+    iota(A("cI"), [[0, 8]], 0, 1, False)
     iota(A("row"), [[1, 160]], -16, 0)
     iota(A("R16"), [[16, 8], [0, 16]], 0, 0)
     iota(A("R32"), [[32, 4], [0, 32]], 0, 0)
-    iota(A("VT", 0, B // 2), [[1, B // 2]], -2047, 0)
+    iota(A("VT", 0, W // 2), [[1, W // 2]], -2047, 0)
     iota(A("RP"), [[1, 32], [0, 16]], 0, 0)
-    iota(A("kk"), [[0, 14], [1, 16]], 0, 0)
     iota(A("lanb"), [[32, 7], [0, 2]], -352, 0)
-    iota(A("par"), [[0, 7], [16, 2]], 15, 0)
-    act(A("VT", B // 2, B), A("VT", 0, B // 2), bias=float(B // 2))
-    ms(A("thi"), 0)
-    dma("y", A("thi", p=(15, 128, 16)), T.th[:], NOM["xs"])
-    dma("y", A("wti"), T.wt[:], NOM["xs"])
-    for j, msk in ((0, 15), (1, 112), (2, 31), (4, 96), (5, 16)):
+    iota(A("par"), [[0, 7], [1, 2]], 0, 0)
+    act(A("VT", W // 2, W), A("VT", 0, W // 2), bias=float(W // 2))
+    dma("y", A("thi", p=G8), T.th[:], NOM["xs"] - 2 * NOM["issue"])
+    dma("y", A("wti"), T.wt[:], NOM["xs"] - 2 * NOM["issue"])
+    for j, msk in ((0, 15), (1, 112), (2, 31), (4, 96), (5, 16), (6, 1), (7, 6)):
         ts(A("cI", j, j + 1), A("cI", j, j + 1), msk, OP.bitwise_and)
-    cp(A("cF", 0, 6), A("cI"))
+    cp(A("cF", 0, 8), A("cI"))
     ms(A("one"), 1.0)
     ms(A("DC"), 0.0)
-    ms(A("own"), 0.0)
     ms(A("a1", L, LP), -1.0)
-    for piece, value in ((A("cur"), L + B - 2047 - 4096), (A("TT", W, B + 192), 0), (A("mex"), 0), (A("snd", 0, 3 * U), 0), (A("kg", U, 64), 0)):
+    for piece, value in ((A("cur"), L - 1023), (A("cz"), B - 1024 - 4096), (A("TT", W, B + 192), 0), (A("VT", W, B), 0), (A("mex"), 0),
+                         (A("snd", 0, 3 * U), 0), (A("omf", 78, 96), 0), (A("Z0"), 0), (A("Sx"), -1), (A("Sy"), 0), (A("Sm"), -8192),
+                         (A("Sf"), 8192), (A("td"), 0), (A("td", 6, 27, 9), 3 * 2 ** 22), (A("td", 7, 27, 9), -3 * 2 ** 22), (A("tq", 1, 2), 1),
+                         (A("bt", 16, 108, 36), 0), (A("bt", 4 * rank, 108, 36), 0), (A("bt", 20, 36), -2 ** 23), (A("bt", 56, 72), -2 ** 23),
+                         (A("bt", 92, 108), -2 ** 23)):
         iota(piece, [[0, width(piece)]], value, 0)
     ts(A("oda"), A("odi"), 2047, OP.add)
     cp(A("od16"), A("odi"))
     ts(A("odb"), A("oda"), 2047, OP.bitwise_and)
     cp(A("om16"), A("odb"))
-    ts(col(6), col(0), 1.0, OP.add, 2.0, OP.min)
-    ts(col(7), col(0), 15.0, OP.is_lt, BIG, OP.mult)
+    if WIN:
+        cp(A("omf", 0, 78), A("odb"))
+    ts(col(8), col(0), 1.0, OP.add, 2.0, OP.min)
     ts(col(10), col(5), 0.0, OP.is_equal)
     ts(col(11), col(5), 0.0, OP.is_gt)
     ts(A("IW"), A("row"), col(3), OP.is_equal)
@@ -613,39 +786,47 @@ def rank_program(g, core, T, topo):
     ts(A("O32"), A("R32"), col(4), OP.is_equal)
     ts(A("RP"), A("RP"), col(2), OP.is_equal)
     ts(A("DK"), A("Ib"), col(0), OP.mult, 2048.0, OP.mult)
-    ts(A("DP"), A("Ib"), col(6), OP.mult, float(2 ** 27), OP.mult)
+    ts(A("DP"), A("Ib"), col(8), OP.mult, float(2 ** 27), OP.mult)
     ts(A("Lt"), A("row", 16, 144), col(3), OP.is_gt)
     tt(A("Lt"), A("Lt"), A("O32"), OP.mult)
-    ts(A("rst"), A("kk"), 0.0, OP.is_equal, BIG, OP.mult)
     for q in range(2):
         for g0 in range(2):
             at = 16 + 16 * (q - g0)
             act(A("LL", 128 * (2 * q + g0), 128 * (2 * q + g0 + 1)), A("IW", at, at + 128), scale=col(10 + q))
-    for name, src, sc in (("ZG", "Z1", -32768.0), ("ZM", "Z1", 65536.0), ("O3f", "O32", 32768.0), ("In", "Ib", -1.0), ("If", "Ib", 1.0),
-                          ("Zn", "Z1", -1.0), ("Z2", "Z1", 2.0), ("Bn", "B1", -1.0)):
+    for name, src, sc in (("ZG", "Z1", -32768.0), ("ZM", "Z1", 65536.0), ("In", "Ib", -1.0), ("If", "Ib", 1.0), ("Bn", "B1", -1.0)):
         act(A(name), A(src), scale=sc)
     act(A("BO", 0, 128), A("B1"), scale=-32768.0)
     for j, k in enumerate(kss[1:]):
         pick(A("BO", 128 * j + 128, 128 * j + 256), A("BO", 0, 128), [[0, 8], [1, 16]], OP.is_ge, 0.0, -k, 0)
     for name, value in (("LZ", 4096.0), ("LW", -560.0)):
         pick(A(name), A("Lt"), [[1, 128]], OP.not_equal, value, 0, -1)
-    rec("g", "iota", lambda e: e.iota(ap(A("Z0")), [[0, 128]], 0, 0, allow_small_or_imprecise_dtypes=True), [A("Z0")], [])
     for name, value in (("IB", BIG), ("ID", 1024.0)):
         pick(A(name), A("Z0"), [[1, 128]], OP.not_equal, value, 0, -1)
     act(A("lanc"), A("lanb"), bias=col(2))
     for l0, l1, lp in CH:
-        ts(A("LE", l0 // 16 + lp // 16, lp // 8), A("lanb", l0 // 16, lp // 16), col(2), OP.add, float(B - 2047 + 352), OP.add)
-    ts(A("mRG"), A("par"), col(2), OP.is_equal)
-    cp(col(8), A("wti"))
-    cp(col(9), A("thi"))
-    act(A("WZ"), A("Z1"), scale=col(8))
-    act(A("ytl", 0, 3), A("one", 0, 3), scale=col(9))
+        ts(A("nr", l0 + lp + 15, 2 * lp, 16), A("lanb", l0 // 16, lp // 16), col(2), OP.add, float(B - 2047 + 352), OP.add)
+    ts(A("mRG"), A("par"), col(6), OP.is_equal, 32768.0, OP.mult)
+    ts(A("O3f"), A("R32"), 1.0 / 16, OP.mult, col(7), OP.is_equal)
+    cp(col(9), A("wti"))
+    cp(A("ytl", 64, 65, p=G8), A("thi", p=G8))
+    act(A("WZ"), A("Z1"), scale=col(9))
+    act(A("ytl", 65, 67, p=G8), A("one", 0, 2, p=G8), scale=A("ytl", 64, 65, p=G8))
+    act(A("S2"), A("B1", 0, 128, 16), scale=2.0)
+    act(A("Iq"), A("Ib", 0, U), scale=0.25)
+    pick(A("Sx"), A("Sx"), [[-16, 8], [0, 17]], OP.is_ge, 0.0, 0, 1)
+    pick(A("Sx"), A("Sx"), [[16, 8], [0, 17]], OP.is_ge, 0.0, 15, -1)
+    for out, src in ((A("Sx", 16, 136, 17), A("Sm")), (A("Sy", 16, 136, 17), A("Sm")), (A("Sf"), A("Sf"))):
+        pick(out, src, [[-16, 8]], OP.is_equal, 0.0, -15, 1)
+    pick(A("r17"), A("mex", 0, 136), [[0, 8], [1, 17]], OP.not_equal, BIG, 0, 0)
+    pick(A("rst"), A("mex", 0, 128), [[0, 8], [1, 16]], OP.not_equal, BIG, 0, 0)
+    ms(A("td", 5, 27, 9), -0.375)
+    ms(A("tq", 0, 1), -0.25)
     for j in range(4):
         now[2] = "tt%d" % j
         ts(A("TT", 512 * j, 512 * j + 512), A("nbi", 512 * j, 512 * j + 512), -2047.0, OP.add)
     now[2] = "set"
-    act(A("thx", 0, 14), A("mRG"), scale=A("ytl", 0, 1))
-    mm(A("pg", 0, 14), A("O3f"), A("thx", 0, 14), True)
+    act(A("thx", 0, 14, p=G8), A("mRG", p=G8), scale=A("ytl", 64, 65, p=G8))
+    mm(A("pg", 0, 14), A("O3f", p=G8), A("thx", 0, 14, p=G8), True)
     cp(A("thP"), A("pg", 0, 14))
     tabled = (0, 14, 26, 40, 52, 66, 78)
     act(A("VT", B, B + LP), IND(A("VT", 0, W), A("od16", 0, 14)))
@@ -653,14 +834,14 @@ def rank_program(g, core, T, topo):
         act(A("VT", B + 16 * j0, B + 16 * j1), IND(A("VT", 0, W), A("od16", j0, j1)))
 
     def own_of(t, l0, l1):
-        return A("own", 320 * (t % 2) + l0, 320 * (t % 2) + l1)
+        return A("own", L * (t % 2) + l0, L * (t % 2) + l1)
 
-    def dif_at(c):
-        return 0 if c < len(CH) - 1 else LP + cut
+    def flags(s, w0=0, wp=14):
+        return A("fr", 14 * (s % 3) + w0, 14 * (s % 3) + wp)
 
     def guests_in(t):
         j = t - 3
-        now[0], now[2] = t, "gh"
+        now[:] = [t, 0, "gh"]
         gin, xb = A("gin%d" % j), A("xb", U * (j % 2), U * (j % 2) + U)
         rec(None, "", None, [gin], [], ("ga%d" % j, len(common)), 0.0, [sent["g", j]])
         mag = 1.5 * 2 ** 23
@@ -671,64 +852,48 @@ def rank_program(g, core, T, topo):
         ts(A("ha", 0, 3), A("hi", 0, 3), 2047, OP.bitwise_and)
         cp(A("h16", 0, 3), A("ha", 0, 3))
         ts(A("g16"), IND(A("TO%d" % j) if t in KEEP else A("TT", 0, W), A("h16", 0, 3)), 2047.0, OP.add)
-        tt(A("gr"), gin, xb, OP.subtract)
-        act(A("cap", U * (j % 2), U * (j % 2) + U), A("gr"), bias=col(7), scale=8192.0)
-
-    def against(out, got, mine, a, b, how, shift=0):
-        need, have = -(-(b - a) // 32), PAR["ring"][now[0]]
-        if turn[0] % have + need > have:
-            turn[0] = 0
-        bank, at = "pr", 512 * (turn[0] % have)
-        if mine == "xT" and PAR["gb"] is not None:
-            gb = PAR["gb"][now[0] - 3]
-            at = 512 * gb + 16 * (a if gb < 3 and not PAR["two"] else 0)
-            if a and PAR["g2"]:
-                bank, at = "pg", 256
-        else:
-            turn[0] += need
-        for x in range(a, b, 32):
-            n, p0 = min(32, b - x), (x + shift) % 128
-            cell = A(bank, at + 16 * (x - a), at + 16 * (x - a + n))
-            mm(cell, A(mine, x + shift - p0, x + shift - p0 + 128, p=(p0, p0 + n, 1)), A("RP", 0, 16 * n, p=(p0, p0 + n, 1)), True)
-            if how == "s":
-                mm(cell, A("In"), A(got[1], got[2] + 16 * (x - a), got[2] + 16 * (x - a + n)))
-        if how == "v":
-            tt(out, got, A(bank, at, at + 16 * (b - a)), OP.max)
-        else:
-            act(out, A(bank, at, at + 16 * (b - a)), ACT.Abs, None, 0.5)
 
     def guests_judged(t):
         j = t - 3
-        xb, key = A("xb", U * (j % 2), U * (j % 2) + U), A("pg", 64, 64 + U)
-        now[0], now[2] = t, "gM"
-        mm(A("pg", 128, 256, p=(0, U, 1)), xb, A("Ib"), True)
-        (cp if PAR["xq"] == "v" else act)(A("xT", p=(0, U, 1)), A("pg", 128, 256, p=(0, U, 1)))
-        first, h = True, PAR["gv"][j]
+        xb = A("xb", U * (j % 2), U * (j % 2) + U)
+        now[:] = [t, 0, "gM"]
+        mm(A("pq", 128, 256, p=(0, U, 1)), xb, A("Ib"), True)
+        act(A("xT", p=(0, U, 1)), A("pq", 128, 256, p=(0, U, 1)))
+        h = PAR["gv"][j]
         now[2] = "gG"
         if h:
             cp(A("Gg", 0, 16 * h), IND(A("XT", 0, W), A("g16", 0, h)))
         act(A("Gg", 16 * h, 16 * U), IND(A("XT", 0, W), A("g16", h, U)))
-        for a, b, who, how in PAR["guests"][j]:
+        slots48, by_max = (0, U, 1), PAR["guests"][j] == "v"
+
+        def brought():
+            now[2] = "g0"
+            mm(A("pg", 0, 136, p=slots48), xb, A("Sx" if by_max else "Sy"), True)
+            mm(A("pg", 16, 136, 17, slots48), A("gin%d" % j), A("Sf"))
+        parts = [(A("pg", 256, 512), 32, U), (A("pq"), 0, 32)]
+        for cell, a, b in parts:
+            now[2] = "gR"
+            mm(cell, A("xT", p=(a, b, 1)), A("RP", 0, 16 * (b - a), p=(a, b, 1)), True)
             now[2] = "gM"
-            against(A("Ag", 16 * a, 16 * b), A("Gg", 16 * a, 16 * b), "xT", a, b, how)
+            if not by_max:
+                mm(cell, A("In"), A("Gg", 16 * a, 16 * b))
+                act(A("Ag", 16 * a, 16 * b), cell, ACT.Abs, None, 0.5)
+        brought()
+        now[2] = "gM"
+        for cell, a, b in parts if by_max else ():
+            tt(A("Ag", 16 * a, 16 * b), A("Gg", 16 * a, 16 * b), cell, OP.max)
         now[2] = "gs"
-        runs = [(a, b) for a, b, who, how in PAR["guests"][j] if how == "v"]
-        if runs:
-            a, b = runs[0][0], runs[-1][1]
-            mm(key, A("Z0"), xb, True)
-            first = False
-            mm(A("pg", 64 + a, 64 + b), A("Bn"), A("xb", xb[2] + a, xb[2] + b))
-            for k in range(16):
-                mm(A("pg", 64 + a, 64 + b), A("Zn", 15 - k, 143 - k), A("Gg", 16 * a + k, 16 * b, 16))
+        for k in range(16 if by_max else 0):
+            mm(A("pg", k, 136, 17, slots48), A("Gg", k, 16 * U, 16), A("Bn", 0, 128, 16))
         now[2] = "gj"
         for k in range(16):
-            mm(key, A("Z2", 15 - k, 143 - k), A("Ag", k, 16 * U, 16), first and k == 0)
-        tt(A("kg", 0, U), A("pg", 64, 64 + U), A("cap", U * (j % 2), U * (j % 2) + U), OP.min)
-        tr(A("kgT"), A("kg"))
-        scan(A("js"), A("rst", 0, 64), A("kgT"), OP.add, OP.min)
-        tr(A("jC"), A("js"))
-        mine = A("bt", 16 * j + 4 * rank, 16 * j + 4 * rank + 1)
-        top(mine, A("jC"))
+            mm(A("pg", k, 136, 17, slots48), A("Ag", k, 16 * U, 16), A("S2"))
+        scan(A("js", p=slots48), A("r17", p=slots48), A("pg", 0, 136, p=slots48), OP.add, OP.min)
+        mm(A("pq", 0, U, p=G8), A("js", 16, 136, 17, slots48), A("Iq", p=slots48), True)
+        mine = A("bt", 36 * j + 4 * rank, 36 * j + 4 * rank + 1)
+        top(mine[:5] + (G8,), A("pq", 0, U, p=G8))
+        if t == 5:
+            act(A("jC", p=G8), A("pq", 0, U, p=G8), scale=4.0)
         masks = best_masks(core, cores, topo)
 
         def send(e):
@@ -743,15 +908,12 @@ def rank_program(g, core, T, topo):
     def threshold(t):
         j = t - 3
         n = sum(best_masks(c, cores, topo)[core][1] for c in cores if c != core)
-        old = A("ytl", t - 1, t)
-        now[0], now[2] = t, "thr"
-        act(A("th4", j, j + 1), old, bias=0.375, scale=0.25)
-        rec(None, "", None, [A("bt", 16 * j + 4 * r, 16 * j + 4 * r + 1) for r in range(NR) if r != rank], [], ("ba%d" % j, n), 0.0, [sent["b", j]])
-        top(A("bc", j, j + 1), A("bt", 16 * j, 16 * j + 16, 4))
-        ts(A("bi"), A("bc", j, j + 1), 0.25, OP.mult, A("th4", j, j + 1), OP.subtract)
-        ts(A("ytl", t, t + 1), A("bi"), 0.0, OP.max, old, OP.add)
+        now[:] = [t, 0, "thr"]
+        act(A("td", 9 * j + 4, 9 * j + 9, 4, G8), A("tq", p=G8), scale=A("ytl", 63 + t, 64 + t, p=G8))
+        rec(None, "", None, [A("bt", 36 * j + 4 * r, 36 * j + 4 * r + 1) for r in range(NR) if r != rank], [], ("ba%d" % j, n), 0.0, [sent["b", j]])
+        scan(A("ytl", t, 65 + t, 8, G8), A("td", 9 * j, 9 * j + 9, p=G8), A("bt", 36 * j, 36 * j + 36, 4, G8), OP.add, OP.max)
         if t == 3:
-            ts(A("thx", 14, 28), A("mRG"), A("ytl", t, t + 1), OP.mult)
+            ts(A("thx", 14, 28, p=G8), A("mRG", p=G8), A("ytl", 64 + t, 65 + t, p=G8), OP.mult)
 
     def floor_m(scale, l0, lp):
         ts(A("mi", l0 // 16, lp // 16), A("mn", l0 // 16, lp // 16), 2.0 ** -15, OP.mult, -0.46875, OP.add)
@@ -761,42 +923,50 @@ def rank_program(g, core, T, topo):
     def pack(t, l0, l1, lp):
         floor_m(2.0 ** -13, l0, lp)
         s0 = U * (4 - t)
-        tt(IND(A("snd", s0, s0 + 432), A("s16", l0 // 16, l1 // 16)), A("mC", l0, l1), A("ownf", l0, l1), OP.add)
+        tt(IND(A("snd", s0, s0 + 432), A("s16", l0 // 16, l1 // 16)), A("mC", l0, l1), A("ownf", L * (t % 2) + l0, L * (t % 2) + l1), OP.add)
+
+    def columns(t, l0, l1):
+        return IND(A("TT", 0, B + 240 if t - 1 in WIN else B + L * (t + 1)), A3("L16", 0, None, l0 // 16, l1 // 16))
+
+    def entries(l0, l1):
+        return A3("L16", 1, None, l0 // 16, l1 // 16)
 
     def front(t, c):
         now[:2] = [t, c]
         l0, l1, lp = CH[c]
-        n, w0, w1, wp = l1 - l0, l0 // 16, l1 // 16, lp // 16
-        hi = B + L * (t + 1)
-        po = "po%d" % c
-        c16, cc, fl = A("c16", l0, l1), A("DC", cut + l0, cut + l1) if t < 5 else A("cf", l0, l1), A("fl", l0, l1)
-        dif = A("DC", dif_at(c), dif_at(c) + n)
-        own = own_of(t, l0, l1)
-        e16 = A("L16", w0 + wp, wp + w1)
-        parts = [(l0, PAR["c0"]), (PAR["c0"], l1)] if l0 < PAR["c0"] < l1 else [(l0, l1)]
-        for j, (a, b) in enumerate(parts):
-            now[2] = "c%d" % j
-            if t == 0:
-                ts(A("c16", a, b), IND(A("nbi"), A("om16", a // 16, b // 16)), 1.0, OP.add)
-            else:
-                ts(A("c16", a, b), IND(A("TT", 0, hi), A("L16", w0 + a // 16, w0 + b // 16)), 2047.0, OP.add)
+        c16, own = A("c16", l0, l1), own_of(t, l0, l1)
+        now[2] = "c"
+        if t == 0:
+            ts(c16, IND(A("nbi"), A("om16", l0 // 16, l1 // 16)), 1.0, OP.add)
+        else:
+            ts(c16, columns(t, l0, l1), 2047.0, OP.add)
         now[2] = "own"
-        act(own, IND(A("XT", 0, hi), e16) if t else IND(A("XT", 0, W), A("od16", w0, w1)))
+        act(own, IND(A("XT", 0, B + L * (t + 1)), entries(l0, l1)) if t else IND(A("XT", 0, W), A("od16", l0 // 16, l1 // 16)))
         now[2] = "oT"
-        kinds = [x[3] for x in PAR["pieces"][t] if l0 <= x[0] < l1]
-        if "k" in kinds:
-            mm(A(po, 0, n) if PAR["two"] else A("pr", l0, l1), A("Ib"), own, True)
-        if set(kinds) != {"k"}:
-            wide, high = -(-n // 128) * 128, (0, min(n, 128), 1)
-            for j in range(0, wide, 128):
-                mm(A(po, j, j + 128, p=high), own_of(t, l0 + j, l0 + j + high[1]), A("Ib"), True)
-            (cp if PAR["oq"][t] == "v" else act)(A("oT", 256 * c, 256 * c + wide, p=high), A(po, 0, wide, p=high))
+        mm(A("po%d" % c, 0, l1 - l0), A("Ib"), own, True)
+        if t not in PAR["whole"]:
+            numbers(t, l0, l1, lp)
+        elif c == 1:
+            numbers(t, 0, L, LP)
+
+    def windows(t):
+        now[:] = [t, 1, "v16"]
+        bank = PAR["vb"]
+        for q in range(2):
+            for g0 in range(2):
+                for h in range(2):
+                    mm(A(bank, 496 + q, 510, 2), A("LL", 128 * (2 * q + g0), 128 * (2 * q + g0 + 1)),
+                       A("DT", LP * h + 16 * g0, LP * h + LP, 32), g0 + h == 0)
+        ts(A("v16"), A(bank, 496, 510), 2047.0, OP.add)
+
+    def numbers(t, l0, l1, lp):
+        c16, cc, fl, dif = A("c16", l0, l1), A("DC", l0, l1) if t < 5 else A("cf", l0, l1), A("fl", l0, l1), A("DC", LP + l0, LP + l1)
         now[2] = "cc"
         if t == 0:
             vrep, raw = A("VT", B + l0, B + l1), A("cr", l0, l1)
             ts(raw, c16, -2047.0, OP.add)
         else:
-            vrep, raw = IND(A("VT", 0, hi), e16), IND(A("TT", 0, hi), A("L16", 2 * w0, w0 + w1))
+            vrep, raw = IND(A("VT", 0, B + L * (t + 1)), entries(l0, l1)), columns(t, l0, l1)
         ts(fl, c16, 2048.0, OP.is_ge, -2048.0, OP.mult)
         tt(cc, raw, fl, OP.add)
         now[2] = "dif"
@@ -807,224 +977,213 @@ def rank_program(g, core, T, topo):
         now[2] = "DT"
         if t == 5:
             now[2] = "wr"
-            ts(IND(A("yno"), e16), cc, 1.0, OP.mult, 2047.0, OP.add)
-        elif t == 0:
-            tr(A("DT", cut + l0, cut + lp), A("DC", cut + l0, cut + lp))
+            ts(IND(A("yno"), entries(l0, l1)), cc, 1.0, OP.mult, 2047.0, OP.add)
+        elif t and lp - l0 == LP:
+            tr(A("DT"), A("DC"))
         else:
-            tr(A("DT", 2 * l0, 2 * lp), A("DC", 2 * l0, 2 * lp))
-            now[2] = "v16"
-            if c == len(CH) - 1:
-                for q in range(2):
-                    for g0 in range(2):
-                        turned = A("LL", 128 * (2 * q + g0), 128 * (2 * q + g0 + 1))
-                        mm(A(po, 256 + q, 270, 2), turned, A("DT", cut + 16 * g0, cut + LP, 32), g0 == 0)
-                        for d, (x0, x1, xp) in enumerate(CH):
-                            mm(A(po, 256 + x0 // 16 + q, 256 + xp // 16, 2), turned, A("DT", dif_at(d) + 16 * g0, dif_at(d) + xp - x0, 32))
-                ts(A("v16"), A(po, 256, 270), 2047.0, OP.add)
-        for kb, (b0, b1, bp) in enumerate(KB):
-            if l0 <= b0 < l1:
-                keys(t, kb)
+            for h in range(2 if t else 1):
+                tr(A("DT", LP * h + l0, LP * h + lp), A("DC", LP * h + l0, LP * h + lp))
 
-    def keys(t, kb):
-        b0, b1, bp = KB[kb]
-        pk = "pk%d" % kb
+    def so_far(t, c):
+        w0, wp = (CH[c][0] // 16, CH[c][2] // 16) if t in SPLIT else (0, 14)
+        return A("pk%d" % c, 464, 464 + wp - w0), w0, wp
+
+    def keys(t, c):
+        now[:2] = [t, c]
+        b0, b1, bp = CH[c]
+        pk, po = "pk%d" % c, "po%d" % c
+        now[2] = "mk"
+        if t and (c == 1 or t in SPLIT):
+            mk, w0, wp = so_far(t, c)
+            mm(mk, A("If"), A("mn", w0, wp) if t > 1 else A("ks", 15, LP, 16), True)
+            mm(mk, A("IB"), flags(t - 1, w0, wp))
+        if t in (2, 3):
+            bar(t, c, pk)
         now[2] = "ini"
         mm(A(pk, 0, bp - b0), A("DK"), A("one", 0, bp - b0), True)
         now[2] = "pen"
         mm(A(pk, 0, bp - b0), A("DP"), A("a1", b0, bp))
-        pieces = [x for x in PAR["pieces"][t] if b0 <= x[0] < b1]
-        for a, b, who, how in pieces:
-            got, out = A("G", 16 * a, 16 * b), A("M", 16 * a, 16 * b)
-            j = [x[0] for x in PAR["pieces"][t]].index(a)
-            now[2] = "G%d" % j
-            (cp if who == "v" else act)(got, IND(A("XT", 0, B), A("c16", a, b)))
-            now[2] = "M%d" % j
-            if how != "k":
-                against(out, got, "oT", a, b, how, 256 - cut if PAR["two"] and kb else 0)
-        cuts = [x for x in PAR["sums"][t] if b0 <= x <= b1]
-        for a, b in zip(cuts, cuts[1:]):
-            j = PAR["sums"][t].index(a)
-            if [x[3] for x in pieces if x[0] == a] == ["k"]:
-                ks, n, key = PAR["ks"][t][j], b - a, A(pk, a - b0, b - b0)
-                turns = -(-ks // (512 // n))
-                now[2] = "D%d" % j
-                for r in range(turns):
-                    k0, k1, at = ks * r // turns, ks * (r + 1) // turns, 512 * (turn[0] % (3 if t < 3 else 2) if PAR["two"] else 1 + turn[0] % (2 if t < 3 or PAR["gb"][t - 3] == 3 else 1))
-                    turn[0] += 1
-                    for k in range(k0, k1):
-                        cell = A("pr", at + n * (k - k0), at + n * (k - k0 + 1))
-                        mm(cell, A("In"), own_of(t, a, b), True)
-                        mm(cell, A("Ib"), A("G", 16 * a + k, 16 * b, 16))
-                    act(A("M", 16 * a + n * k0, 16 * a + n * k1), A("pr", at, at + n * (k1 - k0)), ACT.Abs, None, 0.5)
-                now[2] = "SG%d" % j
-                if ks < 16:
-                    mm(key, A("BO", 128 * kss.index(ks), 128 * kss.index(ks) + 128), own_of(t, a, b))
-                for k in range(ks, 16):
-                    mm(key, A("ZG", 15 - k, 143 - k), A("G", 16 * a + k, 16 * b, 16))
-                for k in list(range(ks, 16)) + list(range(ks)):
-                    piece = A("M", 16 * a + n * k, 16 * a + n * (k + 1))
-                    if k >= ks:
-                        now[2] = "M%d" % j
-                        tt(piece, A("G", 16 * a + k, 16 * b, 16), A("po%d" % kb, a - b0, b - b0) if PAR["two"] else A("pr", a, b), OP.max)
-                    now[2] = "S%s%d" % ("M" if k >= ks else "A", j)
-                    mm(key, A("ZM", 15 - k, 143 - k), piece)
+        ends = [0] + [x[0] for x in PAR["pieces"][t]]
+        turn = 0
+        for j, (b, who, ks) in enumerate(PAR["pieces"][t]):
+            a = ends[j]
+            if not b0 <= a < b1:
                 continue
-            runs = []
-            for x in pieces:
-                if a <= x[0] < b and x[3] == "v":
-                    if runs and runs[-1][1] == x[0]:
-                        runs[-1][1] = x[1]
-                    else:
-                        runs.append([x[0], x[1]])
-            now[2] = "SG%d" % PAR["sums"][t].index(a)
-            for r0, r1 in runs:
-                mm(A(pk, r0 - b0, r1 - b0), A("BO", 0, 128), own_of(t, r0, r1))
-                for k in range(16):
-                    mm(A(pk, r0 - b0, r1 - b0), A("ZG", 15 - k, 143 - k), A("G", 16 * r0 + k, 16 * r1, 16))
-            now[2] = "SM%d" % PAR["sums"][t].index(a)
-            for k in range(16):
-                mm(A(pk, a - b0, b - b0), A("ZM", 15 - k, 143 - k), A("M", 16 * a + k, 16 * b, 16))
+            now[2] = "G%d" % j
+            if who:
+                cp(A("G", 16 * a, 16 * (a + who)), IND(A("XT", 0, B), A("c16", a, a + who)))
+            if a + who < b:
+                act(A("G", 16 * (a + who), 16 * b), IND(A("XT", 0, B), A("c16", a + who, b)))
+            n, key = b - a, A(pk, a - b0, b - b0)
+            turns = -(-ks // (512 // n))
+            for r in range(turns):
+                k0, k1 = ks * r // turns, ks * (r + 1) // turns
+                bank = ["pr%d" % c, ("pq", "pg")[c]][turn % PAR["ring"][t]]
+                turn += 1
+                now[2] = "D%d" % j
+                for k in range(k0, k1):
+                    cell = A(bank, n * (k - k0), n * (k - k0 + 1))
+                    mm(cell, A("In"), own_of(t, a, b), True)
+                    mm(cell, A("Ib"), A("G", 16 * a + k, 16 * b, 16))
+                act(A("M", 16 * a + n * k0, 16 * a + n * k1), A(bank, 0, n * (k1 - k0)), ACT.Abs, None, 0.5)
+                now[2] = "SA%d" % j
+                for k in range(k0, k1):
+                    mm(key, A("ZM", 15 - k, 143 - k), A("M", 16 * a + n * k, 16 * a + n * (k + 1)))
+            if ks == 16:
+                continue
+            now[2] = "SG%d" % j
+            mm(key, A("BO", 128 * kss.index(ks), 128 * kss.index(ks) + 128), own_of(t, a, b))
+            for k in range(ks, 16):
+                mm(key, A("ZG", 15 - k, 143 - k), A("G", 16 * a + k, 16 * b, 16))
+            for k in range(ks, 16):
+                piece = A("M", 16 * a + n * k, 16 * a + n * (k + 1))
+                now[2] = "M%d" % j
+                tt(piece, A("G", 16 * a + k, 16 * b, 16), A(po, a - b0, b - b0), OP.max)
+                now[2] = "SM%d" % j
+                mm(key, A("ZM", 15 - k, 143 - k), piece)
 
-    def least(t, kb):
-        l0, l1, lp = KB[kb]
-        pk, n, k0 = "pk%d" % kb, lp - l0, LP * (t % 2)
-        kT, ks = A(pk, 256, 256 + n), A("ks", k0 + l0, k0 + lp)
-        now[2] = "k%d" % kb
-        tr(kT, A(pk, 0, n))
-        scan(ks, A("rst", 0, n), kT, OP.add, OP.min)
-        now[2] = "n%d" % kb
-        if t < 5:
-            tt(kT, ks, kT, OP.subtract)
-            tt(A("yy", l0, lp), A("DT", cut + l0, cut + lp), kT, OP.subtract)
-            scan(A("nr", l0, lp), kT, A("yy", l0, lp), OP.max, OP.min)
+    def bar(t, c, bank):
+        w0, wp = CH[c][0] // 16, CH[c][2] // 16
+        thG = A(bank, 496, 496 + wp - w0)
+        now[2] = "old"
+        mm(thG, A("IB"), flags(t - 1, w0, wp), True)
+        mm(thG, A("IB"), flags(t - 2, w0, wp))
+        now[2] = "th"
+        mm(thG, A("O3f", p=G8), A("thx", 14 * (t == 4) + w0, 14 * (t == 4) + wp, p=G8))
 
     def middle(t):
-        now[0], now[2] = t, "ownf"
+        now[:] = [t, 1, "ownf"]
         hi = B + L * (t + 1)
         if 2 <= t <= 4:
-            act(A("ownf"), own_of(t, 0, L))
+            act(A("ownf", L * (t % 2), L * (t % 2) + L), own_of(t, 0, L))
         now[2] = "wr"
         if t < 5:
-            cp(IND(A("TT", 0, W), A("v16" if t else "od16", 0, 13)), A("DC", cut, cut + L))
+            for l0, l1 in ((0, cut), (cut, L)) if t in PAR["wr2"] else ((0, L),):
+                cp(IND(A("TT", 0, W), A("v16" if t else "od16", l0 // 16, l1 // 16)), A("DC", l0, l1))
         if t == 4:
             now[2] = "out"
             act(A("yno", B, B + KN), IND(A("TT", 0, W), A("od16", 0, KN // 16)), bias=2047.0)
         if t + 1 in KEEP:
-            sent["copy", t - 2] = dma("y", A("TO%d" % (t - 2)), A("TT", 0, W), NOM["copy"])
+            dma("y", A("TO%d" % (t - 2)), A("TT", 0, W), NOM["copy"])
         if t < 5:
             now[2] = "seed"
-            act(A("TT", B + 192, hi + L), IND(A("TT", 0, W), A("om16", 12, 13 * (t + 2))), bias=1.0)
+            if t in WIN:
+                act(A("TT", B, B + 240), IND(A("TT", 0, W), A("ow16", 0, 15)), bias=1.0)
+            else:
+                act(A("TT", B + 192, hi + L), IND(A("TT", 0, W), A("om16", 12, 13 * (t + 2))), bias=1.0)
             now[2] = "tab"
             j0, j1 = tabled[t + 1] if t else 0, tabled[t + 2]
             act(A("XT", B + 16 * j0, B + 16 * j1), IND(A("XT", 0, W), A("od16", j0, j1)))
+
+    def slots(c, w0, wp):
+        now[2] = "s16"
+        swap("po%d" % c, 384, (wp - w0) // 2, lambda g0: A("slt", w0 + g0, wp, 2))
+        ts(A("s16", w0, wp), A("po%d" % c, 384, 384 + wp - w0), 560.0, OP.add)
 
     def back(t, c):
         now[:2] = [t, c]
         l0, l1, lp = CH[c]
         n, w0, wp = lp - l0, l0 // 16, lp // 16
         nw = wp - w0
-        po = "po%d" % c
+        pk, po, k0 = "pk%d" % c, "po%d" % c, LP * (t % 2)
         leave = 2 <= t <= 4
-        kmin = A("ks", LP * (t % 2) + l0 + 15, LP * (t % 2) + lp, 16)
-
-        def flags(s):
-            return A("fr", 14 * (s % 3) + w0, 14 * (s % 3) + wp)
-        zb = "pk%d" % c
-        mn, mk, thD, thG = A("mn", w0, wp), A(po if t >= 4 else zb, 464, 464 + nw), A(po, 304, 304 + nw), A(po, 320, 320 + nw)
-        thx = A("thx", 14 * (t == 4) + w0, 14 * (t == 4) + wp)
-
-        whole = t != 4 and c == len(CH) - 1
-        if whole:
-            mn, mk = A("mn"), A(mk[1], 464, 478)
-
-        def so_far():
-            now[2] = "mk"
-            mm(mk, A("If"), mn if t > 1 else A("ks", 15, LP, 16), True)
-            mm(mk, A("IB"), A("fr", 14 * ((t - 1) % 3), 14 * ((t - 1) % 3) + 14) if whole else flags(t - 1))
-        if t == 4 or (t == 5 and whole):
-            so_far()
-        now[2] = "th"
-        if leave:
-            now[2] = "old"
-            mm(thG, A("IB"), flags(t - 1), True)
-            mm(thG, A("IB"), flags(t - 2))
-            now[2] = "th"
-            mm(thG, A("O3f"), thx)
+        kmin = A("ks", k0 + l0 + 15, k0 + lp, 16)
+        thD, thG = A(po, 480, 480 + nw), A(po if t == 4 else pk, 496, 496 + nw)
         if t == 4:
-            mm(thD, A("O3f"), thx, True)
-        for kb in range(2):
-            if l0 <= KB[kb][0] < l1:
-                least(t, kb)
-        if 0 < t < 4 and whole:
-            so_far()
-        now[2] = "fate"
-        kall = A("ks", LP * (t % 2) + 15, LP * (t % 2) + LP, 16)
-        if t == 4 or (t == 5 and whole):
-            tt(mn, kall if whole else kmin, mk, OP.min)
+            bar(t, c, po)
+            mm(thD, A("O3f", p=G8), A("thx", 14 + w0, 14 + wp, p=G8), True)
+        kT, ks = A(pk, 256, 256 + n), A("ks", k0 + l0, k0 + lp)
+        now[2] = "k"
+        tr(kT, A(pk, 0, n))
+        scan(ks, A("rst", 0, n), kT, OP.add, OP.min)
+        if t < 5:
+            yy, ne = A("pr%d" % c, 0, n), A("ne", l0, lp)
+            now[2] = "y0"
+            mm(yy, A("Ib"), A("DT", l0, lp), True)
+            now[2] = "n"
+            tt(ne, ks, kT, OP.is_lt)
+            mm(yy, A("IB"), ne)
+            scan(A("nr", 2 * l0, l0 + lp), ne, yy, OP.mult, OP.min)
+
+        def least_m():
+            now[2] = "mn"
+            mk, m0, mp = so_far(t, c)
+            tt(A("mn", m0, mp), A("ks", k0 + 16 * m0 + 15, k0 + 16 * mp, 16), mk, OP.min)
+        if t in SPLIT or (t == 5 and c == 1):
+            least_m()
         if t == 5:
             return
-        fr, ww, zz = flags(t), A(po, 336, 336 + nw), A(zb, 480, 480 + nw)
-        low = mn if t == 4 else kmin
+        now[2] = "fate"
+        fr, ww, zz = flags(t, w0, wp), A(po, 336, 336 + nw), A(pk if leave else po, 480, 480 + 2 * nw)
+        low = A("mn", w0, wp) if t == 4 else kmin
         if leave:
             tt(A("go", w0, wp), low, thG, OP.is_ge)
         tt(A("dead", w0, wp) if leave else fr, low, thD if t == 4 else A("thP", w0, wp), OP.is_lt)
         if leave:
-            mm(ww, A("LW"), A("go", w0, wp), True)
+            if c:
+                now[2] = "w0"
+                mm(ww, A("Z0"), A("one", 0, nw), True)
+                before(ww, "go", 0, c, True)
+                now[2] = "fate"
+            mm(ww, A("LW"), A("go", w0, wp), not c)
             mm(ww, A("ID"), A("dead", w0, wp))
-            before(ww, "go", 0, c)
+            before(ww, "go", 0, c, False)
             stay = 1.5 * 2 ** 33
             ts(fr, ww, stay, OP.add, stay, OP.not_equal)
             now[2] = "slt"
             tt(A("slt", w0, wp), ww, A("lanc", w0, wp), OP.min)
+        if t in SPLIT and leave:
+            slots(c, w0, wp)
         now[2] = "cu"
-        mm(zz, A("If"), A("cur", w0, wp), True)
+        halves = [A(zz[1], 480 + nw * h, 480 + nw * h + nw) for h in range(2)]
+        mm(zz, A("Ib"), A("cz", 0, 2 * nw), True)
+        for half in halves:
+            mm(half, A("Ib"), A("cur", w0, wp))
+        if t in WIN:
+            mm(halves[0], A("In"), A("base", w0, wp))
+        now[2] = "z0"
+        for half in halves:
+            before(half, "fr", 14 * (t % 3), c, True)
         now[2] = "LE"
-        mm(zz, A("LZ"), fr)
-        before(zz, "fr", 14 * (t % 3), c)
-        tt(A("LE", w0 + wp, 2 * wp), zz, A("LE", w0 + wp, 2 * wp), OP.max)
+        for half in halves:
+            mm(half, A("LZ"), fr)
+            before(half, "fr", 14 * (t % 3), c, False)
         now[2] = "LN"
-        tt(A("LE", 2 * w0, w0 + wp), zz, A("nr", l0 + 15, lp, 16), OP.max)
-
-        def slots():
-            now[2] = "s16"
-            swap(po, 384, nw // 2, [lambda g0: A("slt", w0 + g0, wp, 2)])
-            ts(A("s16", w0, wp), A(po, 384, 384 + nw), 560.0, OP.add)
-        if t in PAR["gofirst"]:
-            slots()
-        if t in PAR["efirst"]:
-            now[2] = "E16"
-            swap(po, 352 + nw, nw // 2, [lambda g0: A("LE", w0 + wp + g0, 2 * wp, 2)])
-            ts(A("L16", w0 + wp, 2 * wp), A(po, 352 + nw, 352 + 2 * nw), 2047.0, OP.add)
-            now[2] = "L16"
-            swap("pk1", 448, nw // 2, [lambda g0: A("LE", 2 * w0 + g0, w0 + wp, 2)])
-            ts(A("L16", 2 * w0, w0 + wp), A("pk1", 448, 448 + nw), 2047.0, OP.add)
-        else:
-            now[2] = "L16"
-            swap(po, 352, nw, [lambda g0: A("LE", 2 * w0 + g0, 2 * wp, 2)])
-            ts(A("L16", 2 * w0, 2 * wp), A(po, 352, 352 + 2 * nw), 2047.0, OP.add)
-        if leave and t not in PAR["gofirst"]:
-            slots()
-        now[2] = "mn"
-        if 0 < t < 4 and whole:
-            tt(mn, kall, mk, OP.min)
+        both = A("nr", 2 * l0 + 15, 2 * lp, 16)
+        tt(both, zz, both, OP.max)
+        now[2] = "L16"
+        swap(po, 352, nw, lambda g0: A("nr", 2 * l0 + 15 + 16 * g0, 2 * lp, 32))
+        ts(A3("L16", 0, 2, w0, wp), A(po, 352, 352 + 2 * nw), 2047.0, OP.add)
+        if t and c == 1 and t not in SPLIT:
+            least_m()
+        if leave and c == 1 and t not in SPLIT:
+            slots(c, 0, 14)
         now[2] = "pack"
-        if t in PAR["split"]:
+        if t in SPLIT and leave:
             pack(t, l0, l1, lp)
 
     def after(t):
-        now[0], now[2] = t, "cur"
+        now[:] = [t, 1, "cur"]
         f0 = 14 * (t % 3)
         if t < 4:
-            mm(A("pk1", 496, 510), A("If"), A("cur"), True)
+            mm(A("pr1", 496, 510), A("Ib"), A("cur"), True)
             for d in range(1, 7):
-                mm(A("pk1", 496, 510 - 2 * d), A("O32"), A("fr", f0 + 2 * d, f0 + 14))
-                mm(A("pk1", 496 + 2 * d, 510), A("O32"), A("fr", f0, f0 + 14 - 2 * d))
-            mm(A("pk1", 496, 510), A("O32"), A("fr", f0, f0 + 14))
-            act(A("cur"), A("pk1", 496, 510), bias=float(L - LP))
+                mm(A("pr1", 496, 510 - 2 * d), A("O32"), A("fr", f0 + 2 * d, f0 + 14))
+                mm(A("pr1", 496 + 2 * d, 510), A("O32"), A("fr", f0, f0 + 14 - 2 * d))
+            mm(A("pr1", 496, 510), A("O32"), A("fr", f0, f0 + 14))
+            ts(A("cur"), A("pr1", 496, 510), float(L - LP), OP.add)
+        if t + 1 in WIN:
+            now[2] = "win"
+            mag = 1.5 * 2 ** 27
+            ts(A("base"), A("cur"), mag, OP.add, 1008.0 - mag, OP.add)
+            for g0 in range(2):
+                mm(A("pr1", 510, 511), A("LL", 128 * g0, 128 * g0 + 128), A("base", g0, g0 + 1), g0 == 0)
+            ts(A("w16", 0, 1), A("pr1", 510, 511), 1.0 / 16, OP.mult, col(0), OP.add)
+            cp(A("ow16"), IND(A("omf"), A("w16", 0, 1)))
         now[2] = "pack"
         if t >= 2:
             j = t - 2
-            if t not in PAR["split"]:
+            if t not in SPLIT:
                 pack(t, 0, L, LP)
             s0 = U * (2 - j)
             dst = cores[(rank + 1 + t % (NR - 1)) % NR]
@@ -1033,43 +1192,51 @@ def rank_program(g, core, T, topo):
                 rid, pid = topo.addr(dst, core)
                 return e.remote_dma(ap(A("gin%d" % j)), ap(A("snd", s0, s0 + U)), T.sem["ga%d" % j], T.sem["left%d" % j], pid, rid,
                                     sum(1 << x for x in common))
-            sent["g", j] = rec("g", "", send, [], [A("snd", s0, s0 + U)], ("left%d" % j, len(common)), NOM["rem"] + (NOM["first"] if j == 0 else 0.0),
-                               [sent["copy", j]] if ("copy", j) in sent and PAR["clear"] else [])
+            sent["g", j] = rec("g", "", send, [], [A("snd", s0, s0 + U)], ("left%d" % j, len(common)), NOM["rem"] + (NOM["first"] if j == 0 else 0.0))
 
-    def guests(t, where):
-        if t >= 3 and PAR["gpos"][t - 3] == where:
-            guests_judged(t)
-            if t == 5:
-                dma("y", T.yg[:], A("jC", 0, U, p=(15, 128, 16)))
-            threshold(t)
+    def guests(t):
+        if t < 5:
+            guests_in(t)
+        guests_judged(t)
+        if t == 5:
+            dma("y", T.yg[:], A("jC", p=G8))
+        threshold(t)
 
-    for c in range(len(CH)):
-        front(0, c)
+    def both_keys(t):
+        if t in PAR["whole"]:
+            front(t, 1)
+            keys(t, 0)
+        else:
+            keys(t, 0)
+            front(t, 1)
+        if 0 < t < 5:
+            windows(t)
+        keys(t, 1)
+
+    front(0, 0)
+    both_keys(0)
     middle(0)
     for t in range(NT - 1):
-        if PAR["two"]:
-            back(t, 0)
-            guests(t, 1)
-            front(t + 1, 0)
-            guests(t, 2)
-        back(t, len(CH) - 1)
+        back(t, 0)
+        if t == 4:
+            guests(4)
+        front(t + 1, 0)
+        back(t, 1)
         after(t)
-        if not PAR["two"]:
-            guests(t, 1)
-        front(t + 1, len(CH) - 1)
-        guests(t, 3)
-        if t + 1 >= 3:
-            guests_in(t + 1)
+        both_keys(t + 1)
+        if t == 4:
+            guests_in(5)
         middle(t + 1)
-        guests(t + 1, 0)
-    dma("y", T.yt[:], A("ytl", 0, NT, p=(15, 128, 16)))
+        if t == 2:
+            guests(3)
+    guests(5)
+    dma("y", T.yt[:], A("ytl", 64, 64 + NT, p=G8))
     now[2] = "out"
     dma("y", T.yn[:], A("yno", B, B + KN), 3500.0)
-    for c, (l0, l1, lp) in enumerate(CH):
-        now[2] = "out"
-        act(A("vf", l0, l1), IND(A("VT", 0, B + Q), A("L16", (l0 + lp) // 16, (lp + l1) // 16)), bias=2047.0)
-        back(5, c)
+    act(A("vf"), IND(A("VT", 0, B + Q), entries(0, L)), bias=2047.0)
     dma("y", T.yv[:], A("vf", p=(0, 128, 16)))
+    for c in range(2):
+        back(5, c)
     floor_m(1.0, 0, LP)
     dma("s", T.ym[:], A("mC", 0, L, p=(15, 128, 16)))
     emit(g, T, ops)

@@ -1,4 +1,5 @@
 import math
+import numpy as np
 from concourse.bass import DstId, RemoteDMATransfer
 from concourse.mybir import AluOpType, AxisListType, ActivationFunctionType
 
@@ -7,34 +8,28 @@ B = 2064
 LP = 224
 H = "float16"
 BIG = float(2 ** 30)
+XS = float(2 ** 29)
 G8 = (0, 8, 1)
 PAR = {
     "cut": 128,
-    "pieces": [[(64, 32, 8), (128, 0, 8), (208, 0, 6)]] * 3 + [[(64, 0, 8), (128, 0, 8), (208, 0, 6)]] * 3,
-    "guests": "vsv", "gv": [24, 0, 24],
+    "pieces": [[(64, who, 8), (128, 0, 8), (208, 0, 6)] for who in (64, 48, 32, 0, 0, 0)],
+    "guests": ["vv", "ss", "vv"], "gv": [[("v", 0, 24), ("s", 24, U)], [("s", 0, U)], [("v", 0, 24), ("s", 24, U)]],
+    "early": [],
     "keep": [3, 4],
     "split": [2, 4],
     "ring": [2, 2, 2, 1, 1, 1],
     "win": [2, 3, 4],
     "whole": [0, 1, 2, 3, 4, 5],
-    "wide": True, "wr2": [], "vb": "pr0",
+    "tts": 1, "wide": [], "wr2": [], "vb": "pr0",
 }
 NOM = {"cyc": 0.83, "gat": 1.56, "sca": 3.8, "vfix": 20.0, "sfix": 50.0, "pe": 0.42, "sem": 130.0, "pel": 60.0, "self": 110.0, "rem": 3300.0,
-       "first": 2500.0, "issue": 1000.0, "far": 1.0, "nb": 5500.0, "xs": 7200.0, "copy": 6000.0,
-       "seed": 3, "passes": 2, "tries": 1200000, "hot": 300.0, "cold": 30.0, "span": 80, "hop": 32, "sweeps": 40, "soft": 0.08, "alone": 0.75, "lead": 4.0, "run": 3, "back": 6000.0}
-DUE = {"set": -100, "tt0": -90, "tt1": -90, "tt2": -87, "tt3": -87, "c": 0, "own": .3, "G0": .6, "G1": .6, "G2": .6, "oT": 1, "cc": 1,
-       "dif": 1.4, "a1": 1.6, "DT": 1.8, "v16": 2, "wr": 2.3, "mk": 2.9, "old": 2.9, "th": 2.95, "ini": 3, "pen": 3.5, "seed": 4,
-       "SG0": 3.9, "SG1": 3.9, "SG2": 3.9, "M0": 4, "M1": 4, "M2": 4, "D0": 4.2, "D1": 4.6, "D2": 4.2, "SM0": 5, "SM1": 5, "SM2": 5,
-       "SA0": 5, "SA1": 5.2, "SA2": 5, "ownf": 5, "y0": 5, "w0": 5.5, "cu": 5.5, "z0": 5.6, "k": 6, "fate": 6.3, "n": 6.5, "slt": 6.6,
-       "mn": 7, "s16": 7, "LN": 7.4, "LE": 7.5, "pack": 7.5, "L16": 8, "out": 8, "tab": 9, "cur": 9, "win": 9}
-for part in ("gh", "gG", "gR", "g0", "gM", "gs", "gj", "thr"):
-    DUE.update({"3" + part: -5, "4" + part: 11, "5" + part: -1})
-VARIANTS = [{"vfix": 23.0, "sfix": 65.0, "cyc": 0.95, "pe": 0.48, "far": 1.07}, {"gat": 1.3, "sca": 3.0},
-            {"vfix": 26.0, "sfix": 80.0, "sem": 140.0, "self": 120.0, "pel": 70.0, "cyc": 1.08, "pe": 0.55, "gat": 1.8, "sca": 4.8, "far": 1.15}]
-STAGES = [((0.2, 1, 1), [(0.5, {("v", 2, 0, "c")}), (0.5, {("v", 2, 1, "c")})]),
-          ((0.25, 1, 1), [(0.7, {("g", 2, 1, "pack")}), (0.15, {("v", 3, 0, "c")}), (0.15, {("v", 3, 1, "c")})]),
-          ((0.35, 1, 1), [(0.8, {("g", 4, 1, "pack")}), (0.1, {("g", 3, 1, "pack")}), (0.1, {("v", 5, 0, "c")})]),
-          ((0.2, 1, 1), [(1.0, None)])]
+       "call": 800.0, "first": 1200.0, "issue": 1000.0, "far": 1.0, "nb": 5500.0, "xs": 7200.0, "copy": 6000.0,
+       "seed": 3, "passes": 25000, "weights": (1.0, 0.0, 0.0, 0.0), "wide": 1800.0, "shake": 4000.0, "warm": 150.0, "cool": 10.0,
+       "tries": 150000, "hot": 60.0, "cold": 10.0, "span": 80, "hop": 32, "sweeps": 20, "soft": 0.08, "alone": 0.0, "run": 3}
+VARIANTS = [{"vfix": 30.0, "sfix": 75.0, "sem": 140.0, "self": 120.0, "pel": 70.0, "cyc": 1.03, "pe": 0.52, "far": 0.8},
+            {"vfix": 26.0, "sfix": 60.0, "cyc": 0.9, "pe": 0.46, "far": 0.72},
+            {"vfix": 33.0, "sfix": 90.0, "sem": 150.0, "self": 125.0, "pel": 75.0, "cyc": 1.2, "pe": 0.61, "gat": 1.95, "sca": 4.5, "far": 0.9},
+            {"vfix": 33.0, "sfix": 80.0, "sem": 150.0, "self": 125.0, "pel": 75.0, "cyc": 1.15, "pe": 0.58, "gat": 1.2, "sca": 4.5, "far": 0.85}]
 ORDER = {}
 F, BF, I, U16 = "float32", "bfloat16", "int32", "uint16"
 
@@ -50,30 +45,31 @@ def _ps():
 SCRATCH = {
     "nbi": _sb(W, I), "TT": _sb(B + Q, F), "XT": _sb(B + Q, BF), "VT": _sb(B + Q, F),
     "TO0": _sb(W, F), "TO1": _sb(W, F), "odi": _sb(78, I), "oda": _sb(78, I), "odb": _sb(78, I), "od16": _sb(78, U16), "om16": _sb(78, U16),
-    "G": _sb(16 * L, BF), "M": _sb(16 * L, BF), "Gg": _sb(16 * U, BF), "Ag": _sb(16 * U, BF),
-    "own": _sb(2 * L, BF), "xT": _sb(128, BF), "Z0": _sb(128, BF), "RP": _sb(512, BF), "ownf": _sb(2 * L, F), "c16": _sb(L, U16),
+    "G": _sb(16 * L, BF), "M": _sb(16 * L, BF), "Mw": _sb(2048, BF), "Gg": _sb(16 * U, BF), "Ag": _sb(16 * U, BF),
+    "own": _sb(2 * LP, BF), "xT": _sb(128, BF), "Z0": _sb(128, BF), "RP": _sb(512, BF), "ownf": _sb(2 * L, F), "c16": _sb(L, U16),
     "cr": _sb(L, H), "fl": _sb(L, H), "DC": _sb(2 * LP, H), "DT": _sb(2 * LP, H), "a1": _sb(LP, BF),
     "ks": _sb(2 * LP, F), "ne": _sb(LP, BF), "nr": _sb(2 * LP, H), "mex": _sb(LP, F), "mC": _sb(LP, F),
     "base": _sb(14, H), "w16": _sb(2, U16), "ow16": _sb(16, U16), "omf": _sb(96, F),
     "dead": _sb(14, BF), "go": _sb(14, BF), "fr": _sb(42, BF),
     "L16": _sb(2, U16, 14), "slt": _sb(14, H), "s16": _sb(14, U16), "v16": _sb(14, U16),
     "mn": _sb(14, F), "mi": _sb(14, I), "thP": _sb(14, F), "thx": _sb(28, F), "cur": _sb(14, H), "cz": _sb(16, H),
-    "row": _sb(160, BF), "IW": _sb(160, BF), "cI": _sb(8, I), "cF": _sb(12, F), "R16": _sb(128, BF), "R32": _sb(128, BF),
+    "row": _sb(160, BF), "cI": _sb(8, I), "cF": _sb(12, F), "R16": _sb(128, BF), "R32": _sb(128, BF),
     "lanb": _sb(14, F), "par": _sb(14, F), "lanc": _sb(14, F), "mRG": _sb(14, F),
-    "Sx": _sb(136, BF), "Sy": _sb(136, BF), "Sm": _sb(8, BF), "Sf": _sb(8, F), "S2": _sb(8, BF), "Iq": _sb(U, F), "r17": _sb(136, F),
-    "td": _sb(27, F), "tq": _sb(2, F), "Z1": _sb(144, BF), "ZM": _sb(144, BF), "ZG": _sb(144, BF), "WZ": _sb(144, BF),
-    "Bn": _sb(128, BF), "Ib": _sb(128, BF), "In": _sb(128, BF), "If": _sb(128, F), "B1": _sb(128, BF), "BO": _sb(128 * 8, BF),
-    "DP": _sb(128, BF), "DK": _sb(128, BF), "O32": _sb(128, BF), "O3f": _sb(128, F), "Lt": _sb(128, BF), "LZ": _sb(128, BF), "LW": _sb(128, BF),
+    "Sx": _sb(136, BF), "Sy": _sb(136, BF), "Sf": _sb(8, F), "S2": _sb(8, BF), "Iq": _sb(U, F), "r17": _sb(136, F),
+    "td": _sb(27, F), "tq": _sb(2, F), "ZM": _sb(144, BF), "ZG": _sb(144, BF),
+    "Bn": _sb(8, BF), "Ib": _sb(128, BF), "In": _sb(128, BF), "If": _sb(128, F), "BO": _sb(128 * 8, BF),
+    "DP": _sb(128, BF), "O32": _sb(128, BF), "O3f": _sb(128, F), "Lt": _sb(128, BF), "LZ": _sb(128, BF), "LW": _sb(128, BF),
     "ID": _sb(128, BF), "IB": _sb(128, BF), "LL": _sb(512, BF),
     "one": _sb(LP, BF), "rst": _sb(128, F),
     "wti": _sb(1, I), "thi": _sb(1, I), "ytl": _sb(72, F),
     "snd": _sb(528, F), "gin0": _sb(U, F), "gin1": _sb(U, F), "gin2": _sb(U, F),
-    "xb": _sb(2 * U, BF), "hi": _sb(4, I), "ha": _sb(4, I), "h16": _sb(4, U16), "g16": _sb(U, U16), "js": _sb(136, F), "jC": _sb(U, F),
+    "idf": _sb(32, F), "id16": _sb(32, U16), "sne": _sb(432, F), "gine": _sb(U, F), "WB": _sb(128, BF), "MB": _sb(57, BF), "hd": _sb(171, F), "hs": _sb(57, F), "hf": _sb(4, F),
+    "xb": _sb(3 * U, BF), "h16": _sb(4, U16), "g16": _sb(U, U16), "js": _sb(136, F), "jC": _sb(U, F),
     "bt": _sb(108, F), "vf": _sb(L, F), "yno": _sb(B + Q, F), "cf": _sb(L, F),
     "pk0": _ps(), "pk1": _ps(), "po0": _ps(), "po1": _ps(), "pr0": _ps(), "pr1": _ps(), "pq": _ps(), "pg": _ps(),
 }
 NDMA = 19
-SEMAPHORES = (["qv", "qs", "qt", "qg", "ga0", "ga1", "ga2", "ba0", "ba1", "ba2"] + ["left%d" % j for j in range(6)]
+SEMAPHORES = (["qv", "qs", "qt", "qg", "ga0", "ga1", "ga2", "gae", "ba0", "ba1", "ba2", "lf0", "lf1", "lf2", "lfe", "left3", "left4", "left5"]
               + ["d%d" % j for j in range(NDMA)])
 OP = AluOpType
 ACT = ActivationFunctionType
@@ -167,7 +163,7 @@ def plan(ops):
         for m in sorted(deps, reverse=True):
             if not done >> m & 1:
                 kept.add(m)
-                done |= ops[m]["done"] | ops[m]["ahead"] | 1 << m
+                done |= ops[m]["done"] | (0 if ops[m]["tok"] else ops[m]["ahead"]) | 1 << m
         if o["q"] is None:
             done, ahead = 0, 0
         o["done"], o["ahead"] = done, ahead
@@ -178,70 +174,113 @@ def plan(ops):
 
 
 def schedule(ops):
-    N = len(ops)
-    pred, succ = [[] for _ in ops], [[] for _ in ops]
-    for n, o in enumerate(ops):
-        for m in o["deps"] | o["after"]:
-            gap = 0.0 if m not in o["deps"] else ops[m]["lat"] + NOM["self" if ops[m]["q"] == o["q"] else "sem"]
-            pred[n].append((m, gap))
-            succ[m].append((n, gap))
-    rest = [0.0] * N
-    for n in range(N - 1, -1, -1):
-        rest[n] = ops[n]["dur"] + max([ops[n]["lat"]] + [rest[s] + gap for s, gap in succ[n]])
+    runs, queue, models, preds, succs, seq = gather_runs(ops, list(range(len(ops))))
+    R, (dur, edges, tail) = len(runs), models[0]
+    ahead = [[(m, gap + dur[m]) for m, gap in e] for e in edges]
+    behind = [[] for _ in runs]
+    for n in range(R):
+        for m, gap in edges[n]:
+            behind[m].append((n, gap + dur[n]))
+    part = [(ops[r[0]]["tag"][:2], ops[r[0]]["tag"][2][0] == "g") for r in runs]
 
-    def place(key, edges, others, first):
-        miss = [len(e) for e in edges]
-        start, busy, seq = [0.0] * N, {}, []
-        todo, at, ready, waiting = sorted(range(N), key=key), 0, [], set()
-        while len(seq) < N:
-            if ready:
-                n = min(ready, key=key)
+    def place(key, need, frees, first):
+        miss = [len(e) for e in need]
+        start, busy, done, ready, passed = [0.0] * R, [([], []) for _ in range(6)], [], [], [False] * R
+        for n in np.argsort(key, kind="stable").tolist():
+            passed[n] = True
+            if miss[n]:
+                continue
+            while True:
+                t, d, c = first[n], dur[n], queue[n]
+                for m, gap in need[n]:
+                    y = start[m] + gap
+                    if y > t:
+                        t = y
+                if c != 5:
+                    begins, ends = busy[c]
+                    j = size = len(ends)
+                    while j and ends[j - 1] > t:
+                        j -= 1
+                    while j < size and begins[j] < t + d:
+                        t = ends[j]
+                        j += 1
+                    begins.insert(j, t)
+                    ends.insert(j, t + d)
+                start[n] = t
+                done.append(n)
+                for s in frees[n]:
+                    miss[s] -= 1
+                    if not miss[s] and passed[s]:
+                        ready.append(s)
+                if not ready:
+                    break
+                n = min(ready, key=lambda x: key[x])
                 ready.remove(n)
-            else:
-                n = todo[at]
-                at += 1
-                if miss[n]:
-                    waiting.add(n)
-                    continue
-            t = max([first[n]] + [start[m] + ops[m]["dur"] + gap for m, gap in edges[n]])
-            if ops[n]["q"]:
-                row = busy.setdefault(ops[n]["q"], [])
-                lo, hi = 0, len(row)
-                while lo < hi:
-                    mid = (lo + hi) // 2
-                    if row[mid][1] <= t:
-                        lo = mid + 1
-                    else:
-                        hi = mid
-                while lo < len(row) and row[lo][0] < t + ops[n]["dur"]:
-                    t = max(t, row[lo][1])
-                    lo += 1
-                row.insert(lo, (t, t + ops[n]["dur"]))
-            start[n] = t
-            seq.append(n)
-            for s, _ in others[n]:
-                miss[s] -= 1
-                if miss[s] == 0 and s in waiting:
-                    waiting.remove(s)
-                    ready.append(s)
-        return start, seq
+        return start, done
 
-    zero, tail = [0.0] * N, [o["lat"] for o in ops]
-    loads = [1e6 * max(0, 5 - n) for n in range(N)]
-    prio = [0.0] * N
-    for n in range(N - 1, -1, -1):
-        t, c, name = ops[n]["tag"]
-        own = 10 * t + NOM["lead"] * c + DUE.get("%d%s" % (t, name), DUE.get(name, 99))
-        prio[n] = min([own - loads[n]] + [prio[s] for s, _ in succ[n]])
-    best = None
-    for _ in range(NOM["passes"]):
-        start, seq = place(lambda n: (prio[n], -rest[n], n), pred, succ, zero)
-        end = max(start[n] + ops[n]["dur"] + tail[n] for n in range(N))
-        if best is None or end < best[0]:
-            best = (end, start, {n: j for j, n in enumerate(seq)})
-        back, _ = place(lambda n: (-start[n] - ops[n]["dur"], -n), succ, pred, tail)
-        prio = [-back[n] - ops[n]["dur"] - loads[n] for n in range(N)]
-    return improve(ops, sorted(range(N), key=lambda n: (best[1][n], best[2][n])))
+    def judge(start, done, back):
+        at = [-start[n] - dur[n] for n in range(R)] if back else start[:]
+        done = done[::-1] if back else done
+        for n in done:
+            for m in preds[n]:
+                if at[m] > at[n]:
+                    at[n] = at[m]
+        order, total = [done[j] for j in np.argsort([at[n] for n in done], kind="stable").tolist()], 0.0
+        for (dk, ek, tk), weight in zip(models, NOM["weights"]):
+            if not weight:
+                continue
+            fin, free, end = [0.0] * R, [0.0] * 6, 0.0
+            for n in order:
+                c = queue[n]
+                t = free[c]
+                for m, gap in ek[n]:
+                    y = fin[m] + gap
+                    if y > t:
+                        t = y
+                t += dk[n]
+                fin[n] = t
+                if c != 5:
+                    free[c] = t
+                t += tk[n]
+                if t > end:
+                    end = t
+            total += weight * end
+        return total, order
+
+    zero, rest = [0.0] * R, [0.0] * R
+    for n in reversed(seq):
+        rest[n] = dur[n] + max([tail[n]] + [rest[s] + gap - dur[s] for s, gap in behind[n]])
+    start, done = place([-y for y in rest], ahead, succs, zero)
+    now, order = judge(start, done, False)
+    best, back, x, passes = (now, order), False, NOM["seed"], NOM["passes"]
+
+    def draw(x):
+        return (x * 6364136223846793005 + 1442695040888963407) % 2 ** 64
+    for it in range(passes):
+        x = draw(x)
+        key = [-start[n] - dur[n] for n in range(R)]
+        one = (x >> 40) % R
+        mid, wide, shake = key[one], NOM["wide"] * ((x >> 20) % 1024) / 1024, NOM["shake"] * ((x >> 30) % 1024) / 1024
+        near = [n for n in range(R) if mid - wide < key[n] < mid + wide]
+        if (x >> 56) % 3 == 0:
+            shake *= 0.5 if x >> 63 else -0.5
+            for n in near:
+                if part[n] == part[one]:
+                    key[n] += shake
+        else:
+            for n in near:
+                x = draw(x)
+                key[n] += shake * ((x >> 40) / 2 ** 24 - 0.5)
+        new, done = place(key, ahead, succs, zero) if back else place(key, behind, preds, tail)
+        v, order = judge(new, done, not back)
+        x = draw(x)
+        heat = NOM["warm"] * (NOM["cool"] / NOM["warm"]) ** (it / passes)
+        if v <= now - heat * math.log(((x >> 40) + 0.5) / 2 ** 24):
+            now, start, back = v, new, not back
+            if v < best[0]:
+                best = (v, order)
+    ORDER["passes"] = best[0]
+    return improve(ops, [n for j in best[1] for n in runs[j]])
 
 
 def gather_runs(ops, order):
@@ -300,111 +339,6 @@ def gather_runs(ops, order):
             if not miss[x]:
                 ready.append(x)
     return runs, queue, models, preds, succs, seq
-
-
-def improve(ops, order):
-    if not NOM["tries"]:
-        return order
-    runs, queue, models, preds, succs, seq = gather_runs(ops, order)
-    R = len(runs)
-
-    def times(seq, mark, state, goals, stop):
-        total, new = 0.0, []
-        for (dur, edges, tail), (fin, marks) in zip(models, state):
-            fin, marks = fin[:], marks[:mark + 1]
-            free = marks[mark][:]
-            for z0 in range(16 * mark, stop, 16):
-                if z0 > 16 * mark:
-                    marks.append(free[:])
-                for n in seq[z0:z0 + 16]:
-                    c = queue[n]
-                    t = free[c]
-                    for m, gap in edges[n]:
-                        x = fin[m] + gap
-                        if x > t:
-                            t = x
-                    t += dur[n]
-                    fin[n] = t
-                    if c != 5:
-                        free[c] = t
-            for w, group in goals:
-                total += w * max([fin[n] + tail[n] for n in group])
-            new.append((fin, marks))
-        return total / len(models), new
-
-    def blocked(seq, k, fin, n, since, stop):
-        dur, edges, tail = models[k]
-        before, ahead, pairs = [None] * 6, {}, []
-        for x in seq[:stop]:
-            ahead[x] = before[queue[x]]
-            before[queue[x]] = x
-        while n is not None and (fin[n] > since[k] or not pairs):
-            why = [m for m, gap in edges[n] if fin[m] + gap >= fin[n] - dur[n] - 1e-6]
-            if why:
-                n = why[0]
-            else:
-                if ahead[n] is not None and ahead[n] not in preds[n]:
-                    pairs.append((ahead[n], n))
-                n = ahead[n]
-        return pairs
-
-    x, since = NOM["seed"], [0.0] * len(models)
-    place = [0] * R
-    for share, named in STAGES:
-        goals = []
-        for w, names in named:
-            goals.append((w, [j for j, r in enumerate(runs) if (ops[r[0]]["q"],) + ops[r[0]]["tag"] in names] if names else
-                          [j for j in range(R) if not succs[j]]))
-        since = [s * share[1] for s in since]
-        for j, a in enumerate(seq):
-            place[a] = j
-        ends = [n for _, group in goals for n in group]
-        stop = max(place[n] for n in ends) + 1
-        now, state = times(seq, 0, [([0.0] * R, [[0.0] * 6]) for _ in models], goals, R)
-        best, pairs, tries = (now, seq, state), None, int(NOM["tries"] * share[0])
-        for it in range(tries):
-            x = (x * 6364136223846793005 + 1442695040888963407) % 2 ** 64
-            if not pairs or it % 16 == 0:
-                k = (x >> 60) % len(models)
-                group = goals[(x >> 50) % len(goals)][1]
-                fin, tail = state[k][0], models[k][2]
-                pairs = blocked(seq, k, fin, max(group, key=lambda n: fin[n] + tail[n]), since, stop)
-                if not pairs:
-                    continue
-            m, n = pairs[(x >> 33) % len(pairs)]
-            i, j = place[m], place[n]
-            if i > j:
-                continue
-            far, forward = (0, 0, 1, 2, 4, 8)[(x >> 20) % 6], (x >> 30) % 2
-            z = i if forward else j
-            while far and 0 < z < R - 1:
-                z += -1 if forward else 1
-                if queue[seq[z]] == queue[n]:
-                    far -= 1
-                    i, j = (z, j) if forward else (i, z)
-            part, move = seq[i:j + 1], {n if forward else m}
-            for a in (reversed(part) if forward else part):
-                if a in move:
-                    move.update([b for b in (preds if forward else succs)[a] if i <= place[b] <= j])
-            if m in move and n in move:
-                continue
-            new = seq[:i] + [a for a in part if (a in move) == bool(forward)] + [a for a in part if (a in move) != bool(forward)] + seq[j + 1:]
-            v, after = times(new, i // 16, state, goals, max(stop, j + 1))
-            heat = NOM["hot"] * share[2] * (NOM["cold"] / NOM["hot"]) ** (it / tries)
-            if v < now or (x >> 8) % 4096 < 4096 * math.exp((now - v) / heat):
-                now, seq, state = v, new, after
-                if it % 3 == 0:
-                    pairs = None
-                for z in range(i, j + 1):
-                    place[seq[z]] = z
-                if j + 1 >= stop:
-                    stop = max(place[n] for n in ends) + 1
-                if v < best[0]:
-                    best = (v, new, after)
-        seq = best[1]
-        since = [max(fin[n] for n in goals[0][1]) - NOM["back"] for fin, _ in best[2]]
-        ORDER.setdefault("stages", []).append(best[0])
-    return [n for j in seq for n in runs[j]]
 
 
 def improve(ops, order):
@@ -633,7 +567,7 @@ def rank_program(g, core, T, topo):
     cut = PAR["cut"]
     CH = [(0, cut, cut), (cut, L, LP)]
     KEEP, SPLIT, WIN = PAR["keep"], PAR["split"], PAR["win"]
-    kss = sorted(set([0] + [x[2] for row in PAR["pieces"] for x in row if x[2] < 16]))
+    kss = sorted(set([0] + [x[2] for row in PAR["pieces"] for x in row]))
     common = [x for x in topo.engines(cores[0], cores[1]) if all(x in topo.engines(a, b) for a in cores for b in cores if a != b)]
 
     def ap(a):
@@ -694,7 +628,7 @@ def rank_program(g, core, T, topo):
 
     def act(out, x, func=None, bias=None, scale=None):
         if bias is not None:
-            rec("s", "act", lambda e: e.activation(ap(out), ap(x), ACT.Identity, bias=ap(bias), scale=scale or 1.0), [out], [x, bias])
+            rec("s", "act", lambda e: e.activation(ap(out), ap(x), ACT.Identity, bias=ap(bias), scale=ap(scale or 1.0)), [out], [x, bias, scale])
         elif scale is not None:
             rec("s", "act", lambda e: e.activation(ap(out), ap(x), func or ACT.Identity, scale=ap(scale)), [out], [x, scale])
         else:
@@ -746,27 +680,28 @@ def rank_program(g, core, T, topo):
     dma("s", A("nbi", 0, W // 2), T.nb[:, 0:W // 2], NOM["nb"] - 1600)
     dma("y", A("nbi", W // 2, W), T.nb[:, W // 2:W], NOM["nb"] - NOM["issue"])
     dma("y", A("XT", 0, W), T.xs[:], NOM["xs"] - 2 * NOM["issue"])
-    cp(A("XT", W, B), A("XT", 0, B - W))
+    dma("y", A("XT", W, B), T.xs[:, 0:B - W], NOM["xs"] - 3 * NOM["issue"] + 200)
     iota(A("cI"), [[0, 8]], 0, 1, False)
     iota(A("row"), [[1, 160]], -16, 0)
     iota(A("R16"), [[16, 8], [0, 16]], 0, 0)
     iota(A("R32"), [[32, 4], [0, 32]], 0, 0)
-    iota(A("VT", 0, W // 2), [[1, W // 2]], -2047, 0)
+    iota(A("VT", 0, 512), [[1, 512]], -2047, 0)
+    for n in (512, 1024):
+        act(A("VT", n, 2 * n), A("VT", 0, n), bias=float(n))
     iota(A("RP"), [[1, 32], [0, 16]], 0, 0)
     iota(A("lanb"), [[32, 7], [0, 2]], -352, 0)
     iota(A("par"), [[0, 7], [1, 2]], 0, 0)
-    act(A("VT", W // 2, W), A("VT", 0, W // 2), bias=float(W // 2))
     dma("y", A("thi", p=G8), T.th[:], NOM["xs"] - 2 * NOM["issue"])
     dma("y", A("wti"), T.wt[:], NOM["xs"] - 2 * NOM["issue"])
-    for j, msk in ((0, 15), (1, 112), (2, 31), (4, 96), (5, 16), (6, 1), (7, 6)):
+    for j, msk in ((0, 15), (1, 112), (2, 31), (4, 96), (6, 1), (7, 6)):
         ts(A("cI", j, j + 1), A("cI", j, j + 1), msk, OP.bitwise_and)
     cp(A("cF", 0, 8), A("cI"))
     ms(A("one"), 1.0)
     ms(A("DC"), 0.0)
     ms(A("a1", L, LP), -1.0)
     for piece, value in ((A("cur"), L - 1023), (A("cz"), B - 1024 - 4096), (A("TT", W, B + 192), 0), (A("VT", W, B), 0), (A("mex"), 0),
-                         (A("snd", 0, 3 * U), 0), (A("omf", 78, 96), 0), (A("Z0"), 0), (A("Sx"), -1), (A("Sy"), 0), (A("Sm"), -8192),
-                         (A("Sf"), 8192), (A("td"), 0), (A("td", 6, 27, 9), 3 * 2 ** 22), (A("td", 7, 27, 9), -3 * 2 ** 22), (A("tq", 1, 2), 1),
+                         (A("snd", 0, 3 * U), 0), (A("omf", 78, 96), 0), (A("Z0"), 0), (A("Sy"), 0), (A("rst"), -1024),
+                         (A("own", L, LP), 0), (A("own", LP + L, 2 * LP), 0), (A("td"), 0), (A("td", 6, 27, 9), 3 * 2 ** 22), (A("td", 7, 27, 9), -3 * 2 ** 22), (A("tq", 1, 2), 1),
                          (A("bt", 16, 108, 36), 0), (A("bt", 4 * rank, 108, 36), 0), (A("bt", 20, 36), -2 ** 23), (A("bt", 56, 72), -2 ** 23),
                          (A("bt", 92, 108), -2 ** 23)):
         iota(piece, [[0, width(piece)]], value, 0)
@@ -777,25 +712,23 @@ def rank_program(g, core, T, topo):
     if WIN:
         cp(A("omf", 0, 78), A("odb"))
     ts(col(8), col(0), 1.0, OP.add, 2.0, OP.min)
-    ts(col(10), col(5), 0.0, OP.is_equal)
-    ts(col(11), col(5), 0.0, OP.is_gt)
-    ts(A("IW"), A("row"), col(3), OP.is_equal)
     ts(A("Ib"), A("row", 16, 144), col(3), OP.is_equal)
-    ts(A("Z1"), A("row", 1, 145), col(1), OP.is_equal)
-    ts(A("B1"), A("R16"), col(1), OP.is_equal)
+    ts(A("In"), A("row", 16, 144), col(3), OP.is_equal, -1.0, OP.mult)
+    for name, value in (("ZG", -32768.0), ("ZM", 65536.0)):
+        ts(A(name), A("row", 1, 145), col(1), OP.is_equal, value, OP.mult)
+    for name, value in (("Bn", -1.0), ("S2", 2.0)):
+        ts(A(name), A("R16", 0, 128, 16), col(1), OP.is_equal, value, OP.mult)
+    ts(A("BO", 0, 128), A("R16"), col(1), OP.is_equal, -32768.0, OP.mult)
     ts(A("O32"), A("R32"), col(4), OP.is_equal)
     ts(A("RP"), A("RP"), col(2), OP.is_equal)
-    ts(A("DK"), A("Ib"), col(0), OP.mult, 2048.0, OP.mult)
     ts(A("DP"), A("Ib"), col(8), OP.mult, float(2 ** 27), OP.mult)
     ts(A("Lt"), A("row", 16, 144), col(3), OP.is_gt)
     tt(A("Lt"), A("Lt"), A("O32"), OP.mult)
     for q in range(2):
         for g0 in range(2):
-            at = 16 + 16 * (q - g0)
-            act(A("LL", 128 * (2 * q + g0), 128 * (2 * q + g0 + 1)), A("IW", at, at + 128), scale=col(10 + q))
-    for name, src, sc in (("ZG", "Z1", -32768.0), ("ZM", "Z1", 65536.0), ("In", "Ib", -1.0), ("If", "Ib", 1.0), ("Bn", "B1", -1.0)):
-        act(A(name), A(src), scale=sc)
-    act(A("BO", 0, 128), A("B1"), scale=-32768.0)
+            pick(A("LL", 128 * (2 * q + g0), 128 * (2 * q + g0 + 1)), A("Z0"), [[-32, 4], [1000 - 2000 * g0, 2], [-1, 16]], OP.not_equal, 1.0,
+                 1000 * g0 - 16 * q, 1)
+    pick(A("If"), A("mex", 0, 128), [[1, 128]], OP.not_equal, 1.0, 0, -1)
     for j, k in enumerate(kss[1:]):
         pick(A("BO", 128 * j + 128, 128 * j + 256), A("BO", 0, 128), [[0, 8], [1, 16]], OP.is_ge, 0.0, -k, 0)
     for name, value in (("LZ", 4096.0), ("LW", -560.0)):
@@ -807,25 +740,40 @@ def rank_program(g, core, T, topo):
         ts(A("nr", l0 + lp + 15, 2 * lp, 16), A("lanb", l0 // 16, lp // 16), col(2), OP.add, float(B - 2047 + 352), OP.add)
     ts(A("mRG"), A("par"), col(6), OP.is_equal, 32768.0, OP.mult)
     ts(A("O3f"), A("R32"), 1.0 / 16, OP.mult, col(7), OP.is_equal)
-    cp(col(9), A("wti"))
+    ts(col(9), A("wti"), 1.0 / XS, OP.mult)
     cp(A("ytl", 64, 65, p=G8), A("thi", p=G8))
-    act(A("WZ"), A("Z1"), scale=col(9))
+    ts(A("WB"), A("R16"), col(1), OP.is_equal, col(9), OP.mult)
+    iota(A("MB"), [[0, 3], [1, 19]], 0, 0)
+    ts(A("MB"), A("MB"), col(0), OP.not_equal, float(2 ** 21), OP.mult)
+    pick(A("MB"), A("MB"), [[0, 3], [-1, 19]], OP.is_ge, float(2 ** 40), 15, 0)
+    iota(A("hd"), [[0, 171]], 0, 0)
+    iota(A("hd", 0, 171, 19), [[0, 9]], 2 ** 23, 0)
+    for at, value in ((17, 1.5 * 2 ** 34), (18, -1.5 * 2 ** 34)):
+        pick(A("hd", at, 171, 19), A("hd", at, 171, 19), [[0, 9]], OP.is_gt, value, 0, 0)
+    for j in range(3):
+        pick(A("hd", 57 * j + 16, 57 * j + 57, 19), A("hd", 57 * j + 16, 57 * j + 57, 19), [[0, 3]], OP.is_gt, 77 * (3 + j) - 1023.5, 0, 0)
+    iota(A("sne", 0, U), [[0, U]], 0, 0)
     act(A("ytl", 65, 67, p=G8), A("one", 0, 2, p=G8), scale=A("ytl", 64, 65, p=G8))
-    act(A("S2"), A("B1", 0, 128, 16), scale=2.0)
-    act(A("Iq"), A("Ib", 0, U), scale=0.25)
-    pick(A("Sx"), A("Sx"), [[-16, 8], [0, 17]], OP.is_ge, 0.0, 0, 1)
+    pick(A("Iq"), A("mex", 0, U), [[1, U]], OP.not_equal, 0.25, 0, -1)
+    pick(A("Sx"), A("Sy"), [[16, 8], [0, 17]], OP.is_gt, -1.0 / XS, 0, -1)
     pick(A("Sx"), A("Sx"), [[16, 8], [0, 17]], OP.is_ge, 0.0, 15, -1)
-    for out, src in ((A("Sx", 16, 136, 17), A("Sm")), (A("Sy", 16, 136, 17), A("Sm")), (A("Sf"), A("Sf"))):
-        pick(out, src, [[-16, 8]], OP.is_equal, 0.0, -15, 1)
+    for out, src, value in ((A("Sx", 16, 136, 17), "Z0", -1.0), (A("Sy", 16, 136, 17), "Z0", -1.0), (A("Sf"), "mex", 1.0)):
+        pick(out, A(src, 0, 8), [[-16, 8]], OP.not_equal, value / 32768, -15, 1)
     pick(A("r17"), A("mex", 0, 136), [[0, 8], [1, 17]], OP.not_equal, BIG, 0, 0)
-    pick(A("rst"), A("mex", 0, 128), [[0, 8], [1, 16]], OP.not_equal, BIG, 0, 0)
+    pick(A("rst"), A("rst"), [[0, 8], [1, 16]], OP.not_equal, BIG, 0, 0)
     ms(A("td", 5, 27, 9), -0.375)
     ms(A("tq", 0, 1), -0.25)
+    on_s = PAR["tts"]
+    iota(A("idf"), [[16, 32]], 0, 0)
+    ts(A("id16"), A("idf"), col(0), OP.add)
     for j in range(4):
         now[2] = "tt%d" % j
-        ts(A("TT", 512 * j, 512 * j + 512), A("nbi", 512 * j, 512 * j + 512), -2047.0, OP.add)
+        if j < 4 - on_s:
+            ts(A("TT", 512 * j, 512 * j + 512), A("nbi", 512 * j, 512 * j + 512), -2047.0, OP.add)
+        else:
+            act(A("TT", 512 * j, 512 * j + 512), IND(A("nbi", 512 * j, 512 * j + 512), A("id16")), bias=-2047.0)
     now[2] = "set"
-    act(A("thx", 0, 14, p=G8), A("mRG", p=G8), scale=A("ytl", 64, 65, p=G8))
+    act(A("thx", 0, 14, p=G8), A("mRG", p=G8), bias=-8192.0, scale=A("ytl", 64, 65, p=G8))
     mm(A("pg", 0, 14), A("O3f", p=G8), A("thx", 0, 14, p=G8), True)
     cp(A("thP"), A("pg", 0, 14))
     tabled = (0, 14, 26, 40, 52, 66, 78)
@@ -834,7 +782,7 @@ def rank_program(g, core, T, topo):
         act(A("VT", B + 16 * j0, B + 16 * j1), IND(A("VT", 0, W), A("od16", j0, j1)))
 
     def own_of(t, l0, l1):
-        return A("own", L * (t % 2) + l0, L * (t % 2) + l1)
+        return A("own", LP * (t % 2) + l0, LP * (t % 2) + l1) if t else A("XT", B + l0, B + l1)
 
     def flags(s, w0=0, wp=14):
         return A("fr", 14 * (s % 3) + w0, 14 * (s % 3) + wp)
@@ -842,49 +790,56 @@ def rank_program(g, core, T, topo):
     def guests_in(t):
         j = t - 3
         now[:] = [t, 0, "gh"]
-        gin, xb = A("gin%d" % j), A("xb", U * (j % 2), U * (j % 2) + U)
-        rec(None, "", None, [gin], [], ("ga%d" % j, len(common)), 0.0, [sent["g", j]])
-        mag = 1.5 * 2 ** 23
-        ts(xb, gin, mag, OP.add, -mag, OP.add)
-        for p in range(16):
-            mm(A("pg", 0, 3), A("WZ", 15 - p, 143 - p), A("xb", xb[2] + p, xb[3], 16), p == 0)
-        ts(A("hi", 0, 3), A("pg", 0, 3), float(77 * t), OP.add)
-        ts(A("ha", 0, 3), A("hi", 0, 3), 2047, OP.bitwise_and)
-        cp(A("h16", 0, 3), A("ha", 0, 3))
+        mag = 1.5 * 2 ** 23 * XS
+        mm(A("pg", 0, 57), A("Ib"), A("MB"), True)
+        for name, gin, xb in landed(j):
+            rec(None, "", None, [gin], [], ("ga" + name, len(common)), 0.0, [sent["g", name]])
+            ts(xb, gin, mag, OP.add, -mag, OP.add)
+            for u in range(3):
+                mm(A("pg", 19 * u, 19 * u + 16), A("WB"), A("xb", xb[2] + 16 * u, xb[2] + 16 * u + 16))
+        scan(A("hs"), A("hd", 57 * j, 57 * j + 57), A("pg", 0, 57), OP.add, OP.min)
+        tt(A("hf", 0, 3), A("hs", 16, 57, 19), A("hs", 18, 57, 19), OP.subtract)
+        ts(A("h16", 0, 3), A("hf", 0, 3), 1023.5, OP.add)
         ts(A("g16"), IND(A("TO%d" % j) if t in KEEP else A("TT", 0, W), A("h16", 0, 3)), 2047.0, OP.add)
+
+    def landed(j):
+        late = (str(j), A("gin%d" % j), A("xb", U * (j % 2), U * (j % 2) + U))
+        return [("e", A("gine"), A("xb", 2 * U, 3 * U)), late] if j + 2 in PAR["early"] else [late]
 
     def guests_judged(t):
         j = t - 3
-        xb = A("xb", U * (j % 2), U * (j % 2) + U)
         now[:] = [t, 0, "gM"]
-        mm(A("pq", 128, 256, p=(0, U, 1)), xb, A("Ib"), True)
-        act(A("xT", p=(0, U, 1)), A("pq", 128, 256, p=(0, U, 1)))
-        h = PAR["gv"][j]
+        for n, (_, gin, xb) in enumerate(landed(j)):
+            mm(A("pq", 128, 256, p=(0, U, 1)), xb, A("Ib"), n == 0)
+        act(A("xT", p=(0, U, 1)), A("pq", 128, 256, p=(0, U, 1)), scale=1.0 / XS)
         now[2] = "gG"
-        if h:
-            cp(A("Gg", 0, 16 * h), IND(A("XT", 0, W), A("g16", 0, h)))
-        act(A("Gg", 16 * h, 16 * U), IND(A("XT", 0, W), A("g16", h, U)))
-        slots48, by_max = (0, U, 1), PAR["guests"][j] == "v"
-
-        def brought():
-            now[2] = "g0"
-            mm(A("pg", 0, 136, p=slots48), xb, A("Sx" if by_max else "Sy"), True)
-            mm(A("pg", 16, 136, 17, slots48), A("gin%d" % j), A("Sf"))
-        parts = [(A("pg", 256, 512), 32, U), (A("pq"), 0, 32)]
-        for cell, a, b in parts:
+        for who, a, b in PAR["gv"][j]:
+            (cp if who == "v" else act)(A("Gg", 16 * a, 16 * b), IND(A("XT", 0, W), A("g16", a, b)))
+        slots48 = (0, U, 1)
+        parts = [(A("pg", 256, 512), 32, U, PAR["guests"][j][1] == "v"), (A("pq"), 0, 32, PAR["guests"][j][0] == "v")]
+        for cell, a, b, by_max in parts:
             now[2] = "gR"
             mm(cell, A("xT", p=(a, b, 1)), A("RP", 0, 16 * (b - a), p=(a, b, 1)), True)
             now[2] = "gM"
             if not by_max:
                 mm(cell, A("In"), A("Gg", 16 * a, 16 * b))
                 act(A("Ag", 16 * a, 16 * b), cell, ACT.Abs, None, 0.5)
-        brought()
+        alike = parts[0][3] == parts[1][3]
+        sums = [(0, U, parts[0][3])] if alike else [x[1:] for x in parts]
+        now[2] = "g0"
+        mm(A("pg", 0, 136, p=slots48), A("Z0", 0, U), A("Sy"), True)
+        for _, gin, xb in landed(j):
+            for a, b, by_max in sums:
+                mm(A("pg", 0, 136, p=(a, b, 1)), A("xb", xb[2] + a, xb[2] + b), A("Sx" if by_max else "Sy"))
+            mm(A("pg", 16, 136, 17, slots48), gin, A("Sf"))
         now[2] = "gM"
-        for cell, a, b in parts if by_max else ():
-            tt(A("Ag", 16 * a, 16 * b), A("Gg", 16 * a, 16 * b), cell, OP.max)
+        for cell, a, b, by_max in parts:
+            if by_max:
+                tt(A("Ag", 16 * a, 16 * b), A("Gg", 16 * a, 16 * b), cell, OP.max)
         now[2] = "gs"
-        for k in range(16 if by_max else 0):
-            mm(A("pg", k, 136, 17, slots48), A("Gg", k, 16 * U, 16), A("Bn", 0, 128, 16))
+        for a, b, by_max in sums:
+            for k in range(16 if by_max else 0):
+                mm(A("pg", k, 136, 17, (a, b, 1)), A("Gg", 16 * a + k, 16 * b, 16), A("Bn"))
         now[2] = "gj"
         for k in range(16):
             mm(A("pg", k, 136, 17, slots48), A("Ag", k, 16 * U, 16), A("S2"))
@@ -903,7 +858,8 @@ def rank_program(g, core, T, topo):
                 trs.append(RemoteDMATransfer(dst_ids=[DstId(rid=rid, pnc=pid)], dma_engine_mask=msk, remote_sem=T.sem["ba%d" % j],
                                              src=ap(mine), dst=ap(mine)))
             return e.remote_dma_fused(trs, local_sem=T.sem["left%d" % (3 + j)])
-        sent["b", j] = rec("g", "", send, [], [mine], ("left%d" % (3 + j), sum(n for _, n in masks.values())), NOM["rem"])
+        sent["b", j] = rec("g", "", send, [], [mine], ("left%d" % (3 + j), sum(n for _, n in masks.values())), NOM["rem"] - NOM["call"])
+        ops[-1]["dur"] = NOM["call"]
 
     def threshold(t):
         j = t - 3
@@ -913,17 +869,26 @@ def rank_program(g, core, T, topo):
         rec(None, "", None, [A("bt", 36 * j + 4 * r, 36 * j + 4 * r + 1) for r in range(NR) if r != rank], [], ("ba%d" % j, n), 0.0, [sent["b", j]])
         scan(A("ytl", t, 65 + t, 8, G8), A("td", 9 * j, 9 * j + 9, p=G8), A("bt", 36 * j, 36 * j + 36, 4, G8), OP.add, OP.max)
         if t == 3:
-            ts(A("thx", 14, 28, p=G8), A("mRG", p=G8), A("ytl", 64 + t, 65 + t, p=G8), OP.mult)
+            ts(A("thx", 14, 28, p=G8), A("mRG", p=G8), A("ytl", 64 + t, 65 + t, p=G8), OP.mult, -8192.0, OP.add)
 
-    def floor_m(scale, l0, lp):
-        ts(A("mi", l0 // 16, lp // 16), A("mn", l0 // 16, lp // 16), 2.0 ** -15, OP.mult, -0.46875, OP.add)
-        ts(A("mex", l0 + 15, lp, 16), A("mi", l0 // 16, lp // 16), 4095.0, OP.min, scale, OP.mult)
-        tr(A("mC", l0, lp), A("mex", l0, lp))
+    def leavers(t, name, src, s0, first):
+        dst = cores[(rank + 1 + t % (NR - 1)) % NR]
+
+        def send(e):
+            rid, pid = topo.addr(dst, core)
+            return e.remote_dma(ap(A("gin" + name)), ap(A(src, s0, s0 + U)), T.sem["ga" + name], T.sem["lf" + name], pid, rid,
+                                sum(1 << x for x in common))
+        sent["g", name] = rec("g", "", send, [], [A(src, s0, s0 + U)], ("lf" + name, len(common)), NOM["rem"] - NOM["call"])
+        ops[-1]["dur"] = NOM["call"] + (NOM["first"] if first else 0.0)
 
     def pack(t, l0, l1, lp):
-        floor_m(2.0 ** -13, l0, lp)
-        s0 = U * (4 - t)
-        tt(IND(A("snd", s0, s0 + 432), A("s16", l0 // 16, l1 // 16)), A("mC", l0, l1), A("ownf", L * (t % 2) + l0, L * (t % 2) + l1), OP.add)
+        mag = 1.5 * 2 ** 38
+        ts(A("mex", l0 + 15, lp, 16), A("mn", l0 // 16, lp // 16), mag, OP.add, -mag, OP.add)
+        tr(A("mC", l0, lp), A("mex", l0, lp))
+        src, s0 = ("sne", 0) if t in PAR["early"] and l0 == 0 else ("snd", U * (4 - t))
+        tt(IND(A(src, s0, s0 + 432), A("s16", l0 // 16, l1 // 16)), A("mC", l0, l1), A("ownf", L * (t % 2) + l0, L * (t % 2) + l1), OP.add)
+        if src == "sne":
+            leavers(t, "e", src, s0, t == 2)
 
     def columns(t, l0, l1):
         return IND(A("TT", 0, B + 240 if t - 1 in WIN else B + L * (t + 1)), A3("L16", 0, None, l0 // 16, l1 // 16))
@@ -941,7 +906,10 @@ def rank_program(g, core, T, topo):
         else:
             ts(c16, columns(t, l0, l1), 2047.0, OP.add)
         now[2] = "own"
-        act(own, IND(A("XT", 0, B + L * (t + 1)), entries(l0, l1)) if t else IND(A("XT", 0, W), A("od16", l0 // 16, l1 // 16)))
+        if t:
+            act(own, IND(A("XT", 0, B + L * (t + 1)), entries(l0, l1)))
+        else:
+            act(own_of(t, l0, lp), IND(A("XT", 0, W), A("od16", l0 // 16, lp // 16)))
         now[2] = "oT"
         mm(A("po%d" % c, 0, l1 - l0), A("Ib"), own, True)
         if t not in PAR["whole"]:
@@ -999,16 +967,16 @@ def rank_program(g, core, T, topo):
             mm(mk, A("IB"), flags(t - 1, w0, wp))
         if t in (2, 3):
             bar(t, c, pk)
+        ends = [0] + [x[0] for x in PAR["pieces"][t]]
+        mine = [(j, ends[j], b, who, ks) for j, (b, who, ks) in enumerate(PAR["pieces"][t]) if b0 <= ends[j] < b1]
+        wide = len(mine) > 1 and t in PAR["wide"]
         now[2] = "ini"
-        mm(A(pk, 0, bp - b0), A("DK"), A("one", 0, bp - b0), True)
+        ks = mine[0][4]
+        mm(A(pk, 0, bp - b0), A("BO", 128 * kss.index(ks), 128 * kss.index(ks) + 128), own_of(t, b0, bp), True)
         now[2] = "pen"
         mm(A(pk, 0, bp - b0), A("DP"), A("a1", b0, bp))
-        ends = [0] + [x[0] for x in PAR["pieces"][t]]
         turn = 0
-        for j, (b, who, ks) in enumerate(PAR["pieces"][t]):
-            a = ends[j]
-            if not b0 <= a < b1:
-                continue
+        for j, a, b, who, ks in mine:
             now[2] = "G%d" % j
             if who:
                 cp(A("G", 16 * a, 16 * (a + who)), IND(A("XT", 0, B), A("c16", a, a + who)))
@@ -1029,14 +997,15 @@ def rank_program(g, core, T, topo):
                 now[2] = "SA%d" % j
                 for k in range(k0, k1):
                     mm(key, A("ZM", 15 - k, 143 - k), A("M", 16 * a + n * k, 16 * a + n * (k + 1)))
-            if ks == 16:
-                continue
             now[2] = "SG%d" % j
-            mm(key, A("BO", 128 * kss.index(ks), 128 * kss.index(ks) + 128), own_of(t, a, b))
             for k in range(ks, 16):
                 mm(key, A("ZG", 15 - k, 143 - k), A("G", 16 * a + k, 16 * b, 16))
+            if wide:
+                if b < b1:
+                    continue
+                a, n, key = b0, b1 - b0, A(pk, 0, b1 - b0)
             for k in range(ks, 16):
-                piece = A("M", 16 * a + n * k, 16 * a + n * (k + 1))
+                piece = A("Mw", n * k, n * (k + 1)) if wide else A("M", 16 * a + n * k, 16 * a + n * (k + 1))
                 now[2] = "M%d" % j
                 tt(piece, A("G", 16 * a + k, 16 * b, 16), A(po, a - b0, b - b0), OP.max)
                 now[2] = "SM%d" % j
@@ -1055,7 +1024,7 @@ def rank_program(g, core, T, topo):
         now[:] = [t, 1, "ownf"]
         hi = B + L * (t + 1)
         if 2 <= t <= 4:
-            act(A("ownf", L * (t % 2), L * (t % 2) + L), own_of(t, 0, L))
+            act(A("ownf", L * (t % 2), L * (t % 2) + L), own_of(t, 0, L), scale=XS)
         now[2] = "wr"
         if t < 5:
             for l0, l1 in ((0, cut), (cut, L)) if t in PAR["wr2"] else ((0, L),):
@@ -1072,7 +1041,7 @@ def rank_program(g, core, T, topo):
             else:
                 act(A("TT", B + 192, hi + L), IND(A("TT", 0, W), A("om16", 12, 13 * (t + 2))), bias=1.0)
             now[2] = "tab"
-            j0, j1 = tabled[t + 1] if t else 0, tabled[t + 2]
+            j0, j1 = tabled[t + 1], tabled[t + 2]
             act(A("XT", B + 16 * j0, B + 16 * j1), IND(A("XT", 0, W), A("od16", j0, j1)))
 
     def slots(c, w0, wp):
@@ -1182,17 +1151,9 @@ def rank_program(g, core, T, topo):
             cp(A("ow16"), IND(A("omf"), A("w16", 0, 1)))
         now[2] = "pack"
         if t >= 2:
-            j = t - 2
             if t not in SPLIT:
                 pack(t, 0, L, LP)
-            s0 = U * (2 - j)
-            dst = cores[(rank + 1 + t % (NR - 1)) % NR]
-
-            def send(e):
-                rid, pid = topo.addr(dst, core)
-                return e.remote_dma(ap(A("gin%d" % j)), ap(A("snd", s0, s0 + U)), T.sem["ga%d" % j], T.sem["left%d" % j], pid, rid,
-                                    sum(1 << x for x in common))
-            sent["g", j] = rec("g", "", send, [], [A("snd", s0, s0 + U)], ("left%d" % j, len(common)), NOM["rem"] + (NOM["first"] if j == 0 else 0.0))
+            leavers(t, str(t - 2), "snd", U * (4 - t), t == 2 and t not in PAR["early"])
 
     def guests(t):
         if t < 5:
@@ -1237,6 +1198,8 @@ def rank_program(g, core, T, topo):
     dma("y", T.yv[:], A("vf", p=(0, 128, 16)))
     for c in range(2):
         back(5, c)
-    floor_m(1.0, 0, LP)
+    ts(A("mi"), A("mn"), 2.0 ** -15, OP.mult)
+    ts(A("mex", 15, LP, 16), A("mi"), 4095.0, OP.min)
+    tr(A("mC"), A("mex"))
     dma("s", T.ym[:], A("mC", 0, L, p=(15, 128, 16)))
     emit(g, T, ops)

import math
import numpy as np
from concourse.bass import DstId, RemoteDMATransfer
from concourse.mybir import AluOpType, AxisListType, ActivationFunctionType

W, L, U, NT, Q, KN = 2048, 208, 48, 6, 1248, 768
B = 2064
LP = 224
H = "float16"
BIG = float(2 ** 30)
XS = float(2 ** 29)
G8 = (0, 8, 1)
PAR = {
    "cut": 128,
    "pieces": [[(64, who, 8), (128, 0, 8), (208, 0, 6)] for who in (64, 48, 32, 0, 0, 0)],
    "guests": ["vv", "ss", "vv"], "gv": [[("v", 0, 24), ("s", 24, U)], [("s", 0, U)], [("v", 0, 24), ("s", 24, U)]],
    "early": [],
    "keep": [3, 4],
    "split": [2, 4],
    "ring": [2, 2, 2, 1, 1, 1],
    "win": [2, 3, 4],
    "whole": [0, 1, 2, 3, 4, 5],
    "tts": 1, "wide": [], "wr2": [], "vb": "pr0",
}
NOM = {"cyc": 0.83, "gat": 1.56, "sca": 3.8, "vfix": 20.0, "sfix": 50.0, "pe": 0.42, "sem": 130.0, "pel": 60.0, "self": 110.0, "rem": 3300.0,
       "call": 800.0, "first": 1200.0, "issue": 1000.0, "far": 1.0, "nb": 5500.0, "xs": 7200.0, "copy": 6000.0,
       "seed": 3, "passes": 25000, "weights": (1.0, 0.0, 0.0, 0.0), "wide": 1800.0, "shake": 4000.0, "warm": 150.0, "cool": 10.0,
       "tries": 150000, "hot": 60.0, "cold": 10.0, "span": 80, "hop": 32, "sweeps": 20, "soft": 0.08, "alone": 0.0, "run": 3}
VARIANTS = [{"vfix": 30.0, "sfix": 75.0, "sem": 140.0, "self": 120.0, "pel": 70.0, "cyc": 1.03, "pe": 0.52, "far": 0.8},
            {"vfix": 26.0, "sfix": 60.0, "cyc": 0.9, "pe": 0.46, "far": 0.72},
            {"vfix": 33.0, "sfix": 90.0, "sem": 150.0, "self": 125.0, "pel": 75.0, "cyc": 1.2, "pe": 0.61, "gat": 1.95, "sca": 4.5, "far": 0.9},
            {"vfix": 33.0, "sfix": 80.0, "sem": 150.0, "self": 125.0, "pel": 75.0, "cyc": 1.15, "pe": 0.58, "gat": 1.2, "sca": 4.5, "far": 0.85}]
ORDER = {}
F, BF, I, U16 = "float32", "bfloat16", "int32", "uint16"


def _sb(n, d, k=None):
    return ("sbuf", [128, n] if k is None else [128, n, k], d)


def _ps():
    return ("psum", [128, 512], F)


SCRATCH = {
    "nbi": _sb(W, I), "TT": _sb(B + Q, F), "XT": _sb(B + Q, BF), "VT": _sb(B + Q, F),
    "TO0": _sb(W, F), "TO1": _sb(W, F), "odi": _sb(78, I), "oda": _sb(78, I), "odb": _sb(78, I), "od16": _sb(78, U16), "om16": _sb(78, U16),
    "G": _sb(16 * L, BF), "M": _sb(16 * L, BF), "Mw": _sb(2048, BF), "Gg": _sb(16 * U, BF), "Ag": _sb(16 * U, BF),
    "own": _sb(2 * LP, BF), "xT": _sb(128, BF), "Z0": _sb(128, BF), "RP": _sb(512, BF), "ownf": _sb(2 * L, F), "c16": _sb(L, U16),
    "cr": _sb(L, H), "fl": _sb(L, H), "DC": _sb(2 * LP, H), "DT": _sb(2 * LP, H), "a1": _sb(LP, BF),
    "ks": _sb(2 * LP, F), "ne": _sb(LP, BF), "nr": _sb(2 * LP, H), "mex": _sb(LP, F), "mC": _sb(LP, F),
    "base": _sb(14, H), "w16": _sb(2, U16), "ow16": _sb(16, U16), "omf": _sb(96, F),
    "dead": _sb(14, BF), "go": _sb(14, BF), "fr": _sb(42, BF),
    "L16": _sb(2, U16, 14), "slt": _sb(14, H), "s16": _sb(14, U16), "v16": _sb(14, U16),
    "mn": _sb(14, F), "mi": _sb(14, I), "thP": _sb(14, F), "thx": _sb(28, F), "cur": _sb(14, H), "cz": _sb(16, H),
    "row": _sb(160, BF), "cI": _sb(8, I), "cF": _sb(12, F), "R16": _sb(128, BF), "R32": _sb(128, BF),
    "lanb": _sb(14, F), "par": _sb(14, F), "lanc": _sb(14, F), "mRG": _sb(14, F),
    "Sx": _sb(136, BF), "Sy": _sb(136, BF), "Sf": _sb(8, F), "S2": _sb(8, BF), "Iq": _sb(U, F), "r17": _sb(136, F),
    "td": _sb(27, F), "tq": _sb(2, F), "ZM": _sb(144, BF), "ZG": _sb(144, BF),
    "Bn": _sb(8, BF), "Ib": _sb(128, BF), "In": _sb(128, BF), "If": _sb(128, F), "BO": _sb(128 * 8, BF),
    "DP": _sb(128, BF), "O32": _sb(128, BF), "O3f": _sb(128, F), "Lt": _sb(128, BF), "LZ": _sb(128, BF), "LW": _sb(128, BF),
    "ID": _sb(128, BF), "IB": _sb(128, BF), "LL": _sb(512, BF),
    "one": _sb(LP, BF), "rst": _sb(128, F),
    "wti": _sb(1, I), "thi": _sb(1, I), "ytl": _sb(72, F),
    "snd": _sb(528, F), "gin0": _sb(U, F), "gin1": _sb(U, F), "gin2": _sb(U, F),
    "idf": _sb(32, F), "id16": _sb(32, U16), "sne": _sb(432, F), "gine": _sb(U, F), "WB": _sb(128, BF), "MB": _sb(57, BF), "hd": _sb(171, F), "hs": _sb(57, F), "hf": _sb(4, F),
    "xb": _sb(3 * U, BF), "h16": _sb(4, U16), "g16": _sb(U, U16), "js": _sb(136, F), "jC": _sb(U, F),
    "bt": _sb(108, F), "vf": _sb(L, F), "yno": _sb(B + Q, F), "cf": _sb(L, F),
    "pk0": _ps(), "pk1": _ps(), "po0": _ps(), "po1": _ps(), "pr0": _ps(), "pr1": _ps(), "pq": _ps(), "pg": _ps(),
}
NDMA = 19
SEMAPHORES = (["qv", "qs", "qt", "qg", "ga0", "ga1", "ga2", "gae", "ba0", "ba1", "ba2", "lf0", "lf1", "lf2", "lfe", "left3", "left4", "left5"]
              + ["d%d" % j for j in range(NDMA)])
OP = AluOpType
ACT = ActivationFunctionType


def A(name, c0=0, c1=None, st=1, p=None):
    return ("a", name, c0, SCRATCH[name][1][1] if c1 is None else c1, st, p)


def A3(name, a0, a1, k0, k1=None):
    return ("b", name, a0, a1, k0, k1)


def IND(win, off):
    return ("i", win, off)


def width(a):
    if a[0] == "i":
        return 16 * width(a[2])
    if a[0] == "b":
        return (1 if a[3] is None else a[3] - a[2]) * (1 if a[5] is None else a[5] - a[4])
    return (a[3] - a[2] + a[4] - 1) // a[4]


def extent(a):
    if a[0] == "b":
        return (a[1], a[2], a[2] + 1 if a[3] is None else a[3], 1, a[4], a[4] + 1 if a[5] is None else a[5])
    return (a[1], a[2], a[3], a[4], 0, 1)


def duration(kind, outs, ins):
    full = [a for a in outs + ins if isinstance(a, tuple)]
    if kind == "mm":
        return max(min(64, width(ins[0])), width(ins[1])) * NOM["pe"] * (4 if SCRATCH[ins[1][1]][2] == F else 1)
    if kind in ("iota", "pick"):
        return (130 if kind == "iota" else 170) + 2 * NOM["cyc"] * width(outs[0])
    ind = [a for a in full if a[0] == "i"]
    if ind:
        return 60 + width(ind[0]) * NOM["cyc"] * (NOM["sca"] if ind[0] is outs[0] else NOM["gat"])
    n = max(width(a) for a in full)
    c = 1.0
    if kind == "tt":
        c = 1.0 if any(SCRATCH[a[1]][0] == "psum" for a in ins) else 2.0
    elif kind not in ("act", "red") and all(SCRATCH[a[1]][2] in (BF, H, U16) for a in full if width(a) == n):
        c = 0.5
    return max(64, n * c) * NOM["cyc"] + NOM["sfix" if kind == "act" else "vfix"]


def best_masks(src, cores, topo):
    peers = sorted([c for c in cores if c != src], key=lambda c: len(topo.engines(src, c)))
    used, out = [], {}
    for c in peers:
        have = [e for e in topo.engines(src, c) if e not in used]
        alike = [d for d in peers if d not in out and topo.mask(src, d) == topo.mask(src, c)]
        n = 1
        while 2 * n <= len(have) // len(alike) and not (out and n >= max(x for _, x in out.values())):
            n *= 2
        used += have[:n]
        out[c] = (sum(1 << e for e in have[:n]), n)
    return out


def plan(ops):
    seen, lines = {}, {}
    for n, o in enumerate(ops):
        deps, after = set(o["more"]), set()
        for (name, c0, c1, st, k0, k1, wr) in o["acc"]:
            ps = SCRATCH[name][0] == "psum"
            for (m, d0, d1, ds, j0, j1, dw) in seen.get(name, []):
                if m == n:
                    continue
                same = ops[m]["q"] == o["q"] and ops[m]["tok"] is None and o["tok"] is None
                over = d0 < c1 and c0 < d1 and j0 < k1 and k0 < j1 and not (st == ds and (c0 - d0) % st)
                if same and o["q"] == "t":
                    if ps and (o["edge"] or ops[m]["edge"]):
                        after.add(m)
                elif (ps and not same) or (over and (dw or wr)):
                    deps.add(m)
            seen.setdefault(name, []).append((n, c0, c1, st, k0, k1, wr))
        if o["line"] is not None:
            if o["line"] in lines:
                after.add(lines[o["line"]])
            lines[o["line"]] = n
        done, ahead, kept, near = 0, 0, set(), set()
        for m in sorted(after, reverse=True):
            if not ahead >> m & 1:
                near.add(m)
                done |= ops[m]["done"]
                ahead |= ops[m]["ahead"] | 1 << m
        for m in sorted(deps, reverse=True):
            if not done >> m & 1:
                kept.add(m)
                done |= ops[m]["done"] | (0 if ops[m]["tok"] else ops[m]["ahead"]) | 1 << m
        if o["q"] is None:
            done, ahead = 0, 0
        o["done"], o["ahead"] = done, ahead
        o["deps"], o["after"] = kept, near - kept
    if len(ops) not in ORDER:
        ORDER[len(ops)] = schedule(ops)
    return ORDER[len(ops)]


def schedule(ops):
    runs, queue, models, preds, succs, seq = gather_runs(ops, list(range(len(ops))))
    R, (dur, edges, tail) = len(runs), models[0]
    ahead = [[(m, gap + dur[m]) for m, gap in e] for e in edges]
    behind = [[] for _ in runs]
    for n in range(R):
        for m, gap in edges[n]:
            behind[m].append((n, gap + dur[n]))
    part = [(ops[r[0]]["tag"][:2], ops[r[0]]["tag"][2][0] == "g") for r in runs]

    def place(key, need, frees, first):
        miss = [len(e) for e in need]
        start, busy, done, ready, passed = [0.0] * R, [([], []) for _ in range(6)], [], [], [False] * R
        for n in np.argsort(key, kind="stable").tolist():
            passed[n] = True
            if miss[n]:
                continue
            while True:
                t, d, c = first[n], dur[n], queue[n]
                for m, gap in need[n]:
                    y = start[m] + gap
                    if y > t:
                        t = y
                if c != 5:
                    begins, ends = busy[c]
                    j = size = len(ends)
                    while j and ends[j - 1] > t:
                        j -= 1
                    while j < size and begins[j] < t + d:
                        t = ends[j]
                        j += 1
                    begins.insert(j, t)
                    ends.insert(j, t + d)
                start[n] = t
                done.append(n)
                for s in frees[n]:
                    miss[s] -= 1
                    if not miss[s] and passed[s]:
                        ready.append(s)
                if not ready:
                    break
                n = min(ready, key=lambda x: key[x])
                ready.remove(n)
        return start, done

    def judge(start, done, back):
        at = [-start[n] - dur[n] for n in range(R)] if back else start[:]
        done = done[::-1] if back else done
        for n in done:
            for m in preds[n]:
                if at[m] > at[n]:
                    at[n] = at[m]
        order, total = [done[j] for j in np.argsort([at[n] for n in done], kind="stable").tolist()], 0.0
        for (dk, ek, tk), weight in zip(models, NOM["weights"]):
            if not weight:
                continue
            fin, free, end = [0.0] * R, [0.0] * 6, 0.0
            for n in order:
                c = queue[n]
                t = free[c]
                for m, gap in ek[n]:
                    y = fin[m] + gap
                    if y > t:
                        t = y
                t += dk[n]
                fin[n] = t
                if c != 5:
                    free[c] = t
                t += tk[n]
                if t > end:
                    end = t
            total += weight * end
        return total, order

    zero, rest = [0.0] * R, [0.0] * R
    for n in reversed(seq):
        rest[n] = dur[n] + max([tail[n]] + [rest[s] + gap - dur[s] for s, gap in behind[n]])
    start, done = place([-y for y in rest], ahead, succs, zero)
    now, order = judge(start, done, False)
    best, back, x, passes = (now, order), False, NOM["seed"], NOM["passes"]

    def draw(x):
        return (x * 6364136223846793005 + 1442695040888963407) % 2 ** 64
    for it in range(passes):
        x = draw(x)
        key = [-start[n] - dur[n] for n in range(R)]
        one = (x >> 40) % R
        mid, wide, shake = key[one], NOM["wide"] * ((x >> 20) % 1024) / 1024, NOM["shake"] * ((x >> 30) % 1024) / 1024
        near = [n for n in range(R) if mid - wide < key[n] < mid + wide]
        if (x >> 56) % 3 == 0:
            shake *= 0.5 if x >> 63 else -0.5
            for n in near:
                if part[n] == part[one]:
                    key[n] += shake
        else:
            for n in near:
                x = draw(x)
                key[n] += shake * ((x >> 40) / 2 ** 24 - 0.5)
        new, done = place(key, ahead, succs, zero) if back else place(key, behind, preds, tail)
        v, order = judge(new, done, not back)
        x = draw(x)
        heat = NOM["warm"] * (NOM["cool"] / NOM["warm"]) ** (it / passes)
        if v <= now - heat * math.log(((x >> 40) + 0.5) / 2 ** 24):
            now, start, back = v, new, not back
            if v < best[0]:
                best = (v, order)
    ORDER["passes"] = best[0]
    return improve(ops, [n for j in best[1] for n in runs[j]])


def gather_runs(ops, order):
    of, runs, last, open_ = [0] * len(ops), [], None, {}
    for n, o in enumerate(ops):
        name, into = o["tag"][2], None
        if (o["q"] == "v" and name[0] == "M") or (o["q"] == "t" and name[:2] == "SM"):
            key = (o["q"], o["tag"])
            if key in open_ and len(runs[open_[key]]) < NOM["run"]:
                into = open_[key]
            else:
                open_[key] = len(runs)
        elif o["q"] == "t":
            if last is not None and ops[last]["tag"] == o["tag"] and not any(ops[m]["q"] in ("v", "s") and m > runs[of[last]][0] for m in o["deps"]):
                into = of[last]
            last = n
        if into is None:
            into = len(runs)
            runs.append([])
        of[n] = into
        runs[into].append(n)
    R = len(runs)
    queue = ["vstgy-".index(ops[r[0]]["q"] or "-") for r in runs]
    models, keep = [], dict(NOM)
    for change in VARIANTS:
        NOM.update(change)
        dur = [o["dur"] if o["tok"] else duration(*o["spec"]) for o in ops]
        lat = [NOM["pel"] if o["q"] == "t" else o["lat"] * NOM["far"] for o in ops]
        edges = []
        for j, r in enumerate(runs):
            e, off = {}, 0.0
            for n in r:
                for m in ops[n]["deps"] | ops[n]["after"]:
                    if of[m] != j:
                        gap = 0.0 if m not in ops[n]["deps"] else lat[m] + NOM["self" if ops[m]["q"] == ops[n]["q"] else "sem"]
                        gap -= off + sum(dur[x] for x in runs[of[m]][runs[of[m]].index(m) + 1:])
                        e[of[m]] = max(e.get(of[m], -1e18), gap)
                off += dur[n]
            edges.append(sorted(e.items()))
        models.append(([sum(dur[n] for n in r) for r in runs], edges, [lat[r[-1]] for r in runs]))
        NOM.update(keep)
    preds, succs = [[m for m, _ in e] for e in models[0][1]], [[] for _ in runs]
    for j in range(R):
        for m in preds[j]:
            succs[m].append(j)
    first, miss, seq = {}, [len(p) for p in preds], []
    for j, n in enumerate(order):
        first.setdefault(of[n], j)
    ready = [j for j in range(R) if not miss[j]]
    while ready:
        j = min(ready, key=lambda x: first[x])
        ready.remove(j)
        seq.append(j)
        for x in succs[j]:
            miss[x] -= 1
            if not miss[x]:
                ready.append(x)
    return runs, queue, models, preds, succs, seq


def improve(ops, order):
    if not NOM["tries"]:
        return order
    runs, queue, every, preds, succs, seq = gather_runs(ops, order)
    R, span, hop, sweeps, soft = len(runs), NOM["span"], NOM["hop"], NOM["sweeps"], NOM["soft"]
    onward = []
    for dur, edges, tail in every:
        e = [[] for _ in range(R)]
        for n in range(R):
            for m, gap in edges[n]:
                e[m].append((n, gap))
        onward.append(e)
    starts = list(range(0, max(1, R - span + hop), hop))
    tries = NOM["tries"] // (sweeps * len(starts))
    x, place, best = NOM["seed"], [0] * R, None

    def times(win, mark, state, limit):
        total, new = 0.0, []
        for k in range(K):
            dur, edges, out, outq = models[k][0], models[k][1], exits[k], exitq[k]
            fin, marks = state[k][0][:], state[k][1][:mark + 1]
            free, end, last = marks[mark]
            free = free[:]
            for z0 in range(8 * mark, len(win), 8):
                if z0 > 8 * mark:
                    marks.append((free[:], end, last))
                for n in win[z0:z0 + 8]:
                    c = queue[n]
                    t = free[c]
                    for m, gap in edges[n]:
                        y = fin[m] + gap
                        if y > t:
                            t = y
                    t += dur[n]
                    fin[n] = t
                    if c != 5:
                        free[c] = t
                    t += out[n]
                    if t > end:
                        end, last = t, n
                if k == K - 1 and total + end > limit:
                    return 1e18, None
            for c in range(3):
                t = free[c] + outq[c]
                total += soft * t
                if t > end:
                    end, last = t, -1 - c
            total += end
            new.append((fin, marks, end, last))
        return total, new

    def blocked(win, k, fin, n):
        dur, edges = models[k][0], models[k][1]
        before, ahead, pairs = [None] * 6, {}, []
        for a in win:
            ahead[a] = before[queue[a]]
            before[queue[a]] = a
        if n < 0:
            n = before[-1 - n]
        while n in ahead:
            t, why = fin[n] - dur[n] - 1e-6, None
            for m, gap in edges[n]:
                if fin[m] + gap >= t:
                    why = m
                    break
            if why is None:
                why = ahead[n]
                if why is not None and why not in preds[n]:
                    pairs.append((why, n))
            n = why
        return pairs

    for sweep in range(sweeps + 1):
        alone = sweep < NOM["alone"] * sweeps
        models, later = (every[:1], onward[:1]) if alone or len(every) == 1 else (every[1:], onward[1:])
        K = len(models)
        if alone:
            best = None
        heat = K * NOM["hot"] * (NOM["cold"] / NOM["hot"]) ** (sweep / max(1, sweeps - 1))
        far, whole = [], 0.0
        for k in range(K):
            dur, tail, e = models[k][0], models[k][2], later[k]
            d, nxt = [0.0] * R, [0.0] * 6
            for n in reversed(seq):
                t = max(tail[n], nxt[queue[n]])
                for s, gap in e[n]:
                    if d[s] + gap > t:
                        t = d[s] + gap
                d[n] = t + dur[n]
                if queue[n] != 5:
                    nxt[queue[n]] = d[n]
            far.append(d)
            whole += max(d) / K
        if not alone and (best is None or whole < best[0]):
            best = (whole, seq[:])
        ORDER.setdefault("sweeps", []).append(round(whole))
        if sweep == sweeps:
            break
        fins, frees = [[0.0] * R for _ in models], [[0.0] * 6 for _ in models]
        for a in starts:
            win, rest = seq[a:a + span], seq[a + span:]
            for j, n in enumerate(win):
                place[n] = j
            inside = set(win)
            exits, exitq = [], []
            for k in range(K):
                out = [0.0] * R
                for n in win:
                    out[n] = max([models[k][2][n]] + [far[k][s] + gap for s, gap in later[k][n] if s not in inside])
                exits.append(out)
                outq = [0.0] * 6
                for n in reversed(rest[:200]):
                    outq[queue[n]] = far[k][n]
                exitq.append(outq)
            now, state = times(win, 0, [(fins[k], [(frees[k], 0.0, -1)]) for k in range(K)], 1e18)
            pairs, size = None, len(win)
            for it in range(tries):
                x = (x * 6364136223846793005 + 1442695040888963407) % 2 ** 64
                if pairs is None:
                    k = (x >> 60) % K
                    pairs = blocked(win, k, state[k][0], state[k][3])
                if not pairs:
                    pairs = None
                    if it > 8:
                        break
                    continue
                m, n = pairs[(x >> 33) % len(pairs)]
                i, j = place[m], place[n]
                step, forward = (0, 0, 1, 2, 4, 8)[(x >> 20) % 6], (x >> 30) % 2
                z = i if forward else j
                while step and 0 < z < size - 1:
                    z += -1 if forward else 1
                    if queue[win[z]] == queue[n]:
                        step -= 1
                        i, j = (z, j) if forward else (i, z)
                part, move = win[i:j + 1], {n if forward else m}
                for b in (reversed(part) if forward else part):
                    if b in move:
                        move.update([y for y in (preds if forward else succs)[b] if y in inside and i <= place[y] <= j])
                if m in move and n in move:
                    continue
                new = win[:i] + [b for b in part if (b in move) == bool(forward)] + [b for b in part if (b in move) != bool(forward)] + win[j + 1:]
                limit = now - heat * math.log(((x >> 8) % 4096 + 0.5) / 4096)
                v, after = times(new, i // 8, state, limit - soft * 2.9 * state[-1][2])
                if v <= limit:
                    now, win, state, pairs = v, new, after, None
                    for z in range(i, j + 1):
                        place[win[z]] = z
                elif it % 16 == 15:
                    pairs = None
            seq[a:a + span] = win
            fins = [s[0] for s in state]
            frees = [s[1][hop // 8][0] if hop // 8 < len(s[1]) else s[1][-1][0] for s in state]
    return [n for j in best[1] for n in runs[j]]


def emit(g, T, ops):
    eng = {"v": g.vector, "s": g.scalar, "t": g.tensor, "g": g, "y": g.sync}
    qsem = {"v": "qv", "s": "qs", "t": "qt", "g": "qg"}
    order = plan(ops)
    last, pos, cnt, close = {}, {}, {}, {}
    for n in order:
        o = ops[n]
        close[o["group"]] = n
        if o["tok"] is None:
            last[o["q"]] = n
            cnt[o["q"]] = cnt.get(o["q"], 0) + 1
            pos[n] = (o["q"], cnt[o["q"]])
        else:
            pos[n] = (("x", n), 1)
    place = {n: j for j, n in enumerate(order)}
    known = {}
    for n in order:
        o = ops[n]
        o["stop"][0] = close[o["group"]] == n
        kn = known.setdefault(o["q"], {})
        o["waits"] = []
        if o["q"] is not None:
            for m in sorted(o["deps"], key=lambda m: -place[m]):
                key, val = pos[m]
                if kn.get(key, 0) < val:
                    o["waits"].append(m)
                    kn[key] = val
                    for k2, v2 in ops[m]["kn"].items():
                        if kn.get(k2, 0) < v2:
                            kn[k2] = v2
        o["kn"] = dict(kn) if o["q"] is not None else {}
    need = set(last.values())
    for o in ops:
        need.update(o["waits"])
    cnt, final = {}, {}
    for n in order:
        o = ops[n]
        o["inc"] = None
        if o["tok"] is None and n in need:
            cnt[o["q"]] = cnt.get(o["q"], 0) + 1
            o["inc"] = (qsem[o["q"]], cnt[o["q"]])
        if o["q"] is None:
            continue
        for m in o["waits"]:
            s, v = ops[m]["tok"] or ops[m]["inc"]
            eng[o["q"]].wait_ge(T.sem[s], v)
        ins = o["fn"](eng[o["q"]])
        if o["inc"]:
            ins.then_inc(T.sem[o["inc"][0]], 1)
            final[o["inc"][0]] = o["inc"][1]
        elif o["tok"]:
            final[o["tok"][0]] = o["tok"][1]
    for s, v in final.items():
        g.wait_ge(T.sem[s], v)


def rank_program(g, core, T, topo):
    rank = T.rank_of(core)
    if rank is None:
        return
    cores = list(T.cores)
    NR = len(cores)
    ops = []
    ndma = [0]
    sent = {}
    now = [9, 0, "set"]
    groups = {}
    cut = PAR["cut"]
    CH = [(0, cut, cut), (cut, L, LP)]
    KEEP, SPLIT, WIN = PAR["keep"], PAR["split"], PAR["win"]
    kss = sorted(set([0] + [x[2] for row in PAR["pieces"] for x in row]))
    common = [x for x in topo.engines(cores[0], cores[1]) if all(x in topo.engines(a, b) for a in cores for b in cores if a != b)]

    def ap(a):
        if not isinstance(a, tuple):
            return a
        if a[0] == "i":
            return ap(a[1]).indirect(ap(a[2]))
        if a[0] == "b":
            return T[a[1]][:, a[2] if a[3] is None else slice(a[2], a[3]), a[4] if a[5] is None else slice(a[4], a[5])]
        _, name, c0, c1, st, p = a
        cs = slice(c0, c1) if st == 1 else slice(c0, c1, st)
        if p is None:
            return T[name][:, cs]
        return T[name][slice(p[0], p[1]) if p[2] == 1 else slice(p[0], p[1], p[2]), cs]

    def rec(q, kind, fn, outs, ins, tok=None, lat=0.0, more=()):
        acc = []
        for lst, wr in ((ins, False), (outs, True)):
            for a in lst:
                if not isinstance(a, tuple):
                    continue
                if a[0] == "i":
                    acc.append(extent(a[1]) + (wr,))
                    acc.append(extent(a[2]) + (False,))
                else:
                    acc.append(extent(a) + (wr,))
        dur = (100.0 if q else 0.0) if tok else duration(kind, outs, ins)
        ops.append({"q": q, "fn": fn, "acc": acc, "tok": tok, "dur": dur, "lat": NOM["pel"] if q == "t" else lat, "more": more,
                    "edge": False, "line": None, "group": None, "stop": [False], "tag": tuple(now), "spec": (kind, outs, ins)})
        return len(ops) - 1

    def line(key):
        ops[-1]["line"] = key

    def cp(out, x):
        rec("v", "cp", lambda e: e.tensor_copy(ap(out), ap(x)), [out], [x])

    def tt(out, x, y, op):
        rec("v", "tt", lambda e: e.tensor_tensor(ap(out), ap(x), ap(y), op), [out], [x, y])

    def ts(out, x, s1, op0, s2=None, op1=None):
        if op1 is None:
            rec("v", "ts", lambda e: e.tensor_scalar(ap(out), ap(x), ap(s1), None, op0), [out], [x, s1])
        else:
            rec("v", "ts", lambda e: e.tensor_scalar(ap(out), ap(x), ap(s1), ap(s2), op0, op1), [out], [x, s1, s2])

    def scan(out, d0, d1, op0, op1):
        rec("v", "ts", lambda e: e.tensor_tensor_scan(ap(out), ap(d0), ap(d1), 0.0, op0, op1), [out], [d0, d1])

    def tr(out, x):
        rec("v", "ts", lambda e: e.transpose(ap(out), ap(x)), [out], [x])

    def top(out, x):
        rec("v", "red", lambda e: e.tensor_reduce(ap(out), ap(x), AxisListType.X, OP.max), [out], [x])

    def ms(out, c):
        rec("v", "ts", lambda e: e.memset(ap(out), c), [out], [])

    def act(out, x, func=None, bias=None, scale=None):
        if bias is not None:
            rec("s", "act", lambda e: e.activation(ap(out), ap(x), ACT.Identity, bias=ap(bias), scale=ap(scale or 1.0)), [out], [x, bias, scale])
        elif scale is not None:
            rec("s", "act", lambda e: e.activation(ap(out), ap(x), func or ACT.Identity, scale=ap(scale)), [out], [x, scale])
        else:
            rec("s", "act", lambda e: e.activation(ap(out), ap(x), func or ACT.Copy), [out], [x])

    def mm(out, lhs, rhs, start=False):
        stop = [False]
        rec("t", "mm", lambda e: e.matmul(ap(out), ap(lhs), ap(rhs), start, stop[0]), [out], [lhs, rhs])
        if start:
            groups[out[1]] = len(ops)
        ops[-1].update({"edge": start, "group": groups[out[1]], "stop": stop})

    def iota(out, pat, base, cm, flt=True):
        if flt:
            rec("g", "iota", lambda e: e.iota(ap(out), pat, base, cm, allow_small_or_imprecise_dtypes=True), [out], [])
        else:
            rec("g", "iota", lambda e: e.iota(ap(out), pat, base, cm), [out], [])
        if out[1] in ("cI", "row", "R16", "R32") or out[1:3] == ("VT", 0):
            line("iota")

    def pick(out, x, pat, cmp, fill, base, cm):
        rec("g", "pick", lambda e: e.affine_select(ap(out), ap(x), pat, cmp, fill, base, cm), [out], [x])

    def dma(q, out, x, lat=2200.0):
        s = "d%d" % ndma[0]
        ndma[0] += 1
        n = rec(q, "dma", lambda e: e.dma_start(ap(out), ap(x)).then_inc(T.sem[s], 16), [out], [x], (s, 16), lat - NOM["issue"])
        ops[-1]["dur"] = NOM["issue"]
        if now[0] == 9:
            line("load" + q)
        return n

    def col(j):
        return A("cF", j, j + 1)

    def swap(bank, out0, n, src):
        for q in range(2):
            for g0 in range(2):
                mm(A(bank, out0 + q, out0 + 2 * n, 2), A("LL", 128 * (2 * q + g0), 128 * (2 * q + g0 + 1)), src(g0), g0 == 0)

    def before(out, name, at, c, early):
        b0, b1 = CH[c][0] // 32, CH[c][2] // 32
        for d in range(1, b1):
            lo = max(b0, d)
            if (d >= b1 - b0) == early:
                mm(A(out[1], out[2] + 2 * (lo - b0), out[3]), A("O32"), A(name, at + 2 * (lo - d), at + 2 * (b1 - d)))

    dma("y", A("odi"), T.od[:], 2300.0)
    dma("s", A("nbi", 0, W // 2), T.nb[:, 0:W // 2], NOM["nb"] - 1600)
    dma("y", A("nbi", W // 2, W), T.nb[:, W // 2:W], NOM["nb"] - NOM["issue"])
    dma("y", A("XT", 0, W), T.xs[:], NOM["xs"] - 2 * NOM["issue"])
    dma("y", A("XT", W, B), T.xs[:, 0:B - W], NOM["xs"] - 3 * NOM["issue"] + 200)
    iota(A("cI"), [[0, 8]], 0, 1, False)
    iota(A("row"), [[1, 160]], -16, 0)
    iota(A("R16"), [[16, 8], [0, 16]], 0, 0)
    iota(A("R32"), [[32, 4], [0, 32]], 0, 0)
    iota(A("VT", 0, 512), [[1, 512]], -2047, 0)
    for n in (512, 1024):
        act(A("VT", n, 2 * n), A("VT", 0, n), bias=float(n))
    iota(A("RP"), [[1, 32], [0, 16]], 0, 0)
    iota(A("lanb"), [[32, 7], [0, 2]], -352, 0)
    iota(A("par"), [[0, 7], [1, 2]], 0, 0)
    dma("y", A("thi", p=G8), T.th[:], NOM["xs"] - 2 * NOM["issue"])
    dma("y", A("wti"), T.wt[:], NOM["xs"] - 2 * NOM["issue"])
    for j, msk in ((0, 15), (1, 112), (2, 31), (4, 96), (6, 1), (7, 6)):
        ts(A("cI", j, j + 1), A("cI", j, j + 1), msk, OP.bitwise_and)
    cp(A("cF", 0, 8), A("cI"))
    ms(A("one"), 1.0)
    ms(A("DC"), 0.0)
    ms(A("a1", L, LP), -1.0)
    for piece, value in ((A("cur"), L - 1023), (A("cz"), B - 1024 - 4096), (A("TT", W, B + 192), 0), (A("VT", W, B), 0), (A("mex"), 0),
                         (A("snd", 0, 3 * U), 0), (A("omf", 78, 96), 0), (A("Z0"), 0), (A("Sy"), 0), (A("rst"), -1024),
                         (A("own", L, LP), 0), (A("own", LP + L, 2 * LP), 0), (A("td"), 0), (A("td", 6, 27, 9), 3 * 2 ** 22), (A("td", 7, 27, 9), -3 * 2 ** 22), (A("tq", 1, 2), 1),
                         (A("bt", 16, 108, 36), 0), (A("bt", 4 * rank, 108, 36), 0), (A("bt", 20, 36), -2 ** 23), (A("bt", 56, 72), -2 ** 23),
                         (A("bt", 92, 108), -2 ** 23)):
        iota(piece, [[0, width(piece)]], value, 0)
    ts(A("oda"), A("odi"), 2047, OP.add)
    cp(A("od16"), A("odi"))
    ts(A("odb"), A("oda"), 2047, OP.bitwise_and)
    cp(A("om16"), A("odb"))
    if WIN:
        cp(A("omf", 0, 78), A("odb"))
    ts(col(8), col(0), 1.0, OP.add, 2.0, OP.min)
    ts(A("Ib"), A("row", 16, 144), col(3), OP.is_equal)
    ts(A("In"), A("row", 16, 144), col(3), OP.is_equal, -1.0, OP.mult)
    for name, value in (("ZG", -32768.0), ("ZM", 65536.0)):
        ts(A(name), A("row", 1, 145), col(1), OP.is_equal, value, OP.mult)
    for name, value in (("Bn", -1.0), ("S2", 2.0)):
        ts(A(name), A("R16", 0, 128, 16), col(1), OP.is_equal, value, OP.mult)
    ts(A("BO", 0, 128), A("R16"), col(1), OP.is_equal, -32768.0, OP.mult)
    ts(A("O32"), A("R32"), col(4), OP.is_equal)
    ts(A("RP"), A("RP"), col(2), OP.is_equal)
    ts(A("DP"), A("Ib"), col(8), OP.mult, float(2 ** 27), OP.mult)
    ts(A("Lt"), A("row", 16, 144), col(3), OP.is_gt)
    tt(A("Lt"), A("Lt"), A("O32"), OP.mult)
    for q in range(2):
        for g0 in range(2):
            pick(A("LL", 128 * (2 * q + g0), 128 * (2 * q + g0 + 1)), A("Z0"), [[-32, 4], [1000 - 2000 * g0, 2], [-1, 16]], OP.not_equal, 1.0,
                 1000 * g0 - 16 * q, 1)
    pick(A("If"), A("mex", 0, 128), [[1, 128]], OP.not_equal, 1.0, 0, -1)
    for j, k in enumerate(kss[1:]):
        pick(A("BO", 128 * j + 128, 128 * j + 256), A("BO", 0, 128), [[0, 8], [1, 16]], OP.is_ge, 0.0, -k, 0)
    for name, value in (("LZ", 4096.0), ("LW", -560.0)):
        pick(A(name), A("Lt"), [[1, 128]], OP.not_equal, value, 0, -1)
    for name, value in (("IB", BIG), ("ID", 1024.0)):
        pick(A(name), A("Z0"), [[1, 128]], OP.not_equal, value, 0, -1)
    act(A("lanc"), A("lanb"), bias=col(2))
    for l0, l1, lp in CH:
        ts(A("nr", l0 + lp + 15, 2 * lp, 16), A("lanb", l0 // 16, lp // 16), col(2), OP.add, float(B - 2047 + 352), OP.add)
    ts(A("mRG"), A("par"), col(6), OP.is_equal, 32768.0, OP.mult)
    ts(A("O3f"), A("R32"), 1.0 / 16, OP.mult, col(7), OP.is_equal)
    ts(col(9), A("wti"), 1.0 / XS, OP.mult)
    cp(A("ytl", 64, 65, p=G8), A("thi", p=G8))
    ts(A("WB"), A("R16"), col(1), OP.is_equal, col(9), OP.mult)
    iota(A("MB"), [[0, 3], [1, 19]], 0, 0)
    ts(A("MB"), A("MB"), col(0), OP.not_equal, float(2 ** 21), OP.mult)
    pick(A("MB"), A("MB"), [[0, 3], [-1, 19]], OP.is_ge, float(2 ** 40), 15, 0)
    iota(A("hd"), [[0, 171]], 0, 0)
    iota(A("hd", 0, 171, 19), [[0, 9]], 2 ** 23, 0)
    for at, value in ((17, 1.5 * 2 ** 34), (18, -1.5 * 2 ** 34)):
        pick(A("hd", at, 171, 19), A("hd", at, 171, 19), [[0, 9]], OP.is_gt, value, 0, 0)
    for j in range(3):
        pick(A("hd", 57 * j + 16, 57 * j + 57, 19), A("hd", 57 * j + 16, 57 * j + 57, 19), [[0, 3]], OP.is_gt, 77 * (3 + j) - 1023.5, 0, 0)
    iota(A("sne", 0, U), [[0, U]], 0, 0)
    act(A("ytl", 65, 67, p=G8), A("one", 0, 2, p=G8), scale=A("ytl", 64, 65, p=G8))
    pick(A("Iq"), A("mex", 0, U), [[1, U]], OP.not_equal, 0.25, 0, -1)
    pick(A("Sx"), A("Sy"), [[16, 8], [0, 17]], OP.is_gt, -1.0 / XS, 0, -1)
    pick(A("Sx"), A("Sx"), [[16, 8], [0, 17]], OP.is_ge, 0.0, 15, -1)
    for out, src, value in ((A("Sx", 16, 136, 17), "Z0", -1.0), (A("Sy", 16, 136, 17), "Z0", -1.0), (A("Sf"), "mex", 1.0)):
        pick(out, A(src, 0, 8), [[-16, 8]], OP.not_equal, value / 32768, -15, 1)
    pick(A("r17"), A("mex", 0, 136), [[0, 8], [1, 17]], OP.not_equal, BIG, 0, 0)
    pick(A("rst"), A("rst"), [[0, 8], [1, 16]], OP.not_equal, BIG, 0, 0)
    ms(A("td", 5, 27, 9), -0.375)
    ms(A("tq", 0, 1), -0.25)
    on_s = PAR["tts"]
    iota(A("idf"), [[16, 32]], 0, 0)
    ts(A("id16"), A("idf"), col(0), OP.add)
    for j in range(4):
        now[2] = "tt%d" % j
        if j < 4 - on_s:
            ts(A("TT", 512 * j, 512 * j + 512), A("nbi", 512 * j, 512 * j + 512), -2047.0, OP.add)
        else:
            act(A("TT", 512 * j, 512 * j + 512), IND(A("nbi", 512 * j, 512 * j + 512), A("id16")), bias=-2047.0)
    now[2] = "set"
    act(A("thx", 0, 14, p=G8), A("mRG", p=G8), bias=-8192.0, scale=A("ytl", 64, 65, p=G8))
    mm(A("pg", 0, 14), A("O3f", p=G8), A("thx", 0, 14, p=G8), True)
    cp(A("thP"), A("pg", 0, 14))
    tabled = (0, 14, 26, 40, 52, 66, 78)
    act(A("VT", B, B + LP), IND(A("VT", 0, W), A("od16", 0, 14)))
    for j0, j1 in ((14, 40), (40, 78)):
        act(A("VT", B + 16 * j0, B + 16 * j1), IND(A("VT", 0, W), A("od16", j0, j1)))

    def own_of(t, l0, l1):
        return A("own", LP * (t % 2) + l0, LP * (t % 2) + l1) if t else A("XT", B + l0, B + l1)

    def flags(s, w0=0, wp=14):
        return A("fr", 14 * (s % 3) + w0, 14 * (s % 3) + wp)

    def guests_in(t):
        j = t - 3
        now[:] = [t, 0, "gh"]
        mag = 1.5 * 2 ** 23 * XS
        mm(A("pg", 0, 57), A("Ib"), A("MB"), True)
        for name, gin, xb in landed(j):
            rec(None, "", None, [gin], [], ("ga" + name, len(common)), 0.0, [sent["g", name]])
            ts(xb, gin, mag, OP.add, -mag, OP.add)
            for u in range(3):
                mm(A("pg", 19 * u, 19 * u + 16), A("WB"), A("xb", xb[2] + 16 * u, xb[2] + 16 * u + 16))
        scan(A("hs"), A("hd", 57 * j, 57 * j + 57), A("pg", 0, 57), OP.add, OP.min)
        tt(A("hf", 0, 3), A("hs", 16, 57, 19), A("hs", 18, 57, 19), OP.subtract)
        ts(A("h16", 0, 3), A("hf", 0, 3), 1023.5, OP.add)
        ts(A("g16"), IND(A("TO%d" % j) if t in KEEP else A("TT", 0, W), A("h16", 0, 3)), 2047.0, OP.add)

    def landed(j):
        late = (str(j), A("gin%d" % j), A("xb", U * (j % 2), U * (j % 2) + U))
        return [("e", A("gine"), A("xb", 2 * U, 3 * U)), late] if j + 2 in PAR["early"] else [late]

    def guests_judged(t):
        j = t - 3
        now[:] = [t, 0, "gM"]
        for n, (_, gin, xb) in enumerate(landed(j)):
            mm(A("pq", 128, 256, p=(0, U, 1)), xb, A("Ib"), n == 0)
        act(A("xT", p=(0, U, 1)), A("pq", 128, 256, p=(0, U, 1)), scale=1.0 / XS)
        now[2] = "gG"
        for who, a, b in PAR["gv"][j]:
            (cp if who == "v" else act)(A("Gg", 16 * a, 16 * b), IND(A("XT", 0, W), A("g16", a, b)))
        slots48 = (0, U, 1)
        parts = [(A("pg", 256, 512), 32, U, PAR["guests"][j][1] == "v"), (A("pq"), 0, 32, PAR["guests"][j][0] == "v")]
        for cell, a, b, by_max in parts:
            now[2] = "gR"
            mm(cell, A("xT", p=(a, b, 1)), A("RP", 0, 16 * (b - a), p=(a, b, 1)), True)
            now[2] = "gM"
            if not by_max:
                mm(cell, A("In"), A("Gg", 16 * a, 16 * b))
                act(A("Ag", 16 * a, 16 * b), cell, ACT.Abs, None, 0.5)
        alike = parts[0][3] == parts[1][3]
        sums = [(0, U, parts[0][3])] if alike else [x[1:] for x in parts]
        now[2] = "g0"
        mm(A("pg", 0, 136, p=slots48), A("Z0", 0, U), A("Sy"), True)
        for _, gin, xb in landed(j):
            for a, b, by_max in sums:
                mm(A("pg", 0, 136, p=(a, b, 1)), A("xb", xb[2] + a, xb[2] + b), A("Sx" if by_max else "Sy"))
            mm(A("pg", 16, 136, 17, slots48), gin, A("Sf"))
        now[2] = "gM"
        for cell, a, b, by_max in parts:
            if by_max:
                tt(A("Ag", 16 * a, 16 * b), A("Gg", 16 * a, 16 * b), cell, OP.max)
        now[2] = "gs"
        for a, b, by_max in sums:
            for k in range(16 if by_max else 0):
                mm(A("pg", k, 136, 17, (a, b, 1)), A("Gg", 16 * a + k, 16 * b, 16), A("Bn"))
        now[2] = "gj"
        for k in range(16):
            mm(A("pg", k, 136, 17, slots48), A("Ag", k, 16 * U, 16), A("S2"))
        scan(A("js", p=slots48), A("r17", p=slots48), A("pg", 0, 136, p=slots48), OP.add, OP.min)
        mm(A("pq", 0, U, p=G8), A("js", 16, 136, 17, slots48), A("Iq", p=slots48), True)
        mine = A("bt", 36 * j + 4 * rank, 36 * j + 4 * rank + 1)
        top(mine[:5] + (G8,), A("pq", 0, U, p=G8))
        if t == 5:
            act(A("jC", p=G8), A("pq", 0, U, p=G8), scale=4.0)
        masks = best_masks(core, cores, topo)

        def send(e):
            trs = []
            for c, (msk, _) in masks.items():
                rid, pid = topo.addr(c, core)
                trs.append(RemoteDMATransfer(dst_ids=[DstId(rid=rid, pnc=pid)], dma_engine_mask=msk, remote_sem=T.sem["ba%d" % j],
                                             src=ap(mine), dst=ap(mine)))
            return e.remote_dma_fused(trs, local_sem=T.sem["left%d" % (3 + j)])
        sent["b", j] = rec("g", "", send, [], [mine], ("left%d" % (3 + j), sum(n for _, n in masks.values())), NOM["rem"] - NOM["call"])
        ops[-1]["dur"] = NOM["call"]

    def threshold(t):
        j = t - 3
        n = sum(best_masks(c, cores, topo)[core][1] for c in cores if c != core)
        now[:] = [t, 0, "thr"]
        act(A("td", 9 * j + 4, 9 * j + 9, 4, G8), A("tq", p=G8), scale=A("ytl", 63 + t, 64 + t, p=G8))
        rec(None, "", None, [A("bt", 36 * j + 4 * r, 36 * j + 4 * r + 1) for r in range(NR) if r != rank], [], ("ba%d" % j, n), 0.0, [sent["b", j]])
        scan(A("ytl", t, 65 + t, 8, G8), A("td", 9 * j, 9 * j + 9, p=G8), A("bt", 36 * j, 36 * j + 36, 4, G8), OP.add, OP.max)
        if t == 3:
            ts(A("thx", 14, 28, p=G8), A("mRG", p=G8), A("ytl", 64 + t, 65 + t, p=G8), OP.mult, -8192.0, OP.add)

    def leavers(t, name, src, s0, first):
        dst = cores[(rank + 1 + t % (NR - 1)) % NR]

        def send(e):
            rid, pid = topo.addr(dst, core)
            return e.remote_dma(ap(A("gin" + name)), ap(A(src, s0, s0 + U)), T.sem["ga" + name], T.sem["lf" + name], pid, rid,
                                sum(1 << x for x in common))
        sent["g", name] = rec("g", "", send, [], [A(src, s0, s0 + U)], ("lf" + name, len(common)), NOM["rem"] - NOM["call"])
        ops[-1]["dur"] = NOM["call"] + (NOM["first"] if first else 0.0)

    def pack(t, l0, l1, lp):
        mag = 1.5 * 2 ** 38
        ts(A("mex", l0 + 15, lp, 16), A("mn", l0 // 16, lp // 16), mag, OP.add, -mag, OP.add)
        tr(A("mC", l0, lp), A("mex", l0, lp))
        src, s0 = ("sne", 0) if t in PAR["early"] and l0 == 0 else ("snd", U * (4 - t))
        tt(IND(A(src, s0, s0 + 432), A("s16", l0 // 16, l1 // 16)), A("mC", l0, l1), A("ownf", L * (t % 2) + l0, L * (t % 2) + l1), OP.add)
        if src == "sne":
            leavers(t, "e", src, s0, t == 2)

    def columns(t, l0, l1):
        return IND(A("TT", 0, B + 240 if t - 1 in WIN else B + L * (t + 1)), A3("L16", 0, None, l0 // 16, l1 // 16))

    def entries(l0, l1):
        return A3("L16", 1, None, l0 // 16, l1 // 16)

    def front(t, c):
        now[:2] = [t, c]
        l0, l1, lp = CH[c]
        c16, own = A("c16", l0, l1), own_of(t, l0, l1)
        now[2] = "c"
        if t == 0:
            ts(c16, IND(A("nbi"), A("om16", l0 // 16, l1 // 16)), 1.0, OP.add)
        else:
            ts(c16, columns(t, l0, l1), 2047.0, OP.add)
        now[2] = "own"
        if t:
            act(own, IND(A("XT", 0, B + L * (t + 1)), entries(l0, l1)))
        else:
            act(own_of(t, l0, lp), IND(A("XT", 0, W), A("od16", l0 // 16, lp // 16)))
        now[2] = "oT"
        mm(A("po%d" % c, 0, l1 - l0), A("Ib"), own, True)
        if t not in PAR["whole"]:
            numbers(t, l0, l1, lp)
        elif c == 1:
            numbers(t, 0, L, LP)

    def windows(t):
        now[:] = [t, 1, "v16"]
        bank = PAR["vb"]
        for q in range(2):
            for g0 in range(2):
                for h in range(2):
                    mm(A(bank, 496 + q, 510, 2), A("LL", 128 * (2 * q + g0), 128 * (2 * q + g0 + 1)),
                       A("DT", LP * h + 16 * g0, LP * h + LP, 32), g0 + h == 0)
        ts(A("v16"), A(bank, 496, 510), 2047.0, OP.add)

    def numbers(t, l0, l1, lp):
        c16, cc, fl, dif = A("c16", l0, l1), A("DC", l0, l1) if t < 5 else A("cf", l0, l1), A("fl", l0, l1), A("DC", LP + l0, LP + l1)
        now[2] = "cc"
        if t == 0:
            vrep, raw = A("VT", B + l0, B + l1), A("cr", l0, l1)
            ts(raw, c16, -2047.0, OP.add)
        else:
            vrep, raw = IND(A("VT", 0, B + L * (t + 1)), entries(l0, l1)), columns(t, l0, l1)
        ts(fl, c16, 2048.0, OP.is_ge, -2048.0, OP.mult)
        tt(cc, raw, fl, OP.add)
        now[2] = "dif"
        tt(dif, vrep, cc, OP.subtract)
        near = 1.5 * 2 ** 28 + 32
        now[2] = "a1"
        ts(A("a1", l0, l1), dif, near, OP.add, near, OP.is_equal)
        now[2] = "DT"
        if t == 5:
            now[2] = "wr"
            ts(IND(A("yno"), entries(l0, l1)), cc, 1.0, OP.mult, 2047.0, OP.add)
        elif t and lp - l0 == LP:
            tr(A("DT"), A("DC"))
        else:
            for h in range(2 if t else 1):
                tr(A("DT", LP * h + l0, LP * h + lp), A("DC", LP * h + l0, LP * h + lp))

    def so_far(t, c):
        w0, wp = (CH[c][0] // 16, CH[c][2] // 16) if t in SPLIT else (0, 14)
        return A("pk%d" % c, 464, 464 + wp - w0), w0, wp

    def keys(t, c):
        now[:2] = [t, c]
        b0, b1, bp = CH[c]
        pk, po = "pk%d" % c, "po%d" % c
        now[2] = "mk"
        if t and (c == 1 or t in SPLIT):
            mk, w0, wp = so_far(t, c)
            mm(mk, A("If"), A("mn", w0, wp) if t > 1 else A("ks", 15, LP, 16), True)
            mm(mk, A("IB"), flags(t - 1, w0, wp))
        if t in (2, 3):
            bar(t, c, pk)
        ends = [0] + [x[0] for x in PAR["pieces"][t]]
        mine = [(j, ends[j], b, who, ks) for j, (b, who, ks) in enumerate(PAR["pieces"][t]) if b0 <= ends[j] < b1]
        wide = len(mine) > 1 and t in PAR["wide"]
        now[2] = "ini"
        ks = mine[0][4]
        mm(A(pk, 0, bp - b0), A("BO", 128 * kss.index(ks), 128 * kss.index(ks) + 128), own_of(t, b0, bp), True)
        now[2] = "pen"
        mm(A(pk, 0, bp - b0), A("DP"), A("a1", b0, bp))
        turn = 0
        for j, a, b, who, ks in mine:
            now[2] = "G%d" % j
            if who:
                cp(A("G", 16 * a, 16 * (a + who)), IND(A("XT", 0, B), A("c16", a, a + who)))
            if a + who < b:
                act(A("G", 16 * (a + who), 16 * b), IND(A("XT", 0, B), A("c16", a + who, b)))
            n, key = b - a, A(pk, a - b0, b - b0)
            turns = -(-ks // (512 // n))
            for r in range(turns):
                k0, k1 = ks * r // turns, ks * (r + 1) // turns
                bank = ["pr%d" % c, ("pq", "pg")[c]][turn % PAR["ring"][t]]
                turn += 1
                now[2] = "D%d" % j
                for k in range(k0, k1):
                    cell = A(bank, n * (k - k0), n * (k - k0 + 1))
                    mm(cell, A("In"), own_of(t, a, b), True)
                    mm(cell, A("Ib"), A("G", 16 * a + k, 16 * b, 16))
                act(A("M", 16 * a + n * k0, 16 * a + n * k1), A(bank, 0, n * (k1 - k0)), ACT.Abs, None, 0.5)
                now[2] = "SA%d" % j
                for k in range(k0, k1):
                    mm(key, A("ZM", 15 - k, 143 - k), A("M", 16 * a + n * k, 16 * a + n * (k + 1)))
            now[2] = "SG%d" % j
            for k in range(ks, 16):
                mm(key, A("ZG", 15 - k, 143 - k), A("G", 16 * a + k, 16 * b, 16))
            if wide:
                if b < b1:
                    continue
                a, n, key = b0, b1 - b0, A(pk, 0, b1 - b0)
            for k in range(ks, 16):
                piece = A("Mw", n * k, n * (k + 1)) if wide else A("M", 16 * a + n * k, 16 * a + n * (k + 1))
                now[2] = "M%d" % j
                tt(piece, A("G", 16 * a + k, 16 * b, 16), A(po, a - b0, b - b0), OP.max)
                now[2] = "SM%d" % j
                mm(key, A("ZM", 15 - k, 143 - k), piece)

    def bar(t, c, bank):
        w0, wp = CH[c][0] // 16, CH[c][2] // 16
        thG = A(bank, 496, 496 + wp - w0)
        now[2] = "old"
        mm(thG, A("IB"), flags(t - 1, w0, wp), True)
        mm(thG, A("IB"), flags(t - 2, w0, wp))
        now[2] = "th"
        mm(thG, A("O3f", p=G8), A("thx", 14 * (t == 4) + w0, 14 * (t == 4) + wp, p=G8))

    def middle(t):
        now[:] = [t, 1, "ownf"]
        hi = B + L * (t + 1)
        if 2 <= t <= 4:
            act(A("ownf", L * (t % 2), L * (t % 2) + L), own_of(t, 0, L), scale=XS)
        now[2] = "wr"
        if t < 5:
            for l0, l1 in ((0, cut), (cut, L)) if t in PAR["wr2"] else ((0, L),):
                cp(IND(A("TT", 0, W), A("v16" if t else "od16", l0 // 16, l1 // 16)), A("DC", l0, l1))
        if t == 4:
            now[2] = "out"
            act(A("yno", B, B + KN), IND(A("TT", 0, W), A("od16", 0, KN // 16)), bias=2047.0)
        if t + 1 in KEEP:
            dma("y", A("TO%d" % (t - 2)), A("TT", 0, W), NOM["copy"])
        if t < 5:
            now[2] = "seed"
            if t in WIN:
                act(A("TT", B, B + 240), IND(A("TT", 0, W), A("ow16", 0, 15)), bias=1.0)
            else:
                act(A("TT", B + 192, hi + L), IND(A("TT", 0, W), A("om16", 12, 13 * (t + 2))), bias=1.0)
            now[2] = "tab"
            j0, j1 = tabled[t + 1], tabled[t + 2]
            act(A("XT", B + 16 * j0, B + 16 * j1), IND(A("XT", 0, W), A("od16", j0, j1)))

    def slots(c, w0, wp):
        now[2] = "s16"
        swap("po%d" % c, 384, (wp - w0) // 2, lambda g0: A("slt", w0 + g0, wp, 2))
        ts(A("s16", w0, wp), A("po%d" % c, 384, 384 + wp - w0), 560.0, OP.add)

    def back(t, c):
        now[:2] = [t, c]
        l0, l1, lp = CH[c]
        n, w0, wp = lp - l0, l0 // 16, lp // 16
        nw = wp - w0
        pk, po, k0 = "pk%d" % c, "po%d" % c, LP * (t % 2)
        leave = 2 <= t <= 4
        kmin = A("ks", k0 + l0 + 15, k0 + lp, 16)
        thD, thG = A(po, 480, 480 + nw), A(po if t == 4 else pk, 496, 496 + nw)
        if t == 4:
            bar(t, c, po)
            mm(thD, A("O3f", p=G8), A("thx", 14 + w0, 14 + wp, p=G8), True)
        kT, ks = A(pk, 256, 256 + n), A("ks", k0 + l0, k0 + lp)
        now[2] = "k"
        tr(kT, A(pk, 0, n))
        scan(ks, A("rst", 0, n), kT, OP.add, OP.min)
        if t < 5:
            yy, ne = A("pr%d" % c, 0, n), A("ne", l0, lp)
            now[2] = "y0"
            mm(yy, A("Ib"), A("DT", l0, lp), True)
            now[2] = "n"
            tt(ne, ks, kT, OP.is_lt)
            mm(yy, A("IB"), ne)
            scan(A("nr", 2 * l0, l0 + lp), ne, yy, OP.mult, OP.min)

        def least_m():
            now[2] = "mn"
            mk, m0, mp = so_far(t, c)
            tt(A("mn", m0, mp), A("ks", k0 + 16 * m0 + 15, k0 + 16 * mp, 16), mk, OP.min)
        if t in SPLIT or (t == 5 and c == 1):
            least_m()
        if t == 5:
            return
        now[2] = "fate"
        fr, ww, zz = flags(t, w0, wp), A(po, 336, 336 + nw), A(pk if leave else po, 480, 480 + 2 * nw)
        low = A("mn", w0, wp) if t == 4 else kmin
        if leave:
            tt(A("go", w0, wp), low, thG, OP.is_ge)
        tt(A("dead", w0, wp) if leave else fr, low, thD if t == 4 else A("thP", w0, wp), OP.is_lt)
        if leave:
            if c:
                now[2] = "w0"
                mm(ww, A("Z0"), A("one", 0, nw), True)
                before(ww, "go", 0, c, True)
                now[2] = "fate"
            mm(ww, A("LW"), A("go", w0, wp), not c)
            mm(ww, A("ID"), A("dead", w0, wp))
            before(ww, "go", 0, c, False)
            stay = 1.5 * 2 ** 33
            ts(fr, ww, stay, OP.add, stay, OP.not_equal)
            now[2] = "slt"
            tt(A("slt", w0, wp), ww, A("lanc", w0, wp), OP.min)
        if t in SPLIT and leave:
            slots(c, w0, wp)
        now[2] = "cu"
        halves = [A(zz[1], 480 + nw * h, 480 + nw * h + nw) for h in range(2)]
        mm(zz, A("Ib"), A("cz", 0, 2 * nw), True)
        for half in halves:
            mm(half, A("Ib"), A("cur", w0, wp))
        if t in WIN:
            mm(halves[0], A("In"), A("base", w0, wp))
        now[2] = "z0"
        for half in halves:
            before(half, "fr", 14 * (t % 3), c, True)
        now[2] = "LE"
        for half in halves:
            mm(half, A("LZ"), fr)
            before(half, "fr", 14 * (t % 3), c, False)
        now[2] = "LN"
        both = A("nr", 2 * l0 + 15, 2 * lp, 16)
        tt(both, zz, both, OP.max)
        now[2] = "L16"
        swap(po, 352, nw, lambda g0: A("nr", 2 * l0 + 15 + 16 * g0, 2 * lp, 32))
        ts(A3("L16", 0, 2, w0, wp), A(po, 352, 352 + 2 * nw), 2047.0, OP.add)
        if t and c == 1 and t not in SPLIT:
            least_m()
        if leave and c == 1 and t not in SPLIT:
            slots(c, 0, 14)
        now[2] = "pack"
        if t in SPLIT and leave:
            pack(t, l0, l1, lp)

    def after(t):
        now[:] = [t, 1, "cur"]
        f0 = 14 * (t % 3)
        if t < 4:
            mm(A("pr1", 496, 510), A("Ib"), A("cur"), True)
            for d in range(1, 7):
                mm(A("pr1", 496, 510 - 2 * d), A("O32"), A("fr", f0 + 2 * d, f0 + 14))
                mm(A("pr1", 496 + 2 * d, 510), A("O32"), A("fr", f0, f0 + 14 - 2 * d))
            mm(A("pr1", 496, 510), A("O32"), A("fr", f0, f0 + 14))
            ts(A("cur"), A("pr1", 496, 510), float(L - LP), OP.add)
        if t + 1 in WIN:
            now[2] = "win"
            mag = 1.5 * 2 ** 27
            ts(A("base"), A("cur"), mag, OP.add, 1008.0 - mag, OP.add)
            for g0 in range(2):
                mm(A("pr1", 510, 511), A("LL", 128 * g0, 128 * g0 + 128), A("base", g0, g0 + 1), g0 == 0)
            ts(A("w16", 0, 1), A("pr1", 510, 511), 1.0 / 16, OP.mult, col(0), OP.add)
            cp(A("ow16"), IND(A("omf"), A("w16", 0, 1)))
        now[2] = "pack"
        if t >= 2:
            if t not in SPLIT:
                pack(t, 0, L, LP)
            leavers(t, str(t - 2), "snd", U * (4 - t), t == 2 and t not in PAR["early"])

    def guests(t):
        if t < 5:
            guests_in(t)
        guests_judged(t)
        if t == 5:
            dma("y", T.yg[:], A("jC", p=G8))
        threshold(t)

    def both_keys(t):
        if t in PAR["whole"]:
            front(t, 1)
            keys(t, 0)
        else:
            keys(t, 0)
            front(t, 1)
        if 0 < t < 5:
            windows(t)
        keys(t, 1)

    front(0, 0)
    both_keys(0)
    middle(0)
    for t in range(NT - 1):
        back(t, 0)
        if t == 4:
            guests(4)
        front(t + 1, 0)
        back(t, 1)
        after(t)
        both_keys(t + 1)
        if t == 4:
            guests_in(5)
        middle(t + 1)
        if t == 2:
            guests(3)
    guests(5)
    dma("y", T.yt[:], A("ytl", 64, 64 + NT, p=G8))
    now[2] = "out"
    dma("y", T.yn[:], A("yno", B, B + KN), 3500.0)
    act(A("vf"), IND(A("VT", 0, B + Q), entries(0, L)), bias=2047.0)
    dma("y", T.yv[:], A("vf", p=(0, 128, 16)))
    for c in range(2):
        back(5, c)
    ts(A("mi"), A("mn"), 2.0 ** -15, OP.mult)
    ts(A("mex", 15, LP, 16), A("mi"), 4095.0, OP.min)
    tr(A("mC"), A("mex"))
    dma("s", T.ym[:], A("mC", 0, L, p=(15, 128, 16)))
    emit(g, T, ops)
